import numpy as np, ml_dtypes
CORES = [10,34,74,98]
N = 4
BF = ml_dtypes.bfloat16
def gentries(a):
    return np.ascontiguousarray(a.reshape(8, 16, -1).transpose(0, 2, 1)).reshape(8, -1)
def gtable(e):
    e = np.asarray(e); return np.ascontiguousarray(e.reshape(8, -1, 16).transpose(0, 2, 1)).reshape(128, -1).astype(np.int32)
W, T, K, C, J, RO = 4096, 256, 16, 16, 4, 4
Q = W // T
def lay(v):
    return np.ascontiguousarray(v.transpose(0, 1, 3, 2)).reshape(N, 128, -1).astype(np.float32).astype(BF)
def pack(x, s, m, z, w, kp):
    return {"rec": lay(x), "st": lay(s.reshape(N, 8, T * K, 16)), "nm": np.stack([gtable(a.reshape(8, -1)) for a in m]), "arr": lay(z),
            "wt": np.ascontiguousarray(w.reshape(N, 128, 1)).astype(np.int32), "kap": np.stack([gtable(a) for a in kp])}
def consts(rng):
    return rng.integers(0, 256, (N, 8, 16)), rng.integers(0, 1024, (N, 8, C))
def make(rng, base, sp, wild):
    share = rng.choice(np.array([0.5, 0.7, 0.9]), (N, 8, 1, 1))
    def mix(n):
        v = np.clip(base + ((rng.random((N, 8, T, n, 16)) - 0.5) * sp).astype(np.int64), 0, 255)
        return np.where((rng.random((N, 8, T, n)) < share)[..., None], v, wild((N, 8, T, n)))
    x = mix(Q).reshape(N, 8, W, 16); s = mix(K); z = mix(1)[:, :, :, 0]
    own = Q * np.arange(T)[:, None] + rng.integers(0, Q, (N, 8, T, K))
    m = np.where(rng.random((N, 8, T, K)) < share, own, rng.integers(0, W, (N, 8, T, K)))
    return x, s, m, z
def setup_inputs(rng):
    x, s, m, z = make(rng, rng.integers(0, 256, (N, 8, T, 1, 16)), 24.0, lambda sh: rng.integers(0, 256, sh + (16,)))
    return pack(x, s, m, z, *consts(rng))
def setup_inputs_spread(rng):
    def uneven(sh):
        return np.minimum((np.exp2(8 * rng.random(sh + (1,))) * rng.random(sh + (16,))).astype(np.int64), 255)
    base = uneven((N, 8, T, 1)); x, s, m, z = make(rng, base, 0.5 * base + 2, uneven)
    m = np.where(rng.random((N, 8, T, K)) < 0.3, np.minimum((W * rng.random((N, 8, T, K)) ** 3).astype(np.int64), W - 1), m)
    w = np.minimum(np.exp2(8 * rng.random((N, 8, 16))).astype(np.int64) - 1, 255); kp = np.minimum(np.exp2(10 * rng.random((N, 8, C))).astype(np.int64) - 1, 1023)
    return pack(x, s, m, z, w, kp)
def setup_inputs_ends(rng):
    def ext(sh):
        k = rng.integers(0, 3, sh + (1,)); return 255 * np.where(k == 2, rng.integers(0, 2, sh + (16,)), k)
    x = ext((N, 8, W)); s = ext((N, 8, T, K)); z = ext((N, 8, T)); h = T // 2
    m = (W - 1) * rng.integers(0, 2, (N, 8, T, K)); w = 255 * rng.integers(0, 2, (N, 8, 16)); kp = 1023 * rng.integers(0, 2, (N, 8, C))
    w[:, 0, 3] = 0; kp[:, 0, 3] = 0
    w[:, 7] = 255; kp[:, 7] = 1023; x[:, 7] = 0; s[:, 7, h:] = 255; m[:, 7, h:] = W - 1
    z[:, 7] = 255 * rng.integers(0, 2, (N, T, 1)); z[:, 7, h:] = 255
    u = (16 * 255 * 255) & (W - 1); c = ((u * u >> 5) + 1023 * u + 1023) & (W - 1); x[0::2, 7, c, 15] = 1
    x[:, 6] = 0; s[:, 6, h:] = 0; z[:, 6, h:] = 0
    s[:, 5, T - 1] = 0; s[:, 5, T - 1, K - 1] = 255; z[:, 5, T - 1] = 255
    s[:, 5, T - 2] = 255; z[:, 5, T - 2] = 0
    s[:, 5, T - 3] = 0; s[:, 5, T - 3, K - 1, 15] = 1; z[:, 5, T - 3] = 255
    s[:, 5, T - 4] = 255; s[:, 5, T - 4, K - 2, 15] = 254; z[:, 5, T - 4] = 0
    x[:, 4] = rng.integers(0, 4, (N, W, 16)); s[:, 4] = rng.integers(252, 256, (N, T, K, 16))
    z[:, 4, :h] = rng.integers(252, 256, (N, h, 16)); z[:, 4, h:] = rng.integers(0, 4, (N, T - h, 16))
    m[:, 4] = rng.integers(0, W, (N, T, K)); w[:, 4] = rng.integers(0, 256, (N, 16)); kp[:, 4] = rng.integers(0, 1024, (N, C))
    return pack(x, s, m, z, w, kp)
def setup_inputs_corners(rng):
    gi = np.arange(8)[None, :]; ri = np.arange(N)[:, None]; row = np.arange(K); lane = np.arange(T)
    kind = np.argsort(rng.random((N, 8, T)), axis=-1) % 8; code = np.argsort(rng.random((N, 8, T)), axis=-1) % 6
    kind[:, :, T - 1] = gi; code[:, :, T - 1] = (gi + ri) % 6
    goal = np.array([0, K - 1, K - 2, K - 1 - J, K - J, 0, 0, 0])[kind]; goal = np.where(kind == 7, rng.integers(0, K, kind.shape), goal)
    z = rng.integers(0, 101, (N, 8, T, 16)); z[kind == 6] = np.array([255, 1] + [0] * 14)
    s = rng.integers(150, 256, (N, 8, T, K, 16)); hit = (row == goal[..., None]) | (kind == 5)[..., None]
    s = np.where(hit[..., None], z[:, :, :, None, :], s)
    tot = np.sum(z, axis=-1); n = Q * lane + (tot & (Q - 1)); far = Q * lane + ((tot + 1) & (Q - 1))
    x = rng.integers(0, 101, (N, 8, W, 16)); x[:, :, 0] = 0; x[:, :, W - 1] = 255
    a, b, c = np.nonzero(code == 3); x[a, b, far[a, b, c]] = 255
    k = code[..., None]; n1 = n[..., None]; last = np.where(row == (goal + J)[..., None], far[..., None], n1)
    m = np.where(k == 4, rng.integers(0, W, (N, 8, T, K)), np.roll(n, -1, axis=2)[..., None])
    m = np.where(k == 0, n1, np.where(k == 1, 0, np.where(k == 2, W - 1, np.where(k == 3, last, m))))
    w, kp = consts(rng); w[:, 0::2, 0] = (W - 1) // 255; w[:, 0::2, 1] = (W - 1) % 255; w[:, 5] = 0
    kp[:, 0] = 1023; kp[:, 3] = 0
    return pack(x, s, m, z, w, kp)
def setup_inputs_crowd(rng):
    v = rng.integers(40, 80, (N, 8, 16)); v[..., 0] |= 1
    v[..., 1] += (np.sum(v, axis=-1) & (Q - 1)) == 1
    w, kp = consts(rng); w[..., 0] ^= 1 - (np.sum(w * v, axis=-1) & 1)
    kp[..., 1] = 2 * (kp[..., 1] >> 1); kp[..., 2] |= 1
    x = v[:, :, None, :] + rng.integers(0, 4, (N, 8, W, 16)); x[:, :, 0::Q] = v[:, :, None, :]
    x[:, :, 1::Q] = v[:, :, None, :] + 100 + rng.integers(0, 75, (N, 8, T, 16))
    s = rng.integers(0, 256, (N, 8, T, K, 16)); s[:, :, :, 0] = v[:, :, None, :]
    z = np.repeat(v[:, :, None, :], T, axis=2)
    go = np.ones((N, 8, T), bool)
    for q in range(1, N):
        for g in range(8):
            mode = int(rng.integers(0, 4)) if q > 2 else int(rng.integers(0, 2))
            if q == 1: mode = 1 if g == 7 else 0
            if q == 2 and g == 3: mode = 1
            if mode == 1: go[q, g, T - 1 if q == 1 else int(rng.integers(0, T))] = False
            if mode == 2: go[q, g] = False
            if mode == 3: go[q, g] = rng.permutation(T) < T // 2
    off = Q * rng.integers(0, T, (N, 8, T, K)) + 1; off[:, 0::2] = off[:, 0::2, :1, :1]
    m = np.where(go[..., None], off, Q * rng.integers(0, T, (N, 8, T, K)))
    y = np.where(go[1][..., None], x[1][np.arange(8)[:, None], m[1, :, :, 1]], np.abs(z[1] - s[1, :, :, K - 1]))
    s[2, :, :, K - 1] = np.maximum(y - rng.integers(0, 4, y.shape), 0)
    return pack(x, s, m, z, w, kp)
def setup_inputs_ties(rng):
    p = rng.integers(20, 236, (N, 8, 16)); e = 20 * (np.arange(16) & 1)
    pats = np.stack([p, p + 10, p - 10, p + e, p + 20 - e], axis=2); a = np.arange(N)[:, None, None]; b = np.arange(8)[None, :, None]
    x = pats[a, b, rng.integers(0, 5, (N, 8, W))]; z = pats[a, b, rng.integers(0, 5, (N, 8, T))]
    s = pats[a, b, rng.integers(0, 5, (N, 8, T * K))].reshape(N, 8, T, K, 16)
    return pack(x, s, rng.integers(0, W, (N, 8, T, K)), z, *consts(rng))
def check_inputs(d):
    bad = []
    for k, hi in (("rec", 255), ("st", 255), ("nm", W - 1), ("arr", 255), ("wt", 255), ("kap", 1023)):
        v = np.asarray(d[k]).astype(np.float64)
        if not (np.all(v >= 0) and np.all(v <= hi)): bad.append("range of " + k)
        elif np.any(v != np.floor(v)): bad.append("whole numbers in " + k)
    return bad
def unlay(a):
    return np.ascontiguousarray(a.astype(np.float32).astype(np.int32).reshape(N, 8, 16, -1).transpose(0, 1, 3, 2))
def reference(rec, st, nm, arr, wt, kap):
    x = unlay(rec); s = unlay(st).reshape(N, 8, T, K, 16); z = unlay(arr)
    m = np.stack([gentries(a) for a in nm]).astype(np.int32).reshape(N, 8, T, K)
    w = wt.astype(np.int32).reshape(N, 8, 1, 16); kp = np.stack([gentries(a) for a in kap]).astype(np.int32)[:, :, None, :]
    ri = np.arange(N)[:, None, None]; gi = np.arange(8)[None, :, None]; li = np.arange(T)[None, None, :]; row = np.arange(K)
    cnt = np.zeros((N, 1, 1, 1), np.int32)
    for t in range(RO):
        n = (Q * li + (np.sum(z, axis=-1) & (Q - 1))).astype(np.int32)
        x[ri, gi, n] = z
        g = np.argmin(np.sum(np.abs(s - z[:, :, :, None, :]), axis=-1, dtype=np.int32), axis=-1)
        mid = (s[ri, gi, li, g] + z) >> 1
        low = row < g[..., None]
        s = np.where(low[..., None], np.concatenate([s[:, :, :, 1:], s[:, :, :, -1:]], axis=3), s)
        m = np.where(low, np.concatenate([m[..., 1:], m[..., -1:]], axis=3), m)
        s[ri, gi, li, g] = mid; m[ri, gi, li, g] = n
        rel = np.zeros((N, 8, T), bool); gone = np.zeros((N, 8, T), np.int32)
        for j in range(1, J + 1):
            live = g + j < K; p = np.minimum(g + j, K - 1)
            b = s[ri, gi, li, p - 1]
            u = (np.sum(w * b, axis=-1, dtype=np.int32) & (W - 1))[..., None]
            c = ((u * u >> 5) + kp * u + kp[..., :1] * j + cnt) & (W - 1)
            old = m[ri, gi, li, p]; c[..., 0] = old
            v = x[ri[..., None], gi[..., None], c]
            f = np.argmin(np.sum(np.abs(v - b[:, :, :, None, :]), axis=-1, dtype=np.int32), axis=-1)
            e = c[ri, gi, li, f]; xe = v[ri, gi, li, f]
            s[ri, gi, li, p] = np.where(live[..., None], (b + xe) >> 1, s[ri, gi, li, p])
            m[ri, gi, li, p] = np.where(live, e, old)
            now = live & (e != old) & ~rel
            gone = np.where(now, old, gone); rel = rel | now
        nxt = np.where(rel[..., None], x[ri, gi, gone], np.abs(z - s[:, :, :, K - 1]))
        cnt = (np.sum(rel, axis=(1, 2)).astype(np.int32) & 63).reshape(N, 1, 1, 1)
        z = np.stack([nxt[(q - 1 - t % 3) % N] for q in range(N)])
    mo = np.stack([gtable(a.reshape(8, -1)) for a in m])
    return {"so": lay(s.reshape(N, 8, T * K, 16)), "mo": mo.astype(np.float32), "zo": lay(z)}

@@ -1,0 +1,560 @@
+from concourse.mybir import AluOpType as ALU, ActivationFunctionType as AF, AxisListType as AX
+
+NS = 2
+CH = (0, 4, 10, 16)
+VB = (0, 4, 6, 10, 14, 16)
+IX = 10
+XV = 0
+RB, RV = 8, (0, 5)
+GV = 4
+PLS = 1
+BONUS, LOOK, PASSES, NOISE, SEED, SHIFT, SPAN = 2000.0, 60.0, 200, 300.0, 1, 1000.0, 6000.0
+HOP, SAME, NET = 110.0, 70.0, 3500.0
+GC, VF, PEC = 1.55 * 0.83 * 1.15, 0.83 * 1.2, 0.45
+MAGIC = 12582912.0
+BF, F32, I32, U16 = "bfloat16", "float32", "int32", "uint16"
+
+SCRATCH = {"X": ("sbuf", [128, 4096], BF), "nmi": ("sbuf", [128, 256], I32), "wk": ("sbuf", [128, 16], I32)}
+for _n, _w, _d in [("xf", 144, F32), ("mc", 128, BF), ("xg", 128, F32), ("xm", 128, F32), ("pi", 16, I32), ("col", 16, F32),
+                   ("big", 144, BF), ("bigf", 144, F32), ("wbig", 144, BF), ("idp", 128, BF), ("idn", 128, BF), ("idh", 128, BF),
+                   ("idf", 128, F32), ("shf", 128, F32), ("bof", 128, F32), ("bo8", 32, BF), ("dm", 128, BF), ("rst", 128, F32),
+                   ("c128", 128, BF), ("cq", 128, BF), ("one", 128, BF), ("kd", 128, F32), ("kr", 128, F32), ("rl", 16, U16),
+                   ("rli", 16, I32), ("rs", 8, F32), ("ib", 8, F32), ("rg0", 128, BF), ("rg1", 128, BF), ("cg0", 128, BF),
+                   ("cg1", 128, BF), ("rc", 16, BF), ("cc", 16, BF), ("et", 32, BF), ("eb", 32, BF), ("tb", 128, F32), ("i16", 128, F32),
+                   ("wj", 64, F32), ("kj", 8, F32), ("b1", 16, F32), ("cn", 32, F32), ("cni", 16, I32), ("bc", 48, F32), ("cb", 16, BF)]:
+    SCRATCH[_n] = ("sbuf", [128, _w], _d)
+for _h in "01":
+    for _n, _w, _d in [("pool", 6144, BF), ("aw", 8320, BF), ("mn", 2048, BF), ("z", 640, BF), ("zs", 512, BF), ("xe", 128, BF),
+                       ("run", 128, F32), ("ti", 32, I32), ("ex", 128, BF), ("lg", 48, U16), ("lc", 64, U16), ("ls", 32, U16),
+                       ("sm", 64, F32), ("si", 64, I32), ("p1", 128, F32), ("p2", 128, I32), ("ci", 640, I32), ("cu", 512, U16),
+                       ("M", 128, F32), ("Q", 512, F32), ("KL", 256, F32), ("P", 640, F32), ("pl", 640, F32), ("em", 640, BF),
+                       ("rf", 128, F32), ("ru", 128, U16), ("lw", 64, F32), ("nz", 128, F32), ("dz", 128, BF)]:
+        SCRATCH[_n + _h] = ("sbuf", [128, _w], _d)
+    for _n in ("bS", "bD", "bM", "bG"):
+        SCRATCH[_n + _h] = ("psum", [128, 512], F32)
+SEMAPHORES = (["qV", "qA", "qP", "qG", "sent"] + ["d%d" % i for i in range(32)] + ["in%d" % i for i in range(8)])
+
+
+def build(g, core, T, topo, ops):
+    rank = T.rank_of(core)
+    V, A, P = g.vector, g.scalar, g.tensor
+    last_w, readers, bank = {}, {}, {}
+    cur_h = [0]
+
+    def op(e, fn, r, w, cost, banks=(), sem=None, after=()):
+        i = len(ops)
+        deps = {}
+        for k in r:
+            if k in last_w:
+                deps[last_w[k]] = 0.0
+        for k in w:
+            if k in last_w:
+                deps[last_w[k]] = 0.0
+            for x in readers.get(k, ()):
+                deps[x] = 0.0
+        for k in r:
+            readers.setdefault(k, []).append(i)
+        for k in w:
+            last_w[k] = i
+            readers[k] = []
+        for b in banks:
+            en, cur, prev = bank.get(b, (e, [], []))
+            if en != e:
+                cur, prev = [], cur
+            for x in prev + (cur[-1:] if e == "P" else []):
+                deps[x] = 0.0
+            bank[b] = (e, cur + [i], prev)
+        for x, lat in after:
+            deps[x] = lat
+        deps.pop(i, None)
+        ops.append({"e": e, "fn": fn, "deps": deps, "cost": cost, "sem": sem, "h": cur_h[0]})
+        return i
+
+    def vc(n, k=1.0):
+        return 55 + n * k * VF
+
+    def ts(out, in0, s1, s2, o0, o1, r, w, n, banks=()):
+        if o1 is None:
+            return op("V", lambda: V.tensor_scalar(out, in0, s1, None, o0), r, w, vc(n), banks)
+        return op("V", lambda: V.tensor_scalar(out, in0, s1, s2, o0, o1), r, w, vc(n), banks)
+
+    def tt(out, in0, in1, o, r, w, n, banks=()):
+        return op("V", lambda: V.tensor_tensor(out, in0, in1, o), r, w, vc(n, 1.0 if banks else 2.0), banks)
+
+    def tg(out, win, lst, in1, o, r, w, n):
+        return op("V", lambda: V.tensor_tensor(out, win.indirect(lst), in1, o), r, w, 55 + n * GC)
+
+    def cp(out, in_, r, w, n, banks=()):
+        return op("V", lambda: V.tensor_copy(out, in_), r, w, vc(n), banks)
+
+    def ms(out, c, w, n):
+        return op("V", lambda: V.memset(out, float(c)), [], w, vc(n, 0.5))
+
+    def ag(out, win, lst, r, w, n):
+        return op("A", lambda: A.activation(out, win.indirect(lst), AF.Copy), r, w, 70 + n * GC)
+
+    def vg(out, win, lst, r, w, n):
+        return op("V", lambda: V.tensor_copy(out, win.indirect(lst)), r, w, 55 + n * GC)
+
+    def act(out, in_, f, r, w, n, banks=()):
+        return op("A", lambda: A.activation(out, in_, f), r, w, 70 + n * VF, banks)
+
+    def mm(lst, r, w, bk, fp32=False):
+        def fn():
+            for o, l, x, a, b, _ in lst:
+                ins = P.matmul(o, l, x, a, b)
+            return ins
+        return op("P", fn, r, w, 20 + sum(max(64, m[5]) for m in lst) * PEC * (4 if fp32 else 1), [bk])
+
+    def io(out, pat, base, cm, w, n, flag=True):
+        if flag:
+            return op("G", lambda: g.iota(out, pat, base, cm, allow_small_or_imprecise_dtypes=True), [], w, 130 + 2 * n)
+        return op("G", lambda: g.iota(out, pat, base, cm), [], w, 130 + 2 * n)
+
+    nd = [0]
+
+    def dma(q, out, in_, r, w, cost):
+        s = "d%d" % nd[0]
+        nd[0] += 1
+        Q = g.sync if q == "Y" else A
+        return op(q, lambda: Q.dma_start(out, in_), r, w, cost, sem=s)
+
+    H = [{n: T[n + h] for n in ("pool aw mn z zs xe run ti ex lg lc ls sm si p1 p2 ci cu M Q KL P pl em rf ru lw nz dz "
+                                "bS bD bM bG").split()} for h in "01"]
+    X, col = T.X, T.col
+
+    for h in (0, 1):
+        dma("Y", H[h]["z"][:, 0:128], T.arr[:, 128 * h:128 * h + 128], [], ["z%d0" % h], 2200)
+        dma("Y", H[h]["pool"][:, 0:2048], T.st[:, 2048 * h:2048 * h + 2048], [], ["S%d0" % h], 4000 + 2000 * h)
+        if h == 0:
+            dma("Y", T.wk[:, 0:1], T.wt[:], [], ["wk0"], 2200)
+            dma("Y", T.wk[:, 8:9], T.kap[:], [], ["wk8"], 2200)
+            dma("Y", T.nmi[:], T.nm[:], [], ["nmi"], 4500)
+    for h in (0, 1):
+        dma("Y", X[:, 2048 * h:2048 * h + 2048], T.rec[:, 2048 * h:2048 * h + 2048], [], ["X%d" % h], 8000 + 2000 * h)
+
+    io(T.pi[:, 0:1], [[1, 1]], 0, 1, ["pi0"], 1, False)
+    io(T.xf[:], [[1, 144]], 0, 0, ["xf"], 144)
+    io(T.mc[:], [[0, 8], [1, 16]], 0, 0, ["mc"], 128)
+    io(T.xg[:], [[16, 8], [0, 16]], 0, 0, ["xg"], 128)
+    io(T.xm[:], [[1, 16], [0, 8]], 0, 0, ["xm"], 128)
+    io(T.i16[:], [[16, 128]], 0, 0, ["i16"], 128)
+    io(T.rli[:, 0:8], [[1, 8]], 0, 0, ["rli0"], 8, False)
+    io(T.rli[:, 8:16], [[0, 8]], 0, 1, ["rli8"], 8, False)
+    ts(T.pi[:, 4:5], T.pi[:, 0:1], 15, None, ALU.bitwise_and, None, ["pi0"], ["pi4"], 1)
+    cp(col[:, 0:1], T.pi[:, 0:1], ["pi0"], ["c0"], 1)
+    cp(col[:, 1:2], T.pi[:, 4:5], ["pi4"], ["c1"], 1)
+    tt(col[:, 2:3], col[:, 0:1], col[:, 1:2], ALU.subtract, ["c0", "c1"], ["c2"], 1)
+    ts(col[:, 3:4], col[:, 2:3], 15.0, None, ALU.add, None, ["c2"], ["c3"], 1)
+    ts(col[:, 4:5], col[:, 0:1], -1.0, None, ALU.add, None, ["c0"], ["c4"], 1)
+    ts(col[:, 5:6], col[:, 1:2], 0.0, None, ALU.is_gt, None, ["c1"], ["c5"], 1)
+    cp(col[:, 6:7], T.wk[:, 0:1], ["wk0"], ["c6"], 1)
+    cp(col[:, 7:8], T.wk[:, 8:9], ["wk8"], ["c7"], 1)
+    EQ, MU, AD = ALU.is_equal, ALU.mult, ALU.add
+    x128 = T.xf[:, 0:128]
+    ts(T.idp[:], x128, col[:, 0:1], None, EQ, None, ["xf", "c0"], ["idp"], 128)
+    ts(T.idn[:], x128, col[:, 0:1], -1.0, EQ, MU, ["xf", "c0"], ["idn"], 128)
+    ts(T.idh[:], x128, col[:, 0:1], 0.5, EQ, MU, ["xf", "c0"], ["idh"], 128)
+    ts(T.idf[:], x128, col[:, 0:1], None, EQ, None, ["xf", "c0"], ["idf"], 128)
+    ts(T.shf[:], x128, col[:, 4:5], col[:, 5:6], EQ, MU, ["xf", "c4", "c5"], ["shf"], 128)
+    ts(T.bof[:], T.xg[:], col[:, 2:3], None, EQ, None, ["xg", "c2"], ["bof"], 128)
+    ts(T.big[:], T.xf[:], col[:, 3:4], None, EQ, None, ["xf", "c3"], ["big"], 144)
+    ts(T.bigf[:], T.xf[:], col[:, 3:4], None, EQ, None, ["xf", "c3"], ["bigf"], 144)
+    ts(T.wbig[:], T.xf[:], col[:, 3:4], col[:, 6:7], EQ, MU, ["xf", "c3", "c6"], ["wbig"], 144)
+    ts(T.rs[:], T.xf[:, 0:128:16], col[:, 2:3], None, EQ, None, ["xf", "c2"], ["rs"], 8)
+    for b, s in enumerate((16.0, -32.0, 32.0, -16.0)):
+        ts(T.bo8[:, 8 * b:8 * b + 8], T.rs[:], s, None, MU, None, ["rs"], ["bo%d" % b], 8)
+    ts(T.dm[:], T.mc[:], col[:, 1:2], None, EQ, None, ["mc", "c1"], ["dm"], 128)
+    ts(T.rst[:], T.mc[:], 0.0, 1048576.0, EQ, MU, ["mc"], ["rst"], 128)
+    ms(T.c128[:], 2.0 ** -7, ["c128"], 128)
+    ms(T.cq[:], -2.0 ** -9, ["cq"], 128)
+    ms(T.one[:], 1.0, ["one"], 128)
+    ts(T.rli[:, 8:16], T.rli[:, 8:16], 7, None, ALU.bitwise_and, None, ["rli8"], ["rli8"], 8)
+    cp(T.rl[:], T.rli[:], ["rli0", "rli8"], ["rl"], 16)
+    repg, repr_ = T.rl[:, 0:8], T.rl[:, 8:16]
+    ts(T.ib[:], T.xf[:, 0:128:16], col[:, 1:2], None, AD, None, ["xf", "c1"], ["ib"], 8)
+    ts(T.kd[:], T.xm[:], col[:, 1:2], col[:, 7:8], EQ, MU, ["xm", "c1", "c7"], ["kd"], 128)
+    mm([(T.bG1[:, 0:128], T.bof[:], T.kd[:], True, True, 128)], ["bof", "kd"], ["kp"], "bG_1", True)
+    cp(T.kr[:], T.bG1[:, 0:128], ["kp"], ["kr"], 128, ["bG_1"])
+    ts(T.kj[:, 4:8], T.xf[:, 1:5], 32.0, None, MU, None, ["xf"], ["kj4"], 4)
+    ts(T.kj[:, 0:4], T.kj[:, 4:8], T.kr[:, 0:1], -262156.0, MU, AD, ["kj4", "kr"], ["b10"], 4)
+    ts(T.rc[:, 0:8], T.rs[:], 128.0, None, MU, None, ["rs"], ["rc0"], 8)
+    ts(T.rc[:, 8:16], T.rs[:], 8.0, None, MU, None, ["rs"], ["rc1"], 8)
+    cp(T.cc[:, 0:8], T.ib[:], ["ib"], ["cc0"], 8)
+    cp(T.cc[:, 8:16], T.xf[:, 0:8], ["xf"], ["cc1"], 8)
+    ms(T.rg0[:, 64:128], 0.0, ["rg0"], 64)
+    ms(T.cg0[:, 64:128], 99.0, ["cg0"], 64)
+    ms(T.wj[:], 0.0, ["wj"], 64)
+    for b in (0, 1, 2, 3, 4, 5, 7, 8, 10, 12, 14):
+        cp(T.rg0[:, 8 * b:8 * b + 8], T.rs[:], ["rs"], ["rg0"] if b > 7 else ["rg0_%d" % b], 8)
+    ts(T.cg0[:, 0:8], T.ib[:], 16.0, None, MU, None, ["ib"], ["cg0_0"], 8)
+    for j in range(5):
+        ms(T.cg0[:, 8 + 8 * j:16 + 8 * j], j, ["cg0_%d" % (j + 1)], 8)
+        if j:
+            ms(T.cg0[:, 48 + 16 * j:56 + 16 * j], j, ["cg0"], 8)
+            ms(T.wj[:, 16 * j - 16:16 * j - 8], (5 - j) * 2048, ["wj"], 8)
+    ts(T.rg0[:, 48:56], T.rs[:], 4096.0, None, MU, None, ["rs"], ["rg0_6"], 8)
+    ms(T.cg0[:, 48:56], -40960.0, ["cg0_6"], 8)
+    ts(T.cg0[:, 56:64], T.ib[:], 16.0, 2048.0, MU, AD, ["ib"], ["cg0_7"], 8)
+    RG = [["rg0"] + ["rg0_%d" % b for b in range(8)], ["rg1"]]
+    CG = [["cg0"] + ["cg0_%d" % b for b in range(8)], ["cg1"]]
+    cp(T.rg1[:], T.rg0[:], RG[0], ["rg1"], 64)
+    cp(T.cg1[:], T.cg0[:], CG[0], ["cg1"], 64)
+    ts(T.rg1[:, 48:56], T.rs[:], -4096.0, None, MU, None, ["rs"], ["rg1"], 8)
+    ms(T.cg1[:, 48:56], 45056.0, ["cg1"], 8)
+    ts(T.cg1[:, 56:64], T.ib[:], 16.0, None, MU, None, ["ib"], ["cg1"], 8)
+    for b, (s, a) in enumerate(((16.0, 0.0), (16.0, 2048.0), (16.0, 15.0), (16.0, 2063.0), (1.0, 8192.0))):
+        ts(T.bc[:, 8 * b:8 * b + 8], T.ib[:], s, a, MU, AD, ["ib"], ["bc%d" % b], 8)
+    tb = T.tb
+    ts(T.et[:], T.xf[:, 0:32], col[:, 1:2], None, EQ, None, ["xf", "c1"], ["et"], 32)
+    ts(T.eb[:], T.et[:], -1.0, 8192.0, AD, MU, ["et"], ["eb"], 32)
+    ts(tb[:, 0:16], T.xf[:, 0:16], col[:, 1:2], None, ALU.subtract, None, ["xf", "c1"], ["t0"], 16)
+    ts(tb[:, 16:32], tb[:, 0:16], -4.0, None, ALU.is_lt, None, ["t0"], ["keep"], 16)
+    ts(tb[:, 32:48], tb[:, 0:16], 0.0, None, ALU.is_ge, None, ["t0"], ["le"], 16)
+    ts(tb[:, 48:64], tb[:, 0:16], 0.0, None, ALU.is_gt, None, ["t0"], ["lt"], 16)
+    tt(tb[:, 64:80], tb[:, 16:32], tb[:, 48:64], AD, ["keep", "lt"], ["old"], 16)
+    for par in (0, 1):
+        nb, ob = (2048.0, 0.0) if par == 0 else (0.0, 2048.0)
+        al, tm, k = tb[:, 96 + 16 * par:112 + 16 * par], tb[:, 80:96], "al%d" % par
+        ts(al, tb[:, 0:16], nb + 15.0, None, AD, None, ["t0"], [k], 16)
+        ts(tm, tb[:, 48:64], col[:, 1:2], ob, AD, AD, ["lt", "c1"], ["tm"], 16)
+        tt(tm, tm, al, ALU.subtract, ["tm", k], ["tm"], 16)
+        tt(tm, tm, tb[:, 64:80], MU, ["tm", "old"], ["tm"], 16)
+        tt(al, al, tm, AD, ["tm", k], [k], 16)
+    for h in (0, 1):
+        io(H[h]["pool"][:, 2048:4096], [[0, 2048]], 0, 0, ["new%d%d" % (h, j) for j in range(5)], 2048)
+        cp(H[h]["M"][:], T.nmi[:, 128 * h:128 * h + 128], ["nmi"], ["M%d" % h], 128)
+
+    def sel(tab, q):
+        return tab[:, 15 - q:143 - q]
+
+    def argmin(h, B, k):
+        D = B["bD"][:, 0:128]
+        op("V", lambda: V.tensor_tensor_scan(B["run"][:], T.rst[:], D, 0.0, AD, ALU.min), ["rst", k("D")], [k("run")], vc(128), [k("bD")])
+        cp(B["ti"][:, 8:16], B["run"][:, 15::16], [k("run")], [k("ti8")], 8)
+        ts(B["ti"][:, 0:8], B["ti"][:, 8:16], 15, None, ALU.bitwise_and, None, [k("ti8")], [k("ti0")], 8)
+        tg(B["ex"][:], B["ti"][:, 0:8], repg, T.dm[:], MU, [k("ti0"), "rl", "dm"], [k("ex")], 128)
+
+    def middle(h, B, k, prev, kprev, j):
+        mm([(B["bM"][:, 0:128], T.cq[:], T.one[:], True, False, 128), (B["bM"][:, 0:128], T.idh[:], prev, False, False, 128),
+            (B["bM"][:, 0:128], T.idh[:], B["xe"][:], False, True, 128)], ["cq", "one", "idh", kprev, k("xe")], [k("mid")], k("bM"))
+        ts(B["pool"][:, 2063 - j:4096:16], B["bM"][:, 0:128], MAGIC, MAGIC, AD, ALU.subtract, [k("mid")], ["new%d%d" % (h, j)], 128, [k("bM")])
+
+    def place(h, B, k, j, win, lst, kl):
+        tg(B["P"][:, 128 * j:128 * j + 128], win, lst, T.dm[:], MU, [k("ci%d" % j), k("cj%d0" % j), k("cj%d1" % j), kl, "dm"], [k("P%d" % j)], 128)
+        if PLS:
+            mm([(B["bG"][:, 0:128], T.idp[:], B["em"][:, 128 * j:128 * j + 128], True, False, 32),
+                (B["bG"][:, 0:128], T.bof[:], B["P"][:, 128 * j:128 * j + 128], False, True, 128)], ["bof", "idp", k("em"), k("P%d" % j)], [k("G")], k("bG"), True)
+            act(B["pl"][:, 128 * j:128 * j + 128], B["bG"][:, 0:128], AF.Relu, [k("G")], [k("pl%d" % j)], 128, [k("bG")])
+            return
+        mm([(B["bG"][:, 0:128], T.bof[:], B["P"][:, 128 * j:128 * j + 128], True, True, 128)], ["bof", k("P%d" % j)], [k("G")], k("bG"), True)
+        tt(B["pl"][:, 128 * j:128 * j + 128], B["bG"][:, 0:128], B["em"][:, 128 * j:128 * j + 128], MU, [k("G"), k("em")], [k("pl%d" % j)], 128, [k("bG")])
+
+    def head(t, h):
+        cur_h[0] = h
+        B, par = H[h], t % 2
+        k = lambda s: s + "_%d" % h
+        z, kz, kS = B["z"][:, 128 * t:128 * t + 128], "z%d%d" % (h, t), "S%d%d" % (h, par)
+        s0 = 4096 * par
+        mm([(B["bM"][:, 136:144], sel(T.big, q), B["z"][:, 128 * t + q:128 * t + 128:16], q == 0, q == 15, 8) for q in range(16)], ["big", kz], [k("sz")], k("bM"))
+        cp(B["si"][:, 32:40], B["bM"][:, 136:144], [k("sz")], [k("s32")], 8, [k("bM")])
+        ts(B["si"][:, 40:48], B["si"][:, 32:40], 15, None, ALU.bitwise_and, None, [k("s32")], [k("s40")], 8)
+        tt(B["ci"][:, 0:8], B["si"][:, 40:48], T.bc[:, 8 * h:8 * h + 8], AD, [k("s40"), "bc%d" % h], [k("ci0")], 8)
+        ts(B["ls"][:, 0:8], B["ci"][:, 0:8], -2048.0 * h, None, AD, None, [k("ci0")], [k("ln")], 8)
+        op("V", lambda: V.tensor_copy(X[:, 2048 * h:2048 * h + 2048].indirect(B["ls"][:, 0:8]), z), [k("ln"), kz], ["X%d" % h], 55 + 128 * 4)
+        mm([(B["bD"][:, 0:128], T.c128[:], T.mc[:], True, False, 128)], ["c128", "mc"], [k("D")], k("bD"))
+        row = lambda m: B["pool"][:, s0 + m:s0 + 2048:16]
+        mnm = lambda m: B["mn"][:, 128 * m:128 * m + 128]
+        Dm = lambda m: B["bD"][:, m:128:16]
+        if GV:
+            mm([(B["bM"][:, 256:384], T.idp[:], z, True, True, 128)], ["idp", kz], [k("zp")], k("bM"))
+            mm([(Dm(m), x, T.bo8[:, 0:8], False, False, 8) for m in range(GV) for x in (row(m), z)], [kS, kz, "bo0"], [k("D")], k("bD"))
+            for m in range(GV):
+                tt(mnm(m), row(m), B["bM"][:, 256:384], ALU.min, [kS, k("zp")], [k("mn%d" % m)], 128, [k("bM")])
+        for b, m0 in enumerate(range(GV, 16, 4)):
+            bk, ms_ = "bS" if b % 2 == 0 else "bG", range(m0, min(m0 + 4, 16))
+            lst = []
+            for m in ms_:
+                o = B[bk][:, 128 * (m - m0):128 * (m - m0) + 128]
+                lst += [(o, T.idp[:], row(m), True, False, 128), (o, T.idn[:], z, False, True, 128)]
+            kb = k("sP") if bk == "bS" else k("G")
+            mm(lst, ["idp", "idn", kS, kz], [kb], k(bk))
+            act(B["mn"][:, 128 * m0:128 * (ms_[-1] + 1)], B[bk][:, 0:128 * len(ms_)], AF.Abs, [kb], [k("mn%d" % m) for m in ms_], 128 * len(ms_), [k(bk)])
+        blocks = [range(m0, min(m0 + 4, 16)) for m0 in range(GV, 16, 4)]
+        for b, m0 in enumerate(range(0, GV, 4)):
+            blocks.insert(min(2 * b, len(blocks)), range(m0, min(m0 + 4, GV)))
+        for ms_ in blocks:
+            mm([(Dm(m), mnm(m), T.bo8[:, 8:16] if m < GV else T.bo8[:, 0:8], False, ms_ is blocks[-1] and m == ms_[-1], 8) for m in ms_],
+               [k("mn%d" % m) for m in ms_] + ["bo0", "bo1"], [k("D")], k("bD"))
+        argmin(h, B, k)
+        cv = B["bD"]
+        mm([(cv[:, 128:256], T.idp[:], T["cg%d" % par][:], True, False, 128), (cv[:, 128:256], B["ex"][:], T["rg%d" % par][:], False, True, 128)],
+           ["idp", k("ex")] + RG[par] + CG[par], [k("cv")], k("bD"))
+        cp(B["lg"][:], cv[:, 128:176], [k("cv")], [k("lg")], 48, [k("bD")])
+        o1, o2 = (ALU.max, ALU.min) if par == 0 else (ALU.min, ALU.max)
+        tt(B["sm"][:, 16:24], cv[:, 176:184], T.bc[:, 16 + 8 * par:24 + 8 * par], o1, [k("cv"), "bc%d" % (2 + par)], [k("m16")], 8, [k("bD")])
+        tt(B["sm"][:, 24:32], cv[:, 184:192], B["sm"][:, 16:24], o2, [k("cv"), k("m16")], [k("m24")], 8, [k("bD")])
+        ts(B["lw"][:], cv[:, 192:256], 15.0, None, ALU.is_le, None, [k("cv")], [k("lw")], 64, [k("bD")])
+        ag(B["xe"][:], B["pool"][:, s0:s0 + 2048], B["lg"][:, 0:8], [kS, k("lg")], [k("xe")], 128)
+        middle(h, B, k, z, kz, 0)
+        for j in range(1, 5):
+            tg(B["Q"][:, 128 * j - 128:128 * j], T.et[:, 0:32], B["lg"][:, 8 + 8 * j:16 + 8 * j], B["M"][:], MU, ["et", k("lg"), "M%d" % h], [k("Q%d" % j)], 128)
+        for q in range(16):
+            mm([(B["bG"][:, 256:288], sel(T.bigf, q), B["Q"][:, q::16], q == 0, q == 15, 32)],
+               ["bigf"] + [k("Q%d" % j) for j in range(1, 5)], [k("G")], k("bG"), True)
+        for j in range(1, 5):
+            cp(B["cu"][:, 128 * j - 128:128 * j - 120], B["bG"][:, 248 + 8 * j:256 + 8 * j], [k("G")], [k("cz%d" % j)], 8, [k("bG")])
+            cp(B["ci"][:, 128 * j:128 * j + 8], B["bG"][:, 248 + 8 * j:256 + 8 * j], [k("G")], [k("ci%d" % j)], 8, [k("bG")])
+        cp(B["ls"][:, 8:16], B["sm"][:, 24:32], [k("m24")], [k("l15")], 8)
+        tt(B["lw"][:], B["lw"][:], T.wj[:], MU, [k("lw"), "wj"], [k("lw")], 64)
+        ag(B["em"][:], (T.eb if PLS else T.et)[:, 0:32], B["lg"][:, 8:48], ["et", "eb", k("lg")], [k("em")], 640)
+        tg(B["KL"][:, 0:128], tb[:, 16:32], B["lg"][:, 8:16], B["M"][:], MU, ["keep", k("lg"), "M%d" % h], [k("K")], 128)
+        tg(B["KL"][:, 128:256], tb[:, 32:48], B["lg"][:, 8:16], B["M"][:], MU, ["le", k("lg"), "M%d" % h], [k("L")], 128)
+        tg(B["rf"][:], tb[:, 96 + 16 * par:112 + 16 * par], B["lg"][:, 8:16], T.i16[:], AD, ["al%d" % par, k("lg"), "i16"], [k("rf")], 128)
+        cp(B["ru"][:], B["rf"][:], [k("rf")], [k("ru")], 128)
+
+    def corr(t, h, j):
+        cur_h[0] = h
+        B = H[h]
+        k = lambda s: s + "_%d" % h
+        c0 = 2064 - j
+        s, ks = B["pool"][:, c0:4096:16], "new%d%d" % (h, j - 1)
+        si, sm, a0 = B["si"], B["sm"], 2048 * (j - 1)
+        mm([(B["bM"][:, 128:136], sel(T.wbig, q), B["pool"][:, c0 + 16 * q:4096:256], q == 0, q == 15, 8) for q in range(16)], ["wbig", ks], [k("U")], k("bM"))
+        mm([(B["bS"][:, 128 * c:128 * c + 128], T.idp[:], s, True, True, 128) for c in range(4)], ["idp", ks], [k("sP")], k("bS"))
+        mm([(B["bD"][:, 0:128], T.c128[:], T.mc[:], True, False, 128)], ["c128", "mc"], [k("D")], k("bD"))
+        cp(si[:, 8:16], B["bM"][:, 128:136], [k("U")], [k("s8")], 8, [k("bM")])
+        ts(si[:, 0:8], si[:, 8:16], 4095, None, ALU.bitwise_and, None, [k("s8")], [k("u")], 8)
+        tt(sm[:, 0:8], si[:, 0:8], si[:, 0:8], MU, [k("u")], [k("sq")], 8)
+        b1 = T.kj[:, j - 1:j] if t == 0 else T.b1[:, 4 * t + j - 1:4 * t + j]
+        ts(si[:, 16:24], sm[:, 0:8], b1, 2.0 ** -5, AD, MU, [k("sq"), "b1%d" % t], [k("base")], 8)
+        for x, (e0, e1) in enumerate(((8 * IX, 128), (0, 8 * IX)) if IX else ((0, 128),)):
+            rp, f0 = T.rl[:, 8:8 + (e1 - e0) // 16], max(e0, 8)
+            tg(B["p1"][:, e0:e1], si[:, 0:8], rp, T.kr[:, e0:e1], MU, [k("u"), "rl", "kr"], [k("p1%d" % x)], e1 - e0)
+            tg(B["p2"][:, e0:e1], si[:, 16:24], rp, B["p1"][:, e0:e1], AD, [k("base"), "rl", k("p1%d" % x)], [k("p2%d" % x)], e1 - e0)
+            ts(B["ci"][:, 128 * j + f0:128 * j + e1], B["p2"][:, f0:e1], 4095, None, ALU.bitwise_and, None, [k("p2%d" % x)], [k("cj%d%d" % (j, x))], e1 - f0)
+            cp(B["cu"][:, 128 * j - 128 + f0:128 * j - 128 + e1], B["ci"][:, 128 * j + f0:128 * j + e1], [k("cj%d%d" % (j, x))], [k("cu%d%d" % (j, x))], e1 - f0)
+        if j == 1:
+            place(h, B, k, 0, B["ci"][:, 0:8], repg, "rl")
+        else:
+            place(h, B, k, j - 1, B["ci"][:, 128 * j - 128:128 * j], B["lc"][:, 16 * j - 24:16 * j - 16], k("lc%d" % (j - 1)))
+        ka = lambda m: k("a%d%d" % (j, sum(1 for c in CH[1:] if c <= m)))
+        am = lambda m: B["aw"][:, a0 + 128 * m:a0 + 128 * m + 128]
+        mnm = lambda m: B["mn"][:, 128 * m:128 * m + 128]
+        Dm = lambda m: B["bD"][:, m:128:16]
+        mv = 16 - NS
+        cuts = sorted(set(x for x in VB + CH + (mv,) if x <= mv))
+        for c0_, c1 in list(zip(CH, CH[1:]))[::-1]:
+            kl = [k("cu%d0" % j)] + ([k("cu%d1" % j)] if c0_ < IX else []) + ([k("cz%d" % j)] if c0_ == 0 else [])
+            ag(B["aw"][:, a0 + 128 * c0_:a0 + 128 * c1], X[:, 0:4096], B["cu"][:, 128 * j - 128 + 8 * c0_:128 * j - 128 + 8 * c1],
+               ["X0", "X1"] + kl, [ka(c0_)], 128 * (c1 - c0_))
+            if c1 == 16 and NS:
+                lst = []
+                for m in range(mv, 16):
+                    o = B["bG"][:, 128 * (m - mv):128 * (m - mv) + 128]
+                    lst += [(o, T.idp[:], am(m), True, False, 128), (o, T.idn[:], s, False, True, 128)]
+                mm(lst, ["idp", "idn", ka(15), ks], [k("G")], k("bG"))
+                act(B["mn"][:, 128 * mv:2048], B["bG"][:, 0:128 * NS], AF.Relu, [k("G")], [k("mn%d" % m) for m in range(mv, 16)], 128 * NS, [k("bG")])
+            mm([(Dm(m), am(m), T.bo8[:, 24:32] if m >= mv else T.bo8[:, 0:8], False, False, 8) for m in range(c0_, c1)], [ka(c0_), "bo0", "bo3"], [k("D")], k("bD"))
+            if c0_ == 0 and NS:
+                mm([(Dm(m), mnm(m), T.bo8[:, 16:24], False, False, 8) for m in range(mv, 16)], [k("mn%d" % m) for m in range(mv, 16)] + ["bo2"], [k("D")], k("bD"))
+            for m0, m1 in list(zip(cuts, cuts[1:]))[::-1]:
+                if c0_ <= m0 < c1:
+                    kk = [k("mn%d" % m) for m in range(m0, m1)]
+                    tt(B["mn"][:, 128 * m0:128 * m1], B["aw"][:, a0 + 128 * m0:a0 + 128 * m1], B["bS"][:, 0:128 * (m1 - m0)], ALU.min,
+                       [ka(m0), k("sP")], kk, 128 * (m1 - m0), [k("bS")])
+                    mm([(Dm(m), mnm(m), T.bo8[:, 8:16], False, m0 == 0 and m == m1 - 1, 8) for m in range(m0, m1)], kk + ["bo1"], [k("D")], k("bD"))
+        argmin(h, B, k)
+        cv = B["bD"][:, 128:144]
+        mm([(cv, T.idp[:], T.cc[:], True, False, 16), (cv, B["ex"][:], T.rc[:], False, True, 16)], ["idp", "cc0", "cc1", "rc0", "rc1", k("ex")], [k("cv")], k("bD"))
+        cp(B["lc"][:, 16 * j - 16:16 * j], cv, [k("cv")], [k("lc%d" % j)], 16, [k("bD")])
+        (vg if XV else ag)(B["xe"][:], B["aw"][:, a0:a0 + 2048], B["lc"][:, 16 * j - 16:16 * j - 8], [ka(m) for m in CH[:-1]] + [k("lc%d" % j)], [k("xe")], 128)
+        middle(h, B, k, s, ks, j)
+
+    def tail(t, h):
+        cur_h[0] = h
+        B, par = H[h], t % 2
+        k = lambda s: s + "_%d" % h
+        nz, news = B["nz"], ["new%d%d" % (h, j) for j in range(5)]
+        kS, kN, w0 = "S%d%d" % (h, par), "S%d%d" % (h, 1 - par), 2048 * par
+        win = B["pool"][:, w0:w0 + 4096]
+        ts(nz[:, 0:64], B["lc"][:], 128.0, None, ALU.is_ge, None, [k("lc%d" % j) for j in range(1, 5)], [k("nz")], 64)
+        tt(nz[:, 0:64], nz[:, 0:64], B["lw"][:], MU, [k("nz"), k("lw")], [k("nz")], 64)
+        tt(nz[:, 64:96], nz[:, 0:32], nz[:, 32:64], ALU.max, [k("nz")], [k("n2")], 32)
+        tt(nz[:, 96:104], nz[:, 64:72], nz[:, 80:88], ALU.max, [k("n2")], [k("n3")], 8)
+        tt(nz[:, 104:112], T.bc[:, 32:40], nz[:, 96:104], ALU.subtract, ["bc4", k("n3")], [k("n4")], 8)
+        cp(B["ls"][:, 16:24], nz[:, 104:112], [k("n4")], [k("lsel")], 8)
+        tg(B["dz"][:], win, B["ls"][:, 8:16], B["z"][:, 128 * t:128 * t + 128], ALU.subtract, news + [kS, k("l15"), "z%d%d" % (h, t)], [k("dz")], 128)
+        act(B["aw"][:, 8192:8320], B["dz"][:], AF.Abs, [k("dz")], [k("alt")], 128)
+        zs = B["zs"][:, 128 * t:128 * t + 128]
+        ag(zs, B["aw"][:, 0:8320], B["ls"][:, 16:24], [k("a%d%d" % (j, c)) for j in range(1, 5) for c in range(len(CH) - 1)] + [k("alt"), k("lsel")], [k("zs%d" % t)], 128)
+        dst = T.cores[(rank + 1 + t % 3) % len(T.cores)]
+        rid, pid, _ = topo.addr(dst)
+        sem = "in%d" % (2 * t + h)
+        land = B["z"][:, 128 * t + 128:128 * t + 256]
+        snd = op("G", lambda: g.remote_dma(land, zs, T.sem[sem], T.sem.sent, pid, rid, topo.mask(core, dst)), [k("zs%d" % t)], [], 500, sem="remote")
+        src = T.cores[(rank - 1 - t % 3) % len(T.cores)]
+        op("N", len(topo.engines(src, core)), [], ["z%d%d" % (h, t + 1)], 0, sem=sem, after=[(snd, NET)])
+        if t < 3:
+            ts(T.cn[:, 8 * h:8 * h + 8], nz[:, 96:104], 0.0, None, ALU.is_gt, None, [k("n3")], ["cn%d" % h], 8)
+        n0 = 4096 * (1 - par)
+        nb = 4 if t == 3 else RB
+        w = 2048 // nb
+        for c in range(nb):
+            o, lst = B["pool"][:, n0 + w * c:n0 + w * c + w], B["ru"][:, w * c // 16:w * (c + 1) // 16]
+            (vg if c >= nb - (2 if t == 3 else RV[h]) else ag)(o, win, lst, news + [kS, k("ru"), kN], [k("rb%d" % c)], w)
+            if t == 3:
+                dma("Y", T.so[:, 2048 * h + w * c:2048 * h + w * c + w], o, [k("rb%d" % c)], [], 2200 + w)
+        last_w[kN] = op("N", None, [k("rb%d" % c) for c in range(nb)], [], 0)
+        place(h, B, k, 4, B["ci"][:, 512:640], B["lc"][:, 56:64], k("lc4"))
+        Y = B["bG"][:, 128:256]
+        mm([(Y, T.shf[:], B["KL"][:, 128:256], True, False, 128)], ["shf", k("L")], [k("G")], k("bG"), True)
+        mm([(Y, T.idf[:], B["KL"][:, 0:128], False, False, 128)], ["idf", k("K")], [k("G")], k("bG"), True)
+        for j in range(5):
+            mm([(Y, T.idf[:], B["pl"][:, 128 * j:128 * j + 128], False, j == 4, 128)], ["idf", k("pl%d" % j)], [k("G")], k("bG"), True)
+        act(B["M"][:], Y, AF.Copy, [k("G")], ["M%d" % h], 128, [k("bG")])
+        if t == 3:
+            dma("Y", T.mo[:, 128 * h:128 * h + 128], B["M"][:], ["M%d" % h], [], 2500)
+            dma("Y", T.zo[:, 128 * h:128 * h + 128], B["z"][:, 512:640], ["z%d4" % h], [], 2500)
+
+    for t in range(4):
+        for h in (0, 1):
+            head(t, h)
+        for j in range(1, 5):
+            for h in (0, 1):
+                corr(t, h, j)
+        for h in (0, 1):
+            tail(t, h)
+        if t < 3:
+            cn, cni = T.cn, T.cni
+            op("V", lambda: V.tensor_reduce(cn[:, 16:17], cn[:, 0:16], AX.X, AD), ["cn0", "cn1"], ["cs"], vc(16))
+            cp(T.cb[:, 0:1], cn[:, 16:17], ["cs"], ["cb"], 1)
+            mm([(T.bM1[:, 144:145], T.one[:], T.cb[:, 0:1], True, True, 1)], ["one", "cb"], ["ct"], "bM_1")
+            cp(cni[:, 0:1], T.bM1[:, 144:145], ["ct"], ["cni0"], 1, ["bM_1"])
+            ts(cni[:, 4:5], cni[:, 0:1], 63, None, ALU.bitwise_and, None, ["cni0"], ["cni4"], 1)
+            ts(cn[:, 20:21], cni[:, 4:5], 32.0, None, MU, None, ["cni4"], ["a32"], 1)
+            ts(T.b1[:, 4 * t + 4:4 * t + 8], T.kj[:, 0:4], cn[:, 20:21], None, AD, None, ["b10", "a32"], ["b1%d" % (t + 1)], 4)
+
+
+def lat(ops, a, b):
+    x = ops[b]["deps"][a]
+    if x:
+        return x
+    ea, eb = ops[a]["e"], ops[b]["e"]
+    if eb == "N":
+        return 0.0
+    if ea == eb and not ops[a]["sem"]:
+        return 0.0 if ea == "P" else SAME
+    return HOP
+
+
+def schedule(ops):
+    n = len(ops)
+    fw, bw = [[] for _ in range(n)], [[] for _ in range(n)]
+    for i, o in enumerate(ops):
+        for d in o["deps"]:
+            fw[d].append((i, lat(ops, d, i)))
+            bw[i].append((d, lat(ops, d, i)))
+    pr = [0.0] * n
+    for i in range(n - 1, -1, -1):
+        pr[i] = ops[i]["cost"] + max([pr[s] + l for s, l in fw[i]], default=0.0)
+    pr = [pr[i] - BONUS * ops[i]["h"] for i in range(n)]
+    best, x = None, SEED
+    for p in range(PASSES):
+        order, fin = listed(ops, fw, pr)
+        if best is None or max(fin) <= best[1]:
+            best = (order, max(fin), fin)
+        if p >= 4:
+            fin = list(best[2])
+            x = (x * 1103515245 + 12345) % 2147483648
+            a = best[1] * x / 2147483648
+            x = (x * 1103515245 + 12345) % 2147483648
+            sh = SHIFT * (x / 1073741824 - 1)
+            for i in range(n):
+                if abs(fin[i] - a) < SPAN:
+                    x = (x * 1103515245 + 12345) % 2147483648
+                    fin[i] += NOISE * x / 2147483648 + sh * ops[i]["h"]
+        pr = listed(ops, bw, fin)[1] if p % 2 else [ops[i]["cost"] - fin[i] for i in range(n)]
+    return best[:2]
+
+
+PLAN = {}
+
+
+def listed(ops, edges, pr):
+    n = len(ops)
+    left = [0] * n
+    for i in range(n):
+        for s, _ in edges[i]:
+            left[s] += 1
+    rdy, fin = [0.0] * n, [0.0] * n
+    free = {e: 0.0 for e in "VAPGYN"}
+    cand = {e: [] for e in free}
+    for i in range(n):
+        if not left[i]:
+            cand[ops[i]["e"]].append(i)
+    order = []
+    while len(order) < n:
+        t0, e = min((max(free[e], min(rdy[i] for i in cand[e])), e) for e in free if cand[e])
+        i = max((x for x in cand[e] if rdy[x] <= t0 + LOOK), key=lambda x: (pr[x], -x))
+        cand[e].remove(i)
+        t0 = max(t0, rdy[i])
+        fin[i] = t0 + ops[i]["cost"]
+        free[e] = t0 + 60.0 if e in "YN" else fin[i]
+        order.append(i)
+        for s, l in edges[i]:
+            rdy[s] = max(rdy[s], fin[i] + l)
+            left[s] -= 1
+            if not left[s]:
+                cand[ops[s]["e"]].append(s)
+    return order, fin
+
+
+def rank_program(g, core, T, topo):
+    if T.rank_of(core) is None:
+        return
+    ops = []
+    build(g, core, T, topo, ops)
+    if "order" not in PLAN:
+        PLAN["order"] = schedule(ops)[0]
+    order = PLAN["order"]
+    Q = {"V": g.vector, "A": g.scalar, "P": g.tensor, "G": g, "Y": g.sync}
+    know = {e: {} for e in Q}
+    cnt, mark, clock, join = {}, {}, {}, {}
+    sent = 0
+    for i in order:
+        o = ops[i]
+        e = o["e"]
+        if e == "N" and o["fn"] is None:
+            join[i] = list(o["deps"])
+            continue
+        if e == "N":
+            mark[i], clock[i] = (o["sem"], o["fn"]), {o["sem"]: o["fn"]}
+            cnt[o["sem"]] = o["fn"]
+            continue
+        kn = know[e]
+        need = [x for d in o["deps"] for x in join.get(d, [d]) if not (e == "P" and ops[x]["e"] == "P")]
+        for d in sorted(need, key=lambda d: -mark[d][1]):
+            s, v = mark[d]
+            if kn.get(s, 0) < v and not any(clock[x].get(s, 0) >= v for x in need if mark[x][0] != s):
+                Q[e].wait_ge(T.sem[s], v)
+                kn[s] = v
+        for d in need:
+            for s, v in clock[d].items():
+                kn[s] = max(kn.get(s, 0), v)
+        ins = o["fn"]()
+        if o["sem"] == "remote":
+            sent += 1
+            mark[i], clock[i] = ("sent", 0), {}
+            continue
+        s, inc = (o["sem"], 16) if o["sem"] else ("q" + e, 1)
+        ins.then_inc(T.sem[s], inc)
+        cnt[s] = cnt.get(s, 0) + inc
+        mark[i] = (s, cnt[s])
+        clock[i] = dict(kn)
+        clock[i][s] = cnt[s]
+    cores = T.cores
+    r = T.rank_of(core)
+    g.wait_ge(T.sem.sent, sum(2 * len(topo.engines(core, cores[(r + 1 + t % 3) % len(cores)])) for t in range(4)))
+    for s in sorted(cnt):
+        g.wait_ge(T.sem[s], cnt[s])

@@ -1,38 +1,43 @@
 from concourse.mybir import AluOpType as ALU, ActivationFunctionType as AF, AxisListType as AX
 
-NS = 2
-CH = (0, 4, 10, 16)
-VB = (0, 4, 6, 10, 14, 16)
-IX = 10
-XV = 0
-RB, RV = 8, (0, 5)
+PARTS = (128, 128)
+NS = 4
+CH = (0, 4, 8, 12, 16)
+VB = (0, 4, 8, 12, 16)
+IX = 12
 GV = 4
-PLS = 1
-BONUS, LOOK, PASSES, NOISE, SEED, SHIFT, SPAN = 2000.0, 60.0, 200, 300.0, 1, 1000.0, 6000.0
+NC = 4
+MV = 1
+EX = 1
+RB, RV = 8, (0, 5)
+BONUS, LOOK, PASSES, NOISE, SEED, SHIFT, SPAN = 2000.0, 60.0, 230, 300.0, 5, 1000.0, 6000.0
 HOP, SAME, NET = 110.0, 70.0, 3500.0
 GC, VF, PEC = 1.55 * 0.83 * 1.15, 0.83 * 1.2, 0.45
 MAGIC = 12582912.0
-BF, F32, I32, U16 = "bfloat16", "float32", "int32", "uint16"
+BF, F32, I32, U16, F16 = "bfloat16", "float32", "int32", "uint16", "float16"
 
 SCRATCH = {"X": ("sbuf", [128, 4096], BF), "nmi": ("sbuf", [128, 256], I32), "wk": ("sbuf", [128, 16], I32)}
-for _n, _w, _d in [("xf", 144, F32), ("mc", 128, BF), ("xg", 128, F32), ("xm", 128, F32), ("pi", 16, I32), ("col", 16, F32),
-                   ("big", 144, BF), ("bigf", 144, F32), ("wbig", 144, BF), ("idp", 128, BF), ("idn", 128, BF), ("idh", 128, BF),
-                   ("idf", 128, F32), ("shf", 128, F32), ("bof", 128, F32), ("bo8", 32, BF), ("dm", 128, BF), ("rst", 128, F32),
-                   ("c128", 128, BF), ("cq", 128, BF), ("one", 128, BF), ("kd", 128, F32), ("kr", 128, F32), ("rl", 16, U16),
-                   ("rli", 16, I32), ("rs", 8, F32), ("ib", 8, F32), ("rg0", 128, BF), ("rg1", 128, BF), ("cg0", 128, BF),
-                   ("cg1", 128, BF), ("rc", 16, BF), ("cc", 16, BF), ("et", 32, BF), ("eb", 32, BF), ("tb", 128, F32), ("i16", 128, F32),
-                   ("wj", 64, F32), ("kj", 8, F32), ("b1", 16, F32), ("cn", 32, F32), ("cni", 16, I32), ("bc", 48, F32), ("cb", 16, BF)]:
+for _n, _w, _d in [("xf", 144, F32), ("mc", 128, BF), ("xg", 128, F32), ("xm", 256, F32), ("pi", 16, I32), ("col", 16, F32),
+                   ("big", 144, BF), ("bigh", 144, F16), ("wbig", 144, BF), ("wbh", 144, BF), ("mc2", 128, BF), ("ce", 32, BF),
+                   ("idc", 512, BF), ("idp", 128, BF), ("idn", 128, BF), ("idh", 128, BF), ("idf", 128, F32), ("shf", 128, F32),
+                   ("bof", 128, F32), ("bo8", 32, BF), ("dm", 128, BF), ("rst", 128, F32), ("c128", 128, BF), ("cq", 128, BF),
+                   ("one", 128, BF), ("kr", 256, F32), ("rl", 32, U16), ("rli", 16, I32), ("rs", 8, F32), ("ib", 32, F32),
+                   ("rg0", 128, BF), ("rg1", 128, BF), ("cg0", 128, BF), ("cg1", 128, BF), ("rc", 32, BF), ("cc", 16, BF),
+                   ("et", 32, BF), ("eb", 32, BF), ("dq", 640, BF), ("tb", 128, F32), ("i16", 128, F32), ("wj", 128, F32),
+                   ("kj", 8, F32), ("b1", 16, F32), ("cn", 48, F32), ("cni", 16, I32), ("bc", 64, F32), ("cb", 16, BF)]:
     SCRATCH[_n] = ("sbuf", [128, _w], _d)
+PER = [("pool", 6144, BF), ("aw", 8320, BF), ("mn", 2048, BF), ("z", 640, BF), ("zs", 512, BF), ("xe", 128, BF),
+       ("run", 128, F32), ("si", 96, I32), ("ex", 128, BF), ("lu", 144, U16), ("sm", 192, F32), ("p1", 128, F32), ("p2", 128, I32),
+       ("ci", 640, I32), ("cu", 640, U16), ("M", 1664, F32), ("P", 640, F32), ("em", 512, BF), ("lw", 64, F32), ("fb", 144, BF),
+       ("pl", 640, F32), ("Qh", 512, F16)]
 for _h in "01":
-    for _n, _w, _d in [("pool", 6144, BF), ("aw", 8320, BF), ("mn", 2048, BF), ("z", 640, BF), ("zs", 512, BF), ("xe", 128, BF),
-                       ("run", 128, F32), ("ti", 32, I32), ("ex", 128, BF), ("lg", 48, U16), ("lc", 64, U16), ("ls", 32, U16),
-                       ("sm", 64, F32), ("si", 64, I32), ("p1", 128, F32), ("p2", 128, I32), ("ci", 640, I32), ("cu", 512, U16),
-                       ("M", 128, F32), ("Q", 512, F32), ("KL", 256, F32), ("P", 640, F32), ("pl", 640, F32), ("em", 640, BF),
-                       ("rf", 128, F32), ("ru", 128, U16), ("lw", 64, F32), ("nz", 128, F32), ("dz", 128, BF)]:
+    for _n, _w, _d in PER:
         SCRATCH[_n + _h] = ("sbuf", [128, _w], _d)
-    for _n in ("bS", "bD", "bM", "bG"):
+    for _n in ("bS", "bD", "bM"):
         SCRATCH[_n + _h] = ("psum", [128, 512], F32)
-SEMAPHORES = (["qV", "qA", "qP", "qG", "sent"] + ["d%d" % i for i in range(32)] + ["in%d" % i for i in range(8)])
+for _h in "01":
+    SCRATCH["bG" + _h] = ("psum", [128, 512], F32)
+SEMAPHORES = (["qV", "qA", "qP", "qG", "sent"] + ["d%d" % i for i in range(32)] + ["in%d" % i for i in range(12)])
 
 
 def build(g, core, T, topo, ops):
@@ -96,8 +101,10 @@ def build(g, core, T, topo, ops):
     def vg(out, win, lst, r, w, n):
         return op("V", lambda: V.tensor_copy(out, win.indirect(lst)), r, w, 55 + n * GC)
 
-    def act(out, in_, f, r, w, n, banks=()):
-        return op("A", lambda: A.activation(out, in_, f), r, w, 70 + n * VF, banks)
+    def act(out, in_, f, r, w, n, banks=(), bias=None):
+        if bias is None:
+            return op("A", lambda: A.activation(out, in_, f), r, w, 70 + n * VF, banks)
+        return op("A", lambda: A.activation(out, in_, f, bias=bias), r, w, 70 + n * VF, banks)
 
     def mm(lst, r, w, bk, fp32=False):
         def fn():
@@ -111,36 +118,45 @@ def build(g, core, T, topo, ops):
             return op("G", lambda: g.iota(out, pat, base, cm, allow_small_or_imprecise_dtypes=True), [], w, 130 + 2 * n)
         return op("G", lambda: g.iota(out, pat, base, cm), [], w, 130 + 2 * n)
 
+    def diag(out, s, k):
+        io(out, [[0, 128]], s, 0, [k], 128)
+        op("G", lambda: g.affine_select(out, out, [[-1, 128]], ALU.is_equal, 0.0, 0, 1), [k], [k], 430)
+
     nd = [0]
 
-    def dma(q, out, in_, r, w, cost):
+    def dma(out, in_, r, w, cost):
         s = "d%d" % nd[0]
         nd[0] += 1
-        Q = g.sync if q == "Y" else A
-        return op(q, lambda: Q.dma_start(out, in_), r, w, cost, sem=s)
+        return op("Y", lambda: g.sync.dma_start(out, in_), r, w, cost, sem=s)
 
-    H = [{n: T[n + h] for n in ("pool aw mn z zs xe run ti ex lg lc ls sm si p1 p2 ci cu M Q KL P pl em rf ru lw nz dz "
-                                "bS bD bM bG").split()} for h in "01"]
+    NP = len(PARTS)
+    sizes = sorted(set(PARTS))
+    H = []
+    for h in range(NP):
+        B = {n: T[n + str(h)] for n in [x[0] for x in PER] + ["bS", "bD", "bM"]}
+        B.update({"bG": T["bG%d" % (h % 2)], "n": PARTS[h], "i0": sum(PARTS[:h]), "v": sizes.index(PARTS[h])})
+        H.append(B)
     X, col = T.X, T.col
+    XK = ["X%d" % h for h in range(NP)]
 
-    for h in (0, 1):
-        dma("Y", H[h]["z"][:, 0:128], T.arr[:, 128 * h:128 * h + 128], [], ["z%d0" % h], 2200)
-        dma("Y", H[h]["pool"][:, 0:2048], T.st[:, 2048 * h:2048 * h + 2048], [], ["S%d0" % h], 4000 + 2000 * h)
+    for h, B in enumerate(H):
+        n, i0 = B["n"], B["i0"]
+        dma(B["z"][:, 0:n], T.arr[:, i0:i0 + n], [], ["z%d0" % h], 2200)
+        dma(B["pool"][:, 0:16 * n], T.st[:, 16 * i0:16 * (i0 + n)], [], ["S%d0" % h], 3500 + 1300 * h)
         if h == 0:
-            dma("Y", T.wk[:, 0:1], T.wt[:], [], ["wk0"], 2200)
-            dma("Y", T.wk[:, 8:9], T.kap[:], [], ["wk8"], 2200)
-            dma("Y", T.nmi[:], T.nm[:], [], ["nmi"], 4500)
-    for h in (0, 1):
-        dma("Y", X[:, 2048 * h:2048 * h + 2048], T.rec[:, 2048 * h:2048 * h + 2048], [], ["X%d" % h], 8000 + 2000 * h)
+            dma(T.wk[:, 0:1], T.wt[:], [], ["wk0"], 2200)
+            dma(T.wk[:, 8:9], T.kap[:], [], ["wk8"], 2200)
+            dma(T.nmi[:], T.nm[:], [], ["nmi"], 4500)
+    for h, B in enumerate(H):
+        n, i0 = B["n"], B["i0"]
+        dma(X[:, 16 * i0:16 * (i0 + n)], T.rec[:, 16 * i0:16 * (i0 + n)], [], ["X%d" % h], 7500 + 1300 * h)
 
     io(T.pi[:, 0:1], [[1, 1]], 0, 1, ["pi0"], 1, False)
     io(T.xf[:], [[1, 144]], 0, 0, ["xf"], 144)
     io(T.mc[:], [[0, 8], [1, 16]], 0, 0, ["mc"], 128)
     io(T.xg[:], [[16, 8], [0, 16]], 0, 0, ["xg"], 128)
-    io(T.xm[:], [[1, 16], [0, 8]], 0, 0, ["xm"], 128)
     io(T.i16[:], [[16, 128]], 0, 0, ["i16"], 128)
-    io(T.rli[:, 0:8], [[1, 8]], 0, 0, ["rli0"], 8, False)
-    io(T.rli[:, 8:16], [[0, 8]], 0, 1, ["rli8"], 8, False)
+    io(T.one[:], [[0, 128]], 1, 0, ["one"], 128)
     ts(T.pi[:, 4:5], T.pi[:, 0:1], 15, None, ALU.bitwise_and, None, ["pi0"], ["pi4"], 1)
     cp(col[:, 0:1], T.pi[:, 0:1], ["pi0"], ["c0"], 1)
     cp(col[:, 1:2], T.pi[:, 4:5], ["pi4"], ["c1"], 1)
@@ -155,12 +171,18 @@ def build(g, core, T, topo, ops):
     ts(T.idp[:], x128, col[:, 0:1], None, EQ, None, ["xf", "c0"], ["idp"], 128)
     ts(T.idn[:], x128, col[:, 0:1], -1.0, EQ, MU, ["xf", "c0"], ["idn"], 128)
     ts(T.idh[:], x128, col[:, 0:1], 0.5, EQ, MU, ["xf", "c0"], ["idh"], 128)
-    ts(T.idf[:], x128, col[:, 0:1], None, EQ, None, ["xf", "c0"], ["idf"], 128)
+    diag(T.idf[:], 1, "idf")
     ts(T.shf[:], x128, col[:, 4:5], col[:, 5:6], EQ, MU, ["xf", "c4", "c5"], ["shf"], 128)
     ts(T.bof[:], T.xg[:], col[:, 2:3], None, EQ, None, ["xg", "c2"], ["bof"], 128)
     ts(T.big[:], T.xf[:], col[:, 3:4], None, EQ, None, ["xf", "c3"], ["big"], 144)
-    ts(T.bigf[:], T.xf[:], col[:, 3:4], None, EQ, None, ["xf", "c3"], ["bigf"], 144)
+    ts(T.bigh[:], T.xf[:], col[:, 3:4], None, EQ, None, ["xf", "c3"], ["bigh"], 144)
+    io(col[:, 8:9], [[0, 1]], -2048, 0, ["c8"], 1)
     ts(T.wbig[:], T.xf[:], col[:, 3:4], col[:, 6:7], EQ, MU, ["xf", "c3", "c6"], ["wbig"], 144)
+    if EX:
+        ts(T.mc2[:], T.mc[:], -7.5, None, AD, None, ["mc"], ["mc2"], 64)
+    if MV:
+        ts(T.wbh[:], T.wbig[:], 0.5, None, MU, None, ["wbig"], ["wbh"], 72)
+        ms(col[:, 14:15], -0.5, ["c14"], 1)
     ts(T.rs[:], T.xf[:, 0:128:16], col[:, 2:3], None, EQ, None, ["xf", "c2"], ["rs"], 8)
     for b, s in enumerate((16.0, -32.0, 32.0, -16.0)):
         ts(T.bo8[:, 8 * b:8 * b + 8], T.rs[:], s, None, MU, None, ["rs"], ["bo%d" % b], 8)
@@ -168,46 +190,59 @@ def build(g, core, T, topo, ops):
     ts(T.rst[:], T.mc[:], 0.0, 1048576.0, EQ, MU, ["mc"], ["rst"], 128)
     ms(T.c128[:], 2.0 ** -7, ["c128"], 128)
     ms(T.cq[:], -2.0 ** -9, ["cq"], 128)
-    ms(T.one[:], 1.0, ["one"], 128)
-    ts(T.rli[:, 8:16], T.rli[:, 8:16], 7, None, ALU.bitwise_and, None, ["rli8"], ["rli8"], 8)
-    cp(T.rl[:], T.rli[:], ["rli0", "rli8"], ["rl"], 16)
-    repg, repr_ = T.rl[:, 0:8], T.rl[:, 8:16]
-    ts(T.ib[:], T.xf[:, 0:128:16], col[:, 1:2], None, AD, None, ["xf", "c1"], ["ib"], 8)
-    ts(T.kd[:], T.xm[:], col[:, 1:2], col[:, 7:8], EQ, MU, ["xm", "c1", "c7"], ["kd"], 128)
-    mm([(T.bG1[:, 0:128], T.bof[:], T.kd[:], True, True, 128)], ["bof", "kd"], ["kp"], "bG_1", True)
-    cp(T.kr[:], T.bG1[:, 0:128], ["kp"], ["kr"], 128, ["bG_1"])
+    cp(T.rl[:, 0:8], T.xf[:, 0:8], ["xf"], ["rl"], 8)
+    ib = T.ib[:, 0:8]
+    ts(ib, T.xf[:, 0:128:16], col[:, 1:2], None, AD, None, ["xf", "c1"], ["ib"], 8)
+    io(T.wj[:], [[0, 128]], 0, 0, ["wj"], 128)
+    io(T.cn[:], [[0, 48]], 0, 0, ["cn%d" % h for h in range(NP)], 48)
+    for v, n in enumerate(sizes):
+        nr = n // 16
+        xm, kr = T.xm[:, 128 * v:128 * v + n], T.kr[:, 128 * v:128 * v + n]
+        io(xm, [[1, 16], [0, nr]], 0, 0, ["xm%d" % v], n)
+        ts(xm, xm, col[:, 1:2], col[:, 7:8], EQ, MU, ["xm%d" % v, "c1", "c7"], ["xm%d" % v], n)
+        mm([(T.bG1[:, 0:n], T.bof[:], xm, True, True, n)], ["bof", "xm%d" % v], ["G1"], "bG1", True)
+        cp(kr, T.bG1[:, 0:n], ["G1"], ["kr%d" % v], n, ["bG1"])
+        ts(T.rli[:, 8 * v:8 * v + 8], ib, -(nr - 1) / 2.0, 1.0 / nr, AD, MU, ["ib"], ["rli%d" % v], 8)
+        tm = T.ib[:, 8 + 8 * v:16 + 8 * v]
+        ts(tm, T.rli[:, 8 * v:8 * v + 8], -float(nr), None, MU, None, ["rli%d" % v], ["ibm%d" % v], 8)
+        tt(tm, tm, ib, AD, ["ib", "ibm%d" % v], ["ibm%d" % v], 8)
+        cp(T.rl[:, 8 + 8 * v:16 + 8 * v], tm, ["ibm%d" % v], ["rp%d" % v], 8)
+        for b, s in enumerate((n, nr)):
+            if EX:
+                ms(T.ce[:, 16 * v + 8 * b:16 * v + 8 * b + 8], 7.5 * s, ["ce%d%d" % (v, b)], 8)
+                diag(T.idc[:, 256 * v + 128 * b:256 * v + 128 * b + 128], s, "idc%d%d" % (v, b))
+            else:
+                ts(T.rc[:, 16 * v + 8 * b:16 * v + 8 * b + 8], T.rs[:], float(s), None, MU, None, ["rs"], ["rc%d%d" % (v, b)], 8)
+        for j in range(1, 5):
+            io(T.wj[:, 64 * v + 16 * j - 16:64 * v + 16 * j - 8], [[0, 8]], (5 - j) * 16 * n, 0, ["wj"], 8)
     ts(T.kj[:, 4:8], T.xf[:, 1:5], 32.0, None, MU, None, ["xf"], ["kj4"], 4)
-    ts(T.kj[:, 0:4], T.kj[:, 4:8], T.kr[:, 0:1], -262156.0, MU, AD, ["kj4", "kr"], ["b10"], 4)
-    ts(T.rc[:, 0:8], T.rs[:], 128.0, None, MU, None, ["rs"], ["rc0"], 8)
-    ts(T.rc[:, 8:16], T.rs[:], 8.0, None, MU, None, ["rs"], ["rc1"], 8)
-    cp(T.cc[:, 0:8], T.ib[:], ["ib"], ["cc0"], 8)
+    ts(T.kj[:, 0:4], T.kj[:, 4:8], T.kr[:, 0:1], -262156.0, MU, AD, ["kj4", "kr0"], ["b10"], 4)
+    cp(T.cc[:, 0:8], ib, ["ib"], ["cc0"], 8)
     cp(T.cc[:, 8:16], T.xf[:, 0:8], ["xf"], ["cc1"], 8)
     ms(T.rg0[:, 64:128], 0.0, ["rg0"], 64)
-    ms(T.cg0[:, 64:128], 99.0, ["cg0"], 64)
-    ms(T.wj[:], 0.0, ["wj"], 64)
+    io(T.cg0[:, 64:128], [[1, 4], [99, 2], [0, 8]], 1, 0, ["cg0"], 64)
+    io(T.cg0[:, 8:48], [[1, 5], [0, 8]], 0, 0, ["cg0_1"], 40)
     for b in (0, 1, 2, 3, 4, 5, 7, 8, 10, 12, 14):
         cp(T.rg0[:, 8 * b:8 * b + 8], T.rs[:], ["rs"], ["rg0"] if b > 7 else ["rg0_%d" % b], 8)
-    ts(T.cg0[:, 0:8], T.ib[:], 16.0, None, MU, None, ["ib"], ["cg0_0"], 8)
-    for j in range(5):
-        ms(T.cg0[:, 8 + 8 * j:16 + 8 * j], j, ["cg0_%d" % (j + 1)], 8)
-        if j:
-            ms(T.cg0[:, 48 + 16 * j:56 + 16 * j], j, ["cg0"], 8)
-            ms(T.wj[:, 16 * j - 16:16 * j - 8], (5 - j) * 2048, ["wj"], 8)
+    ts(T.cg0[:, 0:8], ib, 16.0, None, MU, None, ["ib"], ["cg0_0"], 8)
     ts(T.rg0[:, 48:56], T.rs[:], 4096.0, None, MU, None, ["rs"], ["rg0_6"], 8)
-    ms(T.cg0[:, 48:56], -40960.0, ["cg0_6"], 8)
-    ts(T.cg0[:, 56:64], T.ib[:], 16.0, 2048.0, MU, AD, ["ib"], ["cg0_7"], 8)
+    io(T.cg0[:, 48:56], [[0, 8]], -40960, 0, ["cg0_6"], 8)
+    ts(T.cg0[:, 56:64], ib, 16.0, 2048.0, MU, AD, ["ib"], ["cg0_7"], 8)
     RG = [["rg0"] + ["rg0_%d" % b for b in range(8)], ["rg1"]]
     CG = [["cg0"] + ["cg0_%d" % b for b in range(8)], ["cg1"]]
     cp(T.rg1[:], T.rg0[:], RG[0], ["rg1"], 64)
     cp(T.cg1[:], T.cg0[:], CG[0], ["cg1"], 64)
     ts(T.rg1[:, 48:56], T.rs[:], -4096.0, None, MU, None, ["rs"], ["rg1"], 8)
     ms(T.cg1[:, 48:56], 45056.0, ["cg1"], 8)
-    ts(T.cg1[:, 56:64], T.ib[:], 16.0, None, MU, None, ["ib"], ["cg1"], 8)
-    for b, (s, a) in enumerate(((16.0, 0.0), (16.0, 2048.0), (16.0, 15.0), (16.0, 2063.0), (1.0, 8192.0))):
-        ts(T.bc[:, 8 * b:8 * b + 8], T.ib[:], s, a, MU, AD, ["ib"], ["bc%d" % b], 8)
+    ts(T.cg1[:, 56:64], ib, 16.0, None, MU, None, ["ib"], ["cg1"], 8)
+    for b, (s, a) in enumerate([(16.0, 16.0 * B["i0"]) for B in H] + [(16.0, 15.0), (16.0, 2063.0)] + [(1.0, 64.0 * n) for n in sizes]):
+        ts(T.bc[:, 8 * b:8 * b + 8], ib, s, a, MU, AD, ["ib"], ["bc%d" % b], 8)
     tb = T.tb
     ts(T.et[:], T.xf[:, 0:32], col[:, 1:2], None, EQ, None, ["xf", "c1"], ["et"], 32)
-    ts(T.eb[:], T.et[:], -1.0, 8192.0, AD, MU, ["et"], ["eb"], 32)
+    ts(T.eb[:, 0:16], T.xf[:, 0:16], col[:, 1:2], None, ALU.subtract, None, ["xf", "c1"], ["eb"], 16)
+    for j in range(5):
+        diag(T.dq[:, 128 * j:128 * j + 128], -16384 * j if j else -8192, "dq%d" % j)
+        io(col[:, 9 + j:10 + j], [[0, 1]], -8192 * j * j, 0, ["c%d" % (9 + j)], 1)
     ts(tb[:, 0:16], T.xf[:, 0:16], col[:, 1:2], None, ALU.subtract, None, ["xf", "c1"], ["t0"], 16)
     ts(tb[:, 16:32], tb[:, 0:16], -4.0, None, ALU.is_lt, None, ["t0"], ["keep"], 16)
     ts(tb[:, 32:48], tb[:, 0:16], 0.0, None, ALU.is_ge, None, ["t0"], ["le"], 16)
@@ -221,219 +256,267 @@ def build(g, core, T, topo, ops):
         tt(tm, tm, al, ALU.subtract, ["tm", k], ["tm"], 16)
         tt(tm, tm, tb[:, 64:80], MU, ["tm", "old"], ["tm"], 16)
         tt(al, al, tm, AD, ["tm", k], [k], 16)
-    for h in (0, 1):
-        io(H[h]["pool"][:, 2048:4096], [[0, 2048]], 0, 0, ["new%d%d" % (h, j) for j in range(5)], 2048)
-        cp(H[h]["M"][:], T.nmi[:, 128 * h:128 * h + 128], ["nmi"], ["M%d" % h], 128)
+    for h, B in enumerate(H):
+        n, i0 = B["n"], B["i0"]
+        io(B["si"][:, 48:56], [[0, 8]], 0, 0, ["ti0_%d" % h], 8, False)
+        if EX:
+            io(B["fb"][:], [[0, 144]], 0, 0, ["fb_%d" % h], 144)
+        for c in range(11):
+            io(B["pool"][:, 2048 + c:2048 + 16 * n:16], [[0, n]], 0, 0, ["fill%d_%d" % (h, c)], n)
+        for c in range(2 if n < 128 else 0):
+            io(B["pool"][:, 2048 * c + 16 * n:2048 * c + 2048], [[0, 2048 - 16 * n]], 0, 0, ["fill%d_%d" % (h, 11 + c)], 2048 - 16 * n)
+        cp(B["M"][:, 0:n], T.nmi[:, i0:i0 + n], ["nmi"], ["M_%d" % h], n)
+        ts(B["M"][:, 128:128 + n], T.nmi[:, i0:i0 + n], -2048.0, None, AD, None, ["nmi"], ["M2_%d" % h], n)
 
-    def sel(tab, q):
-        return tab[:, 15 - q:143 - q]
+    def sel(tab, q, n=128):
+        return tab[0:n, 15 - q:143 - q]
 
-    def argmin(h, B, k):
-        D = B["bD"][:, 0:128]
-        op("V", lambda: V.tensor_tensor_scan(B["run"][:], T.rst[:], D, 0.0, AD, ALU.min), ["rst", k("D")], [k("run")], vc(128), [k("bD")])
-        cp(B["ti"][:, 8:16], B["run"][:, 15::16], [k("run")], [k("ti8")], 8)
-        ts(B["ti"][:, 0:8], B["ti"][:, 8:16], 15, None, ALU.bitwise_and, None, [k("ti8")], [k("ti0")], 8)
-        tg(B["ex"][:], B["ti"][:, 0:8], repg, T.dm[:], MU, [k("ti0"), "rl", "dm"], [k("ex")], 128)
+    def keys(h):
+        return lambda s: s + str(h % 2) if s in ("G", "bG") else s + "_%d" % h
+
+    def scan(B, k):
+        n = B["n"]
+        op("V", lambda: V.tensor_tensor_scan(B["run"][0:n, :], T.rst[0:n, :], B["bD"][0:n, 0:128], 0.0, AD, ALU.min), ["rst", k("D")], [k("run")], vc(128), [k("bD")])
+
+    def argmin(B, k):
+        n, si = B["n"], B["si"]
+        scan(B, k)
+        cp(si[0:n, 56:64], B["run"][0:n, 15::16], [k("run")], [k("ti8")], 8)
+        ts(si[0:n, 48:56], si[0:n, 56:64], 15, None, ALU.bitwise_and, None, [k("ti8")], [k("ti0")], 8)
+        tg(B["ex"][:], si[:, 48:56], T.rl[:, 0:8], T.dm[:], MU, [k("ti0"), "rl", "dm"], [k("ex")], 128)
+
+    def new(B, j):
+        return B["pool"][:, 2063 - j:2048 + 16 * B["n"]:16]
 
     def middle(h, B, k, prev, kprev, j):
-        mm([(B["bM"][:, 0:128], T.cq[:], T.one[:], True, False, 128), (B["bM"][:, 0:128], T.idh[:], prev, False, False, 128),
-            (B["bM"][:, 0:128], T.idh[:], B["xe"][:], False, True, 128)], ["cq", "one", "idh", kprev, k("xe")], [k("mid")], k("bM"))
-        ts(B["pool"][:, 2063 - j:4096:16], B["bM"][:, 0:128], MAGIC, MAGIC, AD, ALU.subtract, [k("mid")], ["new%d%d" % (h, j)], 128, [k("bM")])
+        n = B["n"]
+        o = B["bM"][:, 256:256 + n]
+        mm([(o, T.cq[:], T.one[:, 0:n], True, False, n), (o, T.idh[:], prev, False, False, n)], ["cq", "one", "idh", kprev], [k("mid")], k("bM"))
+        mm([(o, T.idh[:], B["xe"][:, 0:n], False, True, n)], ["idh", k("xe")], [k("mid")], k("bM"))
+        ts(new(B, j), o, MAGIC, MAGIC, AD, ALU.subtract, [k("mid")], [k("new%d" % j)], n, [k("bM")])
 
-    def place(h, B, k, j, win, lst, kl):
-        tg(B["P"][:, 128 * j:128 * j + 128], win, lst, T.dm[:], MU, [k("ci%d" % j), k("cj%d0" % j), k("cj%d1" % j), kl, "dm"], [k("P%d" % j)], 128)
-        if PLS:
-            mm([(B["bG"][:, 0:128], T.idp[:], B["em"][:, 128 * j:128 * j + 128], True, False, 32),
-                (B["bG"][:, 0:128], T.bof[:], B["P"][:, 128 * j:128 * j + 128], False, True, 128)], ["bof", "idp", k("em"), k("P%d" % j)], [k("G")], k("bG"), True)
-            act(B["pl"][:, 128 * j:128 * j + 128], B["bG"][:, 0:128], AF.Relu, [k("G")], [k("pl%d" % j)], 128, [k("bG")])
-            return
-        mm([(B["bG"][:, 0:128], T.bof[:], B["P"][:, 128 * j:128 * j + 128], True, True, 128)], ["bof", k("P%d" % j)], [k("G")], k("bG"), True)
-        tt(B["pl"][:, 128 * j:128 * j + 128], B["bG"][:, 0:128], B["em"][:, 128 * j:128 * j + 128], MU, [k("G"), k("em")], [k("pl%d" % j)], 128, [k("bG")])
+    def place(B, k, j, win, lst, kl):
+        n = B["n"]
+        Pj, G = B["P"][:, 128 * j:128 * j + n], B["bG"][:, 0:n]
+        tg(Pj, win, lst, T.dm[:, 0:n], MU, [k("ci%d" % j), k("cj%d" % j), k("cj%dx" % j), kl, "dm"], [k("P%d" % j)], n)
+        mm([(G, T.dq[:, 0:128], B["em"][:, 128:128 + n], True, False, 32)]
+           + ([(G, T.dq[:, 128 * j:128 * j + 128], B["em"][:, 0:n], False, False, 32)] if j else [])
+           + [(G, T.bof[:], Pj, False, True, n)], ["bof", "dq0", "dq%d" % j, k("em"), k("en"), k("P%d" % j)], [k("G")], k("bG"), True)
+        act(B["pl"][:, 128 * j:128 * j + n], G, AF.Relu, [k("G"), "c%d" % (9 + j)], [k("pl%d" % j)], n, [k("bG")], col[:, 9 + j:10 + j])
 
     def head(t, h):
         cur_h[0] = h
-        B, par = H[h], t % 2
-        k = lambda s: s + "_%d" % h
-        z, kz, kS = B["z"][:, 128 * t:128 * t + 128], "z%d%d" % (h, t), "S%d%d" % (h, par)
+        B, par, k = H[h], t % 2, keys(h)
+        n, i0, v, si, sm, lu, M, bD = B["n"], B["i0"], B["v"], B["si"], B["sm"], B["lu"], B["M"], B["bD"]
+        nr = n // 16
+        z, kz, kS = B["z"][:, 128 * t:128 * t + n], "z%d%d" % (h, t), "S%d%d" % (h, par)
         s0 = 4096 * par
-        mm([(B["bM"][:, 136:144], sel(T.big, q), B["z"][:, 128 * t + q:128 * t + 128:16], q == 0, q == 15, 8) for q in range(16)], ["big", kz], [k("sz")], k("bM"))
-        cp(B["si"][:, 32:40], B["bM"][:, 136:144], [k("sz")], [k("s32")], 8, [k("bM")])
-        ts(B["si"][:, 40:48], B["si"][:, 32:40], 15, None, ALU.bitwise_and, None, [k("s32")], [k("s40")], 8)
-        tt(B["ci"][:, 0:8], B["si"][:, 40:48], T.bc[:, 8 * h:8 * h + 8], AD, [k("s40"), "bc%d" % h], [k("ci0")], 8)
-        ts(B["ls"][:, 0:8], B["ci"][:, 0:8], -2048.0 * h, None, AD, None, [k("ci0")], [k("ln")], 8)
-        op("V", lambda: V.tensor_copy(X[:, 2048 * h:2048 * h + 2048].indirect(B["ls"][:, 0:8]), z), [k("ln"), kz], ["X%d" % h], 55 + 128 * 4)
-        mm([(B["bD"][:, 0:128], T.c128[:], T.mc[:], True, False, 128)], ["c128", "mc"], [k("D")], k("bD"))
-        row = lambda m: B["pool"][:, s0 + m:s0 + 2048:16]
-        mnm = lambda m: B["mn"][:, 128 * m:128 * m + 128]
-        Dm = lambda m: B["bD"][:, m:128:16]
+        mm([(B["bM"][:, 400:400 + nr], sel(T.big, q), B["z"][:, 128 * t + q:128 * t + n:16], q == 0, q == 15, 8) for q in range(16)], ["big", kz], [k("sz")], k("bM"))
+        cp(si[:, 32:32 + nr], B["bM"][:, 400:400 + nr], [k("sz")], [k("s32")], nr, [k("bM")])
+        ts(si[:, 40:40 + nr], si[:, 32:32 + nr], 15, None, ALU.bitwise_and, None, [k("s32")], [k("s40")], nr)
+        tt(B["ci"][:, 0:nr], si[:, 40:40 + nr], T.bc[:, 8 * h:8 * h + nr], AD, [k("s40"), "bc%d" % h], [k("ci0")], nr)
+        ts(lu[:, 112:112 + nr], B["ci"][:, 0:nr], -16.0 * i0, None, AD, None, [k("ci0")], [k("ln")], nr)
+        op("V", lambda: V.tensor_copy(X[:, 16 * i0:16 * (i0 + n)].indirect(lu[:, 112:112 + nr]), z), [k("ln"), kz], ["X%d" % h], 55 + n * 4)
+        mm([(bD[0:n, 0:128], T.c128[:, 0:n], T.mc[:], True, False, 128)], ["c128", "mc"], [k("D")], k("bD"))
+        w = 512 // n
         if GV:
-            mm([(B["bM"][:, 256:384], T.idp[:], z, True, True, 128)], ["idp", kz], [k("zp")], k("bM"))
-            mm([(Dm(m), x, T.bo8[:, 0:8], False, False, 8) for m in range(GV) for x in (row(m), z)], [kS, kz, "bo0"], [k("D")], k("bD"))
+            zp, row = B["bM"][:, 0:n], lambda m: B["pool"][:, s0 + m:s0 + 16 * n:16]
+            mm([(zp, T.idp[:], z, True, True, n)], ["idp", kz], [k("zp")], k("bM"))
+            mm([(bD[0:n, m:128:16], row(m), T.bo8[:, 0:8], False, False, 8) for m in range(GV)], [kS, "bo0"], [k("D")], k("bD"))
+            mm([(bD[0:n, m:128:16], z, T.bo8[:, 0:8], False, False, 8) for m in range(GV)], [kz, "bo0"], [k("D")], k("bD"))
             for m in range(GV):
-                tt(mnm(m), row(m), B["bM"][:, 256:384], ALU.min, [kS, k("zp")], [k("mn%d" % m)], 128, [k("bM")])
-        for b, m0 in enumerate(range(GV, 16, 4)):
-            bk, ms_ = "bS" if b % 2 == 0 else "bG", range(m0, min(m0 + 4, 16))
+                tt(B["mn"][:, n * m:n * m + n], row(m), zp, ALU.min, [kS, k("zp")], [k("mn%d" % m)], n, [k("bM")])
+        for b, m0 in enumerate(range(GV, 16, w)):
+            bk, ms_ = "bG" if b % 2 else "bS", range(m0, min(m0 + w, 16))
             lst = []
             for m in ms_:
-                o = B[bk][:, 128 * (m - m0):128 * (m - m0) + 128]
-                lst += [(o, T.idp[:], row(m), True, False, 128), (o, T.idn[:], z, False, True, 128)]
+                o = B[bk][:, n * (m - m0):n * (m - m0 + 1)]
+                lst += [(o, T.idp[:], B["pool"][:, s0 + m:s0 + 16 * n:16], True, False, n), (o, T.idn[:], z, False, True, n)]
             kb = k("sP") if bk == "bS" else k("G")
             mm(lst, ["idp", "idn", kS, kz], [kb], k(bk))
-            act(B["mn"][:, 128 * m0:128 * (ms_[-1] + 1)], B[bk][:, 0:128 * len(ms_)], AF.Abs, [kb], [k("mn%d" % m) for m in ms_], 128 * len(ms_), [k(bk)])
-        blocks = [range(m0, min(m0 + 4, 16)) for m0 in range(GV, 16, 4)]
-        for b, m0 in enumerate(range(0, GV, 4)):
-            blocks.insert(min(2 * b, len(blocks)), range(m0, min(m0 + 4, GV)))
-        for ms_ in blocks:
-            mm([(Dm(m), mnm(m), T.bo8[:, 8:16] if m < GV else T.bo8[:, 0:8], False, ms_ is blocks[-1] and m == ms_[-1], 8) for m in ms_],
+            act(B["mn"][:, n * m0:n * (ms_[-1] + 1)], B[bk][:, 0:n * len(ms_)], AF.Abs, [kb], [k("mn%d" % m) for m in ms_], n * len(ms_), [k(bk)])
+        for m0 in range(0, 16, w):
+            ms_ = range(m0, min(m0 + w, 16))
+            mm([(bD[0:n, m:128:16], B["mn"][:, n * m:n * m + n], T.bo8[:, 8:16] if m < GV else T.bo8[:, 0:8], False, m == 15, 8) for m in ms_],
                [k("mn%d" % m) for m in ms_] + ["bo0", "bo1"], [k("D")], k("bD"))
-        argmin(h, B, k)
-        cv = B["bD"]
-        mm([(cv[:, 128:256], T.idp[:], T["cg%d" % par][:], True, False, 128), (cv[:, 128:256], B["ex"][:], T["rg%d" % par][:], False, True, 128)],
+        argmin(B, k)
+        mm([(bD[:, 128:256], T.idp[:], T["cg%d" % par][:], True, False, 128), (bD[:, 128:256], B["ex"][0:n, :], T["rg%d" % par][0:n, :], False, True, 128)],
            ["idp", k("ex")] + RG[par] + CG[par], [k("cv")], k("bD"))
-        cp(B["lg"][:], cv[:, 128:176], [k("cv")], [k("lg")], 48, [k("bD")])
+        cp(lu[:, 0:48], bD[:, 128:176], [k("cv")], [k("lg")], 48, [k("bD")])
         o1, o2 = (ALU.max, ALU.min) if par == 0 else (ALU.min, ALU.max)
-        tt(B["sm"][:, 16:24], cv[:, 176:184], T.bc[:, 16 + 8 * par:24 + 8 * par], o1, [k("cv"), "bc%d" % (2 + par)], [k("m16")], 8, [k("bD")])
-        tt(B["sm"][:, 24:32], cv[:, 184:192], B["sm"][:, 16:24], o2, [k("cv"), k("m16")], [k("m24")], 8, [k("bD")])
-        ts(B["lw"][:], cv[:, 192:256], 15.0, None, ALU.is_le, None, [k("cv")], [k("lw")], 64, [k("bD")])
-        ag(B["xe"][:], B["pool"][:, s0:s0 + 2048], B["lg"][:, 0:8], [kS, k("lg")], [k("xe")], 128)
+        tt(sm[:, 16:24], bD[:, 176:184], T.bc[:, 8 * (NP + par):8 * (NP + par) + 8], o1, [k("cv"), "bc%d" % (NP + par)], [k("m16")], 8, [k("bD")])
+        tt(sm[:, 24:32], bD[:, 184:192], sm[:, 16:24], o2, [k("cv"), k("m16")], [k("m24")], 8, [k("bD")])
+        ts(B["lw"][:], bD[:, 192:256], 15.0, None, ALU.is_le, None, [k("cv")], [k("lw")], 64, [k("bD")])
+        ag(B["xe"][:, 0:n], B["pool"][:, s0:s0 + 16 * n], lu[:, 0:nr], [kS, k("lg")], [k("xe")], n)
         middle(h, B, k, z, kz, 0)
         for j in range(1, 5):
-            tg(B["Q"][:, 128 * j - 128:128 * j], T.et[:, 0:32], B["lg"][:, 8 + 8 * j:16 + 8 * j], B["M"][:], MU, ["et", k("lg"), "M%d" % h], [k("Q%d" % j)], 128)
-        for q in range(16):
-            mm([(B["bG"][:, 256:288], sel(T.bigf, q), B["Q"][:, q::16], q == 0, q == 15, 32)],
-               ["bigf"] + [k("Q%d" % j) for j in range(1, 5)], [k("G")], k("bG"), True)
+            tg(B["Qh"][:, n * j - n:n * j], T.et[:, 0:32], lu[:, 8 + 8 * j:8 + 8 * j + nr], M[:, 128:128 + n], MU, ["et", k("lg"), k("M2")], [k("Q%d" % j)], n)
+        for q0 in range(0, 16, 4):
+            mm([(B["bG"][:, 256:256 + 4 * nr], sel(T.bigh, q), B["Qh"][:, q:4 * n:16], q == 0, q == 15, 32) for q in range(q0, q0 + 4)],
+               ["bigh"] + [k("Q%d" % j) for j in range(1, 5)], [k("G")], k("bG"))
         for j in range(1, 5):
-            cp(B["cu"][:, 128 * j - 128:128 * j - 120], B["bG"][:, 248 + 8 * j:256 + 8 * j], [k("G")], [k("cz%d" % j)], 8, [k("bG")])
-            cp(B["ci"][:, 128 * j:128 * j + 8], B["bG"][:, 248 + 8 * j:256 + 8 * j], [k("G")], [k("ci%d" % j)], 8, [k("bG")])
-        cp(B["ls"][:, 8:16], B["sm"][:, 24:32], [k("m24")], [k("l15")], 8)
-        tt(B["lw"][:], B["lw"][:], T.wj[:], MU, [k("lw"), "wj"], [k("lw")], 64)
-        ag(B["em"][:], (T.eb if PLS else T.et)[:, 0:32], B["lg"][:, 8:48], ["et", "eb", k("lg")], [k("em")], 640)
-        tg(B["KL"][:, 0:128], tb[:, 16:32], B["lg"][:, 8:16], B["M"][:], MU, ["keep", k("lg"), "M%d" % h], [k("K")], 128)
-        tg(B["KL"][:, 128:256], tb[:, 32:48], B["lg"][:, 8:16], B["M"][:], MU, ["le", k("lg"), "M%d" % h], [k("L")], 128)
-        tg(B["rf"][:], tb[:, 96 + 16 * par:112 + 16 * par], B["lg"][:, 8:16], T.i16[:], AD, ["al%d" % par, k("lg"), "i16"], [k("rf")], 128)
-        cp(B["ru"][:], B["rf"][:], [k("rf")], [k("ru")], 128)
+            c0 = B["bG"][:, 256 + nr * (j - 1):256 + nr * j]
+            ts(B["cu"][:, 128 * j - 128:128 * j - 128 + nr], c0, 2048.0, None, AD, None, [k("G")], [k("cz%d" % j)], nr, [k("bG")])
+            ts(B["ci"][:, 128 * j:128 * j + nr], c0, 2048.0, None, AD, None, [k("G")], [k("ci%d" % j)], nr, [k("bG")])
+        cp(lu[:, 120:128], sm[:, 24:32], [k("m24")], [k("l15")], 8)
+        tt(B["lw"][:], B["lw"][:], T.wj[:, 64 * v:64 * v + 64], MU, [k("lw"), "wj"], [k("lw")], 64)
+        hl = lu[:, 8:8 + nr]
+        ag(B["em"][:, 0:n], T.eb[:, 0:16], hl, ["eb", k("lg")], [k("em")], n)
+        act(B["em"][:, 128:128 + n], B["em"][:, 0:n], AF.Square, [k("em")], [k("en")], n)
+        tg(M[:, 256:256 + n], tb[:, 16:32], hl, M[:, 0:n], MU, ["keep", k("lg"), k("M")], [k("K")], n)
+        tg(M[:, 384:384 + n], tb[:, 32:48], hl, M[:, 0:n], MU, ["le", k("lg"), k("M")], [k("L")], n)
+        tg(M[:, 640:640 + n], tb[:, 96 + 16 * par:112 + 16 * par], hl, T.i16[:, 0:n], AD, ["al%d" % par, k("lg"), "i16"], [k("rf")], n)
+        cp(B["cu"][:, 512:512 + n], M[:, 640:640 + n], [k("rf")], [k("ru")], n)
 
     def corr(t, h, j):
         cur_h[0] = h
-        B = H[h]
-        k = lambda s: s + "_%d" % h
-        c0 = 2064 - j
-        s, ks = B["pool"][:, c0:4096:16], "new%d%d" % (h, j - 1)
-        si, sm, a0 = B["si"], B["sm"], 2048 * (j - 1)
-        mm([(B["bM"][:, 128:136], sel(T.wbig, q), B["pool"][:, c0 + 16 * q:4096:256], q == 0, q == 15, 8) for q in range(16)], ["wbig", ks], [k("U")], k("bM"))
-        mm([(B["bS"][:, 128 * c:128 * c + 128], T.idp[:], s, True, True, 128) for c in range(4)], ["idp", ks], [k("sP")], k("bS"))
-        mm([(B["bD"][:, 0:128], T.c128[:], T.mc[:], True, False, 128)], ["c128", "mc"], [k("D")], k("bD"))
-        cp(si[:, 8:16], B["bM"][:, 128:136], [k("U")], [k("s8")], 8, [k("bM")])
-        ts(si[:, 0:8], si[:, 8:16], 4095, None, ALU.bitwise_and, None, [k("s8")], [k("u")], 8)
-        tt(sm[:, 0:8], si[:, 0:8], si[:, 0:8], MU, [k("u")], [k("sq")], 8)
-        b1 = T.kj[:, j - 1:j] if t == 0 else T.b1[:, 4 * t + j - 1:4 * t + j]
-        ts(si[:, 16:24], sm[:, 0:8], b1, 2.0 ** -5, AD, MU, [k("sq"), "b1%d" % t], [k("base")], 8)
-        for x, (e0, e1) in enumerate(((8 * IX, 128), (0, 8 * IX)) if IX else ((0, 128),)):
-            rp, f0 = T.rl[:, 8:8 + (e1 - e0) // 16], max(e0, 8)
-            tg(B["p1"][:, e0:e1], si[:, 0:8], rp, T.kr[:, e0:e1], MU, [k("u"), "rl", "kr"], [k("p1%d" % x)], e1 - e0)
-            tg(B["p2"][:, e0:e1], si[:, 16:24], rp, B["p1"][:, e0:e1], AD, [k("base"), "rl", k("p1%d" % x)], [k("p2%d" % x)], e1 - e0)
-            ts(B["ci"][:, 128 * j + f0:128 * j + e1], B["p2"][:, f0:e1], 4095, None, ALU.bitwise_and, None, [k("p2%d" % x)], [k("cj%d%d" % (j, x))], e1 - f0)
-            cp(B["cu"][:, 128 * j - 128 + f0:128 * j - 128 + e1], B["ci"][:, 128 * j + f0:128 * j + e1], [k("cj%d%d" % (j, x))], [k("cu%d%d" % (j, x))], e1 - f0)
-        if j == 1:
-            place(h, B, k, 0, B["ci"][:, 0:8], repg, "rl")
+        B, k = H[h], keys(h)
+        n, v, si, sm, lu, M, bD, bS = B["n"], B["v"], B["si"], B["sm"], B["lu"], B["M"], B["bD"], B["bS"]
+        nr, c0, a0 = n // 16, 2064 - j, 16 * n * (j - 1)
+        s, ks, U, d2 = new(B, j - 1), k("new%d" % (j - 1)), B["bM"][:, 384:384 + nr], B["em"][:, 256:256 + n]
+        if MV and j > 1:
+            mm([(U, sel(T.wbh, q), B["em"][:, 256 + q:256 + n:16], q == 0, q == 15, 8) for q in range(16)], ["wbh", k("d2")], [k("U")], k("bM"))
+            mm([(bS[:, n * c:n * c + n], T.idh[:], d2, True, True, n) for c in range(NC)], ["idh", k("d2")], [k("sP")], k("bS"))
         else:
-            place(h, B, k, j - 1, B["ci"][:, 128 * j - 128:128 * j], B["lc"][:, 16 * j - 24:16 * j - 16], k("lc%d" % (j - 1)))
+            mm([(U, sel(T.wbig, q), B["pool"][:, c0 + 16 * q:2048 + 16 * n:256], q == 0, q == 15, 8) for q in range(16)], ["wbig", ks], [k("U")], k("bM"))
+            mm([(bS[:, n * c:n * c + n], T.idp[:], s, True, True, n) for c in range(NC)], ["idp", ks], [k("sP")], k("bS"))
+        cp(si[:, 8:8 + nr], U, [k("U")], [k("s8")], nr, [k("bM")])
+        if MV:
+            sc = B["bM"][:, 0:n]
+            if j > 1:
+                mm([(sc, T.idh[:], d2, True, True, n)], ["idh", k("d2")], [k("zp")], k("bM"))
+                act(s, sc, AF.Copy, [k("zp")], [ks], n, [k("bM")])
+            if j < 4:
+                act(M[:, 768:768 + n], sc if j > 1 else s, AF.Identity, [k("zp") if j > 1 else ks, "c14"], [k("sh")], n, [k("bM")] if j > 1 else (), col[:, 14:15])
+        mm([(bD[0:n, 0:128], T.c128[:, 0:n], (T.mc2 if EX else T.mc)[:], True, False, 128)], ["c128", "mc", "mc2"], [k("D")], k("bD"))
+        ts(si[:, 0:nr], si[:, 8:8 + nr], 4095, None, ALU.bitwise_and, None, [k("s8")], [k("u")], nr)
+        tt(sm[:, 0:nr], si[:, 0:nr], si[:, 0:nr], MU, [k("u")], [k("sq")], nr)
+        b1 = T.kj[:, j - 1:j] if t == 0 else T.b1[:, 4 * t + j - 1:4 * t + j]
+        ts(si[:, 16:16 + nr], sm[:, 0:nr], b1, 2.0 ** -5, AD, MU, [k("sq"), "b1%d" % t], [k("base")], nr)
+        for x, (e0, e1) in zip(("", "x"), ((nr * IX, n), (0, nr * IX)) if IX else ((0, n),)):
+            rp, f0 = T.rl[:, 8 + 8 * v:8 + 8 * v + (e1 - e0) // 16], max(e0, nr)
+            tg(B["p1"][:, e0:e1], si[:, 0:nr], rp, T.kr[:, 128 * v + e0:128 * v + e1], MU, [k("u"), "rp%d" % v, "kr%d" % v], [k("p1" + x)], e1 - e0)
+            tg(B["p2"][:, e0:e1], si[:, 16:16 + nr], rp, B["p1"][:, e0:e1], AD, [k("base"), "rp%d" % v, k("p1" + x)], [k("p2" + x)], e1 - e0)
+            ts(B["ci"][:, 128 * j + f0:128 * j + e1], B["p2"][:, f0:e1], 4095, None, ALU.bitwise_and, None, [k("p2" + x)], [k("cj%d" % j + x)], e1 - f0)
+            cp(B["cu"][:, 128 * j - 128 + f0:128 * j - 128 + e1], B["ci"][:, 128 * j + f0:128 * j + e1], [k("cj%d" % j + x)], [k("cu%d" % j + x)], e1 - f0)
+        if j == 1:
+            place(B, k, 0, B["ci"][:, 0:nr], T.rl[:, 0:nr], "rl")
+        else:
+            place(B, k, j - 1, B["ci"][:, 128 * j - 128:128 * j - 128 + n], lu[:, 24 + 16 * j:24 + 16 * j + nr], k("lc%d" % (j - 1)))
         ka = lambda m: k("a%d%d" % (j, sum(1 for c in CH[1:] if c <= m)))
-        am = lambda m: B["aw"][:, a0 + 128 * m:a0 + 128 * m + 128]
-        mnm = lambda m: B["mn"][:, 128 * m:128 * m + 128]
-        Dm = lambda m: B["bD"][:, m:128:16]
+        am = lambda m: B["aw"][:, a0 + n * m:a0 + n * m + n]
+        mnm = lambda m: B["mn"][:, n * m:n * m + n]
+        Dm = lambda m: bD[0:n, m:128:16]
         mv = 16 - NS
         cuts = sorted(set(x for x in VB + CH + (mv,) if x <= mv))
         for c0_, c1 in list(zip(CH, CH[1:]))[::-1]:
-            kl = [k("cu%d0" % j)] + ([k("cu%d1" % j)] if c0_ < IX else []) + ([k("cz%d" % j)] if c0_ == 0 else [])
-            ag(B["aw"][:, a0 + 128 * c0_:a0 + 128 * c1], X[:, 0:4096], B["cu"][:, 128 * j - 128 + 8 * c0_:128 * j - 128 + 8 * c1],
-               ["X0", "X1"] + kl, [ka(c0_)], 128 * (c1 - c0_))
+            ag(B["aw"][:, a0 + n * c0_:a0 + n * c1], X[:, 0:4096], B["cu"][:, 128 * j - 128 + nr * c0_:128 * j - 128 + nr * c1],
+               XK + [k("cu%d" % j)] + ([k("cu%dx" % j)] if c0_ < IX else []) + ([k("cz%d" % j)] if c0_ == 0 else []), [ka(c0_)], n * (c1 - c0_))
             if c1 == 16 and NS:
                 lst = []
                 for m in range(mv, 16):
-                    o = B["bG"][:, 128 * (m - mv):128 * (m - mv) + 128]
-                    lst += [(o, T.idp[:], am(m), True, False, 128), (o, T.idn[:], s, False, True, 128)]
+                    o = B["bG"][:, n * (m - mv):n * (m - mv + 1)]
+                    lst += [(o, T.idp[:], am(m), True, False, n), (o, T.idn[:], s, False, True, n)]
                 mm(lst, ["idp", "idn", ka(15), ks], [k("G")], k("bG"))
-                act(B["mn"][:, 128 * mv:2048], B["bG"][:, 0:128 * NS], AF.Relu, [k("G")], [k("mn%d" % m) for m in range(mv, 16)], 128 * NS, [k("bG")])
+                act(B["mn"][:, n * mv:16 * n], B["bG"][:, 0:n * NS], AF.Relu, [k("G")], [k("mn%d" % m) for m in range(mv, 16)], n * NS, [k("bG")])
             mm([(Dm(m), am(m), T.bo8[:, 24:32] if m >= mv else T.bo8[:, 0:8], False, False, 8) for m in range(c0_, c1)], [ka(c0_), "bo0", "bo3"], [k("D")], k("bD"))
             if c0_ == 0 and NS:
                 mm([(Dm(m), mnm(m), T.bo8[:, 16:24], False, False, 8) for m in range(mv, 16)], [k("mn%d" % m) for m in range(mv, 16)] + ["bo2"], [k("D")], k("bD"))
             for m0, m1 in list(zip(cuts, cuts[1:]))[::-1]:
                 if c0_ <= m0 < c1:
                     kk = [k("mn%d" % m) for m in range(m0, m1)]
-                    tt(B["mn"][:, 128 * m0:128 * m1], B["aw"][:, a0 + 128 * m0:a0 + 128 * m1], B["bS"][:, 0:128 * (m1 - m0)], ALU.min,
-                       [ka(m0), k("sP")], kk, 128 * (m1 - m0), [k("bS")])
+                    tt(B["mn"][:, n * m0:n * m1], B["aw"][:, a0 + n * m0:a0 + n * m1], bS[:, 0:n * (m1 - m0)], ALU.min, [ka(m0), k("sP")], kk, n * (m1 - m0), [k("bS")])
                     mm([(Dm(m), mnm(m), T.bo8[:, 8:16], False, m0 == 0 and m == m1 - 1, 8) for m in range(m0, m1)], kk + ["bo1"], [k("D")], k("bD"))
-        argmin(h, B, k)
-        cv = B["bD"][:, 128:144]
-        mm([(cv, T.idp[:], T.cc[:], True, False, 16), (cv, B["ex"][:], T.rc[:], False, True, 16)], ["idp", "cc0", "cc1", "rc0", "rc1", k("ex")], [k("cv")], k("bD"))
-        cp(B["lc"][:, 16 * j - 16:16 * j], cv, [k("cv")], [k("lc%d" % j)], 16, [k("bD")])
-        (vg if XV else ag)(B["xe"][:], B["aw"][:, a0:a0 + 2048], B["lc"][:, 16 * j - 16:16 * j - 8], [ka(m) for m in CH[:-1]] + [k("lc%d" % j)], [k("xe")], 128)
+        if j == 4:
+            Y = B["bG"][:, 128:128 + n]
+            mm([(Y, T.shf[:], M[:, 384:384 + n], True, False, n)], ["shf", k("L")], [k("G")], k("bG"), True)
+            mm([(Y, T.idf[:], M[:, 256:256 + n], False, False, n)], ["idf", k("K")], [k("G")], k("bG"), True)
+            for x in range(4):
+                mm([(Y, T.idf[:], B["pl"][:, 128 * x:128 * x + n], False, x == 3, n)], ["idf", k("pl%d" % x)], [k("G")], k("bG"), True)
+            act(M[:, 512:512 + n], Y, AF.Copy, [k("G")], [k("Yp")], n, [k("bG")])
+        cv = bD[:, 128:144]
+        if EX:
+            scan(B, k)
+            mm([(cv, T.idp[:], T.cc[:], True, False, 16), (cv, T.c128[:], T.ce[:, 16 * v:16 * v + 16], False, False, 16)],
+               ["idp", "cc0", "cc1", "c128", "ce%d0" % v, "ce%d1" % v], [k("cv")], k("bD"))
+            ts(sm[0:n, 32:40], B["run"][0:n, 15::16], 16 * MAGIC, 16 * MAGIC, AD, ALU.subtract, [k("run")], [k("m32")], 8)
+            tt(B["fb"][0:n, 15:143:16], B["run"][0:n, 15::16], sm[0:n, 32:40], ALU.subtract, [k("run"), k("m32")], [k("fb")], 8)
+            mm([(cv, sel(B["fb"], q, n), T.idc[0:n, 256 * v + q:256 * v + 256:16], False, q == 15, 16) for q in range(16)],
+               ["idc%d0" % v, "idc%d1" % v, k("fb")], [k("cv")], k("bD"))
+        else:
+            argmin(B, k)
+            mm([(cv, T.idp[:], T.cc[:], True, False, 16), (cv, B["ex"][0:n, :], T.rc[0:n, 16 * v:16 * v + 16], False, True, 16)],
+               ["idp", "cc0", "cc1", "rc%d0" % v, "rc%d1" % v, k("ex")], [k("cv")], k("bD"))
+        cp(lu[:, 32 + 16 * j:48 + 16 * j], cv, [k("cv")], [k("lc%d" % j)], 16, [k("bD")])
+        win, lst, kk = B["aw"][:, a0:a0 + 16 * n], lu[:, 32 + 16 * j:32 + 16 * j + nr], [ka(m) for m in CH[:-1]] + [k("lc%d" % j)]
+        if MV and j < 4:
+            tg(M[:, 896:896 + n], win, lst, M[:, 768:768 + n], AD, kk + [k("sh")], [k("tp")], n)
+            ts(d2, M[:, 896:896 + n], 2 * MAGIC, 2 * MAGIC, AD, ALU.subtract, [k("tp")], [k("d2")], n)
+            return
+        ag(B["xe"][:, 0:n], win, lst, kk, [k("xe")], n)
         middle(h, B, k, s, ks, j)
 
     def tail(t, h):
         cur_h[0] = h
-        B, par = H[h], t % 2
-        k = lambda s: s + "_%d" % h
-        nz, news = B["nz"], ["new%d%d" % (h, j) for j in range(5)]
+        B, par, k = H[h], t % 2, keys(h)
+        n, i0, v, lu, M, sm = B["n"], B["i0"], B["v"], B["lu"], B["M"], B["sm"]
+        nr = n // 16
+        news = [k("new%d" % j) for j in range(5)] + [k("fill%d" % h)[:-2] + "_%d" % c for c in range(13)]
         kS, kN, w0 = "S%d%d" % (h, par), "S%d%d" % (h, 1 - par), 2048 * par
-        win = B["pool"][:, w0:w0 + 4096]
-        ts(nz[:, 0:64], B["lc"][:], 128.0, None, ALU.is_ge, None, [k("lc%d" % j) for j in range(1, 5)], [k("nz")], 64)
-        tt(nz[:, 0:64], nz[:, 0:64], B["lw"][:], MU, [k("nz"), k("lw")], [k("nz")], 64)
-        tt(nz[:, 64:96], nz[:, 0:32], nz[:, 32:64], ALU.max, [k("nz")], [k("n2")], 32)
-        tt(nz[:, 96:104], nz[:, 64:72], nz[:, 80:88], ALU.max, [k("n2")], [k("n3")], 8)
-        tt(nz[:, 104:112], T.bc[:, 32:40], nz[:, 96:104], ALU.subtract, ["bc4", k("n3")], [k("n4")], 8)
-        cp(B["ls"][:, 16:24], nz[:, 104:112], [k("n4")], [k("lsel")], 8)
-        tg(B["dz"][:], win, B["ls"][:, 8:16], B["z"][:, 128 * t:128 * t + 128], ALU.subtract, news + [kS, k("l15"), "z%d%d" % (h, t)], [k("dz")], 128)
-        act(B["aw"][:, 8192:8320], B["dz"][:], AF.Abs, [k("dz")], [k("alt")], 128)
-        zs = B["zs"][:, 128 * t:128 * t + 128]
-        ag(zs, B["aw"][:, 0:8320], B["ls"][:, 16:24], [k("a%d%d" % (j, c)) for j in range(1, 5) for c in range(len(CH) - 1)] + [k("alt"), k("lsel")], [k("zs%d" % t)], 128)
+        win = B["pool"][:, w0:w0 + 2048 + 16 * n]
+        ts(sm[:, 64:128], lu[:, 48:112], float(n), None, ALU.is_ge, None, [k("lc%d" % j) for j in range(1, 5)], [k("nz")], 64)
+        tt(sm[:, 64:128], sm[:, 64:128], B["lw"][:], MU, [k("nz"), k("lw")], [k("nz")], 64)
+        tt(sm[:, 128:160], sm[:, 64:96], sm[:, 96:128], ALU.max, [k("nz")], [k("n2")], 32)
+        tt(sm[:, 160:168], sm[:, 128:136], sm[:, 144:152], ALU.max, [k("n2")], [k("n3")], 8)
+        b4 = NP + 2 + v
+        tt(sm[:, 168:168 + nr], T.bc[:, 8 * b4:8 * b4 + nr], sm[:, 160:160 + nr], ALU.subtract, ["bc%d" % b4, k("n3")], [k("n4")], nr)
+        cp(lu[:, 128:128 + nr], sm[:, 168:168 + nr], [k("n4")], [k("lsel")], nr)
+        tg(B["aw"][:, 64 * n:65 * n], win, lu[:, 120:120 + nr], B["z"][:, 128 * t:128 * t + n], ALU.subtract, news + [kS, k("l15"), "z%d%d" % (h, t)], [k("alt")], n)
+        zs = B["zs"][:, 128 * t:128 * t + n]
+        op("A", lambda: A.activation(zs, B["aw"][:, 0:65 * n].indirect(lu[:, 128:128 + nr]), AF.Abs),
+           [k("a%d%d" % (j, c)) for j in range(1, 5) for c in range(len(CH) - 1)] + [k("alt"), k("lsel")], [k("zs%d" % t)], 70 + n * GC)
         dst = T.cores[(rank + 1 + t % 3) % len(T.cores)]
         rid, pid, _ = topo.addr(dst)
-        sem = "in%d" % (2 * t + h)
-        land = B["z"][:, 128 * t + 128:128 * t + 256]
+        sem = "in%d" % (NP * t + h)
+        land = B["z"][:, 128 * t + 128:128 * t + 128 + n]
         snd = op("G", lambda: g.remote_dma(land, zs, T.sem[sem], T.sem.sent, pid, rid, topo.mask(core, dst)), [k("zs%d" % t)], [], 500, sem="remote")
         src = T.cores[(rank - 1 - t % 3) % len(T.cores)]
         op("N", len(topo.engines(src, core)), [], ["z%d%d" % (h, t + 1)], 0, sem=sem, after=[(snd, NET)])
         if t < 3:
-            ts(T.cn[:, 8 * h:8 * h + 8], nz[:, 96:104], 0.0, None, ALU.is_gt, None, [k("n3")], ["cn%d" % h], 8)
-        n0 = 4096 * (1 - par)
+            ts(T.cn[:, 8 * h:8 * h + nr], sm[:, 160:160 + nr], 0.0, None, ALU.is_gt, None, [k("n3")], ["cn%d" % h], nr)
         nb = 4 if t == 3 else RB
-        w = 2048 // nb
+        n0, w = 4096 * (1 - par), 16 * n // nb
         for c in range(nb):
-            o, lst = B["pool"][:, n0 + w * c:n0 + w * c + w], B["ru"][:, w * c // 16:w * (c + 1) // 16]
+            o, lst = B["pool"][:, n0 + w * c:n0 + w * c + w], B["cu"][:, 512 + w * c // 16:512 + w * (c + 1) // 16]
             (vg if c >= nb - (2 if t == 3 else RV[h]) else ag)(o, win, lst, news + [kS, k("ru"), kN], [k("rb%d" % c)], w)
             if t == 3:
-                dma("Y", T.so[:, 2048 * h + w * c:2048 * h + w * c + w], o, [k("rb%d" % c)], [], 2200 + w)
+                dma(T.so[:, 16 * i0 + w * c:16 * i0 + w * c + w], o, [k("rb%d" % c)], [], 2200 + w)
         last_w[kN] = op("N", None, [k("rb%d" % c) for c in range(nb)], [], 0)
-        place(h, B, k, 4, B["ci"][:, 512:640], B["lc"][:, 56:64], k("lc4"))
-        Y = B["bG"][:, 128:256]
-        mm([(Y, T.shf[:], B["KL"][:, 128:256], True, False, 128)], ["shf", k("L")], [k("G")], k("bG"), True)
-        mm([(Y, T.idf[:], B["KL"][:, 0:128], False, False, 128)], ["idf", k("K")], [k("G")], k("bG"), True)
-        for j in range(5):
-            mm([(Y, T.idf[:], B["pl"][:, 128 * j:128 * j + 128], False, j == 4, 128)], ["idf", k("pl%d" % j)], [k("G")], k("bG"), True)
-        act(B["M"][:], Y, AF.Copy, [k("G")], ["M%d" % h], 128, [k("bG")])
-        if t == 3:
-            dma("Y", T.mo[:, 128 * h:128 * h + 128], B["M"][:], ["M%d" % h], [], 2500)
-            dma("Y", T.zo[:, 128 * h:128 * h + 128], B["z"][:, 512:640], ["z%d4" % h], [], 2500)
+        place(B, k, 4, B["ci"][:, 512:512 + n], lu[:, 104:104 + nr], k("lc4"))
+        tt(M[:, 0:n], M[:, 512:512 + n], B["pl"][:, 512:512 + n], AD, [k("Yp"), k("pl4")], [k("M")], n)
+        if t < 3:
+            act(M[:, 128:128 + n], M[:, 0:n], AF.Identity, [k("M"), "c8"], [k("M2")], n, (), col[:, 8:9])
+        else:
+            dma(T.mo[:, i0:i0 + n], M[:, 0:n], [k("M")], [], 2500)
+            dma(T.zo[:, i0:i0 + n], B["z"][:, 512:512 + n], ["z%d4" % h], [], 2500)
 
     for t in range(4):
-        for h in (0, 1):
+        for h in range(NP):
             head(t, h)
         for j in range(1, 5):
-            for h in (0, 1):
+            for h in range(NP):
                 corr(t, h, j)
-        for h in (0, 1):
+        for h in range(NP):
             tail(t, h)
         if t < 3:
-            cn, cni = T.cn, T.cni
-            op("V", lambda: V.tensor_reduce(cn[:, 16:17], cn[:, 0:16], AX.X, AD), ["cn0", "cn1"], ["cs"], vc(16))
-            cp(T.cb[:, 0:1], cn[:, 16:17], ["cs"], ["cb"], 1)
-            mm([(T.bM1[:, 144:145], T.one[:], T.cb[:, 0:1], True, True, 1)], ["one", "cb"], ["ct"], "bM_1")
-            cp(cni[:, 0:1], T.bM1[:, 144:145], ["ct"], ["cni0"], 1, ["bM_1"])
+            cn, cni, bD, kb = T.cn, T.cni, H[-1]["bM"], "bM_%d" % (NP - 1)
+            op("V", lambda: V.tensor_reduce(cn[:, 32:33], cn[:, 0:8 * NP], AX.X, AD), ["cn%d" % h for h in range(NP)], ["cs"], vc(24))
+            cp(T.cb[:, 0:1], cn[:, 32:33], ["cs"], ["cb"], 1)
+            mm([(bD[:, 416:417], T.one[:], T.cb[:, 0:1], True, True, 1)], ["one", "cb"], ["ct"], kb)
+            cp(cni[:, 0:1], bD[:, 416:417], ["ct"], ["cni0"], 1, [kb])
             ts(cni[:, 4:5], cni[:, 0:1], 63, None, ALU.bitwise_and, None, ["cni0"], ["cni4"], 1)
-            ts(cn[:, 20:21], cni[:, 4:5], 32.0, None, MU, None, ["cni4"], ["a32"], 1)
-            ts(T.b1[:, 4 * t + 4:4 * t + 8], T.kj[:, 0:4], cn[:, 20:21], None, AD, None, ["b10", "a32"], ["b1%d" % (t + 1)], 4)
+            ts(cn[:, 36:37], cni[:, 4:5], 32.0, None, MU, None, ["cni4"], ["a32"], 1)
+            ts(T.b1[:, 4 * t + 4:4 * t + 8], T.kj[:, 0:4], cn[:, 36:37], None, AD, None, ["b10", "a32"], ["b1%d" % (t + 1)], 4)
 
 
 def lat(ops, a, b):
@@ -521,7 +604,6 @@ def rank_program(g, core, T, topo):
     Q = {"V": g.vector, "A": g.scalar, "P": g.tensor, "G": g, "Y": g.sync}
     know = {e: {} for e in Q}
     cnt, mark, clock, join = {}, {}, {}, {}
-    sent = 0
     for i in order:
         o = ops[i]
         e = o["e"]
@@ -544,7 +626,6 @@ def rank_program(g, core, T, topo):
                 kn[s] = max(kn.get(s, 0), v)
         ins = o["fn"]()
         if o["sem"] == "remote":
-            sent += 1
             mark[i], clock[i] = ("sent", 0), {}
             continue
         s, inc = (o["sem"], 16) if o["sem"] else ("q" + e, 1)
@@ -555,6 +636,6 @@ def rank_program(g, core, T, topo):
         clock[i][s] = cnt[s]
     cores = T.cores
     r = T.rank_of(core)
-    g.wait_ge(T.sem.sent, sum(2 * len(topo.engines(core, cores[(r + 1 + t % 3) % len(cores)])) for t in range(4)))
+    g.wait_ge(T.sem.sent, sum(len(PARTS) * len(topo.engines(core, cores[(r + 1 + t % 3) % len(cores)])) for t in range(4)))
     for s in sorted(cnt):
         g.wait_ge(T.sem[s], cnt[s])

@@ -1,43 +1,40 @@
 from concourse.mybir import AluOpType as ALU, ActivationFunctionType as AF, AxisListType as AX
 
-PARTS = (128, 128)
+NP, n, nr = 2, 128, 8
 NS = 4
-CH = (0, 4, 8, 12, 16)
+CH = (0, 4, 8, 12, 15, 16)
 VB = (0, 4, 8, 12, 16)
-IX = 12
-GV = 4
-NC = 4
-MV = 1
-EX = 1
-RB, RV = 8, (0, 5)
-BONUS, LOOK, PASSES, NOISE, SEED, SHIFT, SPAN = 2000.0, 60.0, 230, 300.0, 5, 1000.0, 6000.0
+IX = 4
+GV = 2
+SH = 1
+RB, RV, RL = 8, (2, 4), 2
+BONUS, LOOK, PASSES, NOISE, SEED, SHIFT, SPAN = 2000.0, 60.0, 600, 300.0, 5, 1000.0, 6000.0
 HOP, SAME, NET = 110.0, 70.0, 3500.0
-GC, VF, PEC = 1.55 * 0.83 * 1.15, 0.83 * 1.2, 0.45
+MODELS = ((1.15, 1.55), (1.0, 1.2), (1.3, 1.9))
 MAGIC = 12582912.0
+ALT = 64 * n
 BF, F32, I32, U16, F16 = "bfloat16", "float32", "int32", "uint16", "float16"
 
 SCRATCH = {"X": ("sbuf", [128, 4096], BF), "nmi": ("sbuf", [128, 256], I32), "wk": ("sbuf", [128, 16], I32)}
-for _n, _w, _d in [("xf", 144, F32), ("mc", 128, BF), ("xg", 128, F32), ("xm", 256, F32), ("pi", 16, I32), ("col", 16, F32),
-                   ("big", 144, BF), ("bigh", 144, F16), ("wbig", 144, BF), ("wbh", 144, BF), ("mc2", 128, BF), ("ce", 32, BF),
-                   ("idc", 512, BF), ("idp", 128, BF), ("idn", 128, BF), ("idh", 128, BF), ("idf", 128, F32), ("shf", 128, F32),
-                   ("bof", 128, F32), ("bo8", 32, BF), ("dm", 128, BF), ("rst", 128, F32), ("c128", 128, BF), ("cq", 128, BF),
-                   ("one", 128, BF), ("kr", 256, F32), ("rl", 32, U16), ("rli", 16, I32), ("rs", 8, F32), ("ib", 32, F32),
-                   ("rg0", 128, BF), ("rg1", 128, BF), ("cg0", 128, BF), ("cg1", 128, BF), ("rc", 32, BF), ("cc", 16, BF),
-                   ("et", 32, BF), ("eb", 32, BF), ("dq", 640, BF), ("tb", 128, F32), ("i16", 128, F32), ("wj", 128, F32),
-                   ("kj", 8, F32), ("b1", 16, F32), ("cn", 48, F32), ("cni", 16, I32), ("bc", 64, F32), ("cb", 16, BF)]:
+for _n, _w, _d in [("xb", 144, BF), ("db", 128, BF), ("mc", 128, BF), ("mc2", 128, BF), ("xm", 128, F32), ("pi", 32, I32), ("col", 16, F32),
+                   ("big", 144, BF), ("bigh", 144, F16), ("wbh", 144, F16), ("idp", 128, BF), ("idn", 128, BF), ("id16", 128, F16),
+                   ("sh16", 128, F16), ("bof", 128, F32), ("bo8", 32, BF), ("dm", 128, BF), ("rst", 128, BF), ("c128", 128, BF),
+                   ("one", 128, BF), ("kr", 128, F32), ("rl", 16, U16), ("rs", 8, BF), ("ib", 8, F32), ("hc", 512, BF), ("cc", 384, BF),
+                   ("hp", 32, BF), ("hq", 32, BF), ("cp", 32, BF), ("cq", 32, BF), ("on", 640, BF), ("pk", 128, BF), ("pl", 128, BF),
+                   ("lo", 128, BF), ("dd", 32, BF), ("i32", 128, BF), ("zv", 128, BF), ("rsn", 448, BF), ("lc", 40, F32), ("kj", 8, F32), ("b1", 16, F32),
+                   ("cn", 16, BF), ("cni", 16, I32), ("bc", 24, F32)]:
     SCRATCH[_n] = ("sbuf", [128, _w], _d)
-PER = [("pool", 6144, BF), ("aw", 8320, BF), ("mn", 2048, BF), ("z", 640, BF), ("zs", 512, BF), ("xe", 128, BF),
-       ("run", 128, F32), ("si", 96, I32), ("ex", 128, BF), ("lu", 144, U16), ("sm", 192, F32), ("p1", 128, F32), ("p2", 128, I32),
-       ("ci", 640, I32), ("cu", 640, U16), ("M", 1664, F32), ("P", 640, F32), ("em", 512, BF), ("lw", 64, F32), ("fb", 144, BF),
-       ("pl", 640, F32), ("Qh", 512, F16)]
+PER = [("pool", 8192, BF), ("aw", 65 * n, BF), ("mn", 2048, BF), ("z", 640, BF), ("zs", 512, BF), ("run", 128, F32), ("si", 64, I32),
+       ("lu", 112, U16), ("sm", 96, F32), ("p1", 128, F32), ("p2", 128, I32), ("ci", 152, I32), ("cu", 152, U16), ("ru", 128, U16),
+       ("nn", 8, I32), ("P", 640, F32), ("Qh", 512, F16), ("N7", 896, F16), ("oh", 128, BF), ("sq", 128, F16), ("tp", 128, F16),
+       ("sh", 128, F32), ("fb", 144, BF), ("M", 128, F32)]
 for _h in "01":
     for _n, _w, _d in PER:
         SCRATCH[_n + _h] = ("sbuf", [128, _w], _d)
-    for _n in ("bS", "bD", "bM"):
+    for _n in ("bS", "bD", "bM", "bG"):
         SCRATCH[_n + _h] = ("psum", [128, 512], F32)
-for _h in "01":
-    SCRATCH["bG" + _h] = ("psum", [128, 512], F32)
-SEMAPHORES = (["qV", "qA", "qP", "qG", "sent"] + ["d%d" % i for i in range(32)] + ["in%d" % i for i in range(12)])
+SEMAPHORES = (["qV", "qA", "qP", "qG", "sent"] + ["d%d" % i for i in range(32)] + ["in%d" % i for i in range(8)])
+EQ, MU, AD, SU, MX, MN, AND = ALU.is_equal, ALU.mult, ALU.add, ALU.subtract, ALU.max, ALU.min, ALU.bitwise_and
 
 
 def build(g, core, T, topo, ops):
@@ -69,436 +66,369 @@ def build(g, core, T, topo, ops):
             for x in prev + (cur[-1:] if e == "P" else []):
                 deps[x] = 0.0
             bank[b] = (e, cur + [i], prev)
-        for x, lat in after:
-            deps[x] = lat
+        for x, lat_ in after:
+            deps[x] = lat_
         deps.pop(i, None)
-        ops.append({"e": e, "fn": fn, "deps": deps, "cost": cost, "sem": sem, "h": cur_h[0]})
+        ops.append({"e": e, "fn": fn, "deps": deps, "c": cost, "sem": sem, "h": cur_h[0]})
         return i
 
-    def vc(n, k=1.0):
-        return 55 + n * k * VF
-
-    def ts(out, in0, s1, s2, o0, o1, r, w, n, banks=()):
+    def ts(out, in0, s1, s2, o0, o1, r, w, c, banks=()):
         if o1 is None:
-            return op("V", lambda: V.tensor_scalar(out, in0, s1, None, o0), r, w, vc(n), banks)
-        return op("V", lambda: V.tensor_scalar(out, in0, s1, s2, o0, o1), r, w, vc(n), banks)
+            return op("V", lambda: V.tensor_scalar(out, in0, s1, None, o0), r, w, (55, c, 0), banks)
+        return op("V", lambda: V.tensor_scalar(out, in0, s1, s2, o0, o1), r, w, (55, c, 0), banks)
 
-    def tt(out, in0, in1, o, r, w, n, banks=()):
-        return op("V", lambda: V.tensor_tensor(out, in0, in1, o), r, w, vc(n, 1.0 if banks else 2.0), banks)
+    def tt(out, in0, in1, o, r, w, c, banks=()):
+        return op("V", lambda: V.tensor_tensor(out, in0, in1, o), r, w, (55, c if banks else 2 * c, 0), banks)
 
-    def tg(out, win, lst, in1, o, r, w, n):
-        return op("V", lambda: V.tensor_tensor(out, win.indirect(lst), in1, o), r, w, 55 + n * GC)
+    def tg(out, win, lst, in1, o, r, w, c):
+        return op("V", lambda: V.tensor_tensor(out, win.indirect(lst), in1, o), r, w, (55, 0, c))
 
-    def cp(out, in_, r, w, n, banks=()):
-        return op("V", lambda: V.tensor_copy(out, in_), r, w, vc(n), banks)
+    def cp(out, in_, r, w, c, banks=()):
+        return op("V", lambda: V.tensor_copy(out, in_), r, w, (55, c, 0), banks)
 
-    def ms(out, c, w, n):
-        return op("V", lambda: V.memset(out, float(c)), [], w, vc(n, 0.5))
+    def ms(out, x, w, c, banks=()):
+        return op("V", lambda: V.memset(out, float(x)), [], w, (55, c / 2, 0), banks)
 
-    def ag(out, win, lst, r, w, n):
-        return op("A", lambda: A.activation(out, win.indirect(lst), AF.Copy), r, w, 70 + n * GC)
+    def scan(out, d0, d1, o0, o1, r, w, c, banks):
+        return op("V", lambda: V.tensor_tensor_scan(out, d0, d1, 0.0, o0, o1), r, w, (55, c, 0), banks)
 
-    def vg(out, win, lst, r, w, n):
-        return op("V", lambda: V.tensor_copy(out, win.indirect(lst)), r, w, 55 + n * GC)
+    def ag(out, win, lst, r, w, c, f=AF.Copy):
+        return op("A", lambda: A.activation(out, win.indirect(lst), f), r, w, (70, 0, c))
 
-    def act(out, in_, f, r, w, n, banks=(), bias=None):
-        if bias is None:
-            return op("A", lambda: A.activation(out, in_, f), r, w, 70 + n * VF, banks)
-        return op("A", lambda: A.activation(out, in_, f, bias=bias), r, w, 70 + n * VF, banks)
+    def vg(out, win, lst, r, w, c):
+        return op("V", lambda: V.tensor_copy(out, win.indirect(lst)), r, w, (55, 0, c))
 
-    def mm(lst, r, w, bk, fp32=False):
+    def act(out, in_, f, r, w, c, banks=(), bias=0.0, scale=1.0):
+        return op("A", lambda: A.activation(out, in_, f, bias=bias, scale=scale), r, w, (70, c, 0), banks)
+
+    def mm(lst, r, w, bk):
         def fn():
             for o, l, x, a, b, _ in lst:
                 ins = P.matmul(o, l, x, a, b)
             return ins
-        return op("P", fn, r, w, 20 + sum(max(64, m[5]) for m in lst) * PEC * (4 if fp32 else 1), [bk])
+        return op("P", fn, r, w, (20, sum(max(64, m[5]) for m in lst) / 2, 0), [bk])
 
-    def io(out, pat, base, cm, w, n, flag=True):
+    def io(out, pat, base, cm, w, c, flag=True):
         if flag:
-            return op("G", lambda: g.iota(out, pat, base, cm, allow_small_or_imprecise_dtypes=True), [], w, 130 + 2 * n)
-        return op("G", lambda: g.iota(out, pat, base, cm), [], w, 130 + 2 * n)
+            return op("G", lambda: g.iota(out, pat, base, cm, allow_small_or_imprecise_dtypes=True), [], w, (130, 2 * c, 0))
+        return op("G", lambda: g.iota(out, pat, base, cm), [], w, (130, 2 * c, 0))
 
-    def diag(out, s, k):
-        io(out, [[0, 128]], s, 0, [k], 128)
-        op("G", lambda: g.affine_select(out, out, [[-1, 128]], ALU.is_equal, 0.0, 0, 1), [k], [k], 430)
+    def keep(out, pat, base, cm, fill, k, c):
+        return op("G", lambda: g.affine_select(out, out, pat, ALU.is_ge, float(fill), base, cm), [k], [k], (170, 2 * c, 0))
 
     nd = [0]
 
     def dma(out, in_, r, w, cost):
         s = "d%d" % nd[0]
         nd[0] += 1
-        return op("Y", lambda: g.sync.dma_start(out, in_), r, w, cost, sem=s)
+        return op("Y", lambda: g.sync.dma_start(out, in_), r, w, (cost, 0, 0), sem=s)
 
-    NP = len(PARTS)
-    sizes = sorted(set(PARTS))
-    H = []
-    for h in range(NP):
-        B = {n: T[n + str(h)] for n in [x[0] for x in PER] + ["bS", "bD", "bM"]}
-        B.update({"bG": T["bG%d" % (h % 2)], "n": PARTS[h], "i0": sum(PARTS[:h]), "v": sizes.index(PARTS[h])})
-        H.append(B)
+    H = [{x: T[x + str(h)] for x in [y[0] for y in PER] + ["bS", "bD", "bM", "bG"]} for h in range(NP)]
     X, col = T.X, T.col
     XK = ["X%d" % h for h in range(NP)]
 
+    def states(B, par):
+        return B["pool"][:, 4096 * par + 2048:4096 * par + 4096]
+
     for h, B in enumerate(H):
-        n, i0 = B["n"], B["i0"]
-        dma(B["z"][:, 0:n], T.arr[:, i0:i0 + n], [], ["z%d0" % h], 2200)
-        dma(B["pool"][:, 0:16 * n], T.st[:, 16 * i0:16 * (i0 + n)], [], ["S%d0" % h], 3500 + 1300 * h)
+        dma(B["z"][:, 0:n], T.arr[:, n * h:n * h + n], [], ["z%d0" % h], 2200)
+        dma(states(B, 0), T.st[:, 2048 * h:2048 * h + 2048], [], ["S%d0" % h], 3500 + 1300 * h)
         if h == 0:
             dma(T.wk[:, 0:1], T.wt[:], [], ["wk0"], 2200)
             dma(T.wk[:, 8:9], T.kap[:], [], ["wk8"], 2200)
             dma(T.nmi[:], T.nm[:], [], ["nmi"], 4500)
-    for h, B in enumerate(H):
-        n, i0 = B["n"], B["i0"]
-        dma(X[:, 16 * i0:16 * (i0 + n)], T.rec[:, 16 * i0:16 * (i0 + n)], [], ["X%d" % h], 7500 + 1300 * h)
+    for h in range(NP):
+        dma(X[:, 2048 * h:2048 * h + 2048], T.rec[:, 2048 * h:2048 * h + 2048], [], ["X%d" % h], 7500 + 1300 * h)
 
-    io(T.pi[:, 0:1], [[1, 1]], 0, 1, ["pi0"], 1, False)
-    io(T.xf[:], [[1, 144]], 0, 0, ["xf"], 144)
+    lowb, upb = ([[16, 8], [0, 16]], 15, -1), ([[-16, 8], [0, 16]], 0, 1)
+    io(col[:, 0:1], [[0, 1]], 0, 1, ["c0"], 1)
+    io(T.pi[:, 0:16], [[0, 16]], 0, 1, ["pi0"], 16, False)
+    io(T.xb[:], [[1, 144]], 0, 0, ["xb"], 144)
     io(T.mc[:], [[0, 8], [1, 16]], 0, 0, ["mc"], 128)
-    io(T.xg[:], [[16, 8], [0, 16]], 0, 0, ["xg"], 128)
-    io(T.i16[:], [[16, 128]], 0, 0, ["i16"], 128)
-    io(T.one[:], [[0, 128]], 1, 0, ["one"], 128)
-    ts(T.pi[:, 4:5], T.pi[:, 0:1], 15, None, ALU.bitwise_and, None, ["pi0"], ["pi4"], 1)
-    cp(col[:, 0:1], T.pi[:, 0:1], ["pi0"], ["c0"], 1)
-    cp(col[:, 1:2], T.pi[:, 4:5], ["pi4"], ["c1"], 1)
-    tt(col[:, 2:3], col[:, 0:1], col[:, 1:2], ALU.subtract, ["c0", "c1"], ["c2"], 1)
-    ts(col[:, 3:4], col[:, 2:3], 15.0, None, ALU.add, None, ["c2"], ["c3"], 1)
-    ts(col[:, 4:5], col[:, 0:1], -1.0, None, ALU.add, None, ["c0"], ["c4"], 1)
-    ts(col[:, 5:6], col[:, 1:2], 0.0, None, ALU.is_gt, None, ["c1"], ["c5"], 1)
+    io(T.db[:], [[1, 128]], 0, -1, ["db"], 128)
+    keep(T.db[:], *lowb, 99, "db", 128)
+    keep(T.db[:], *upb, 99, "db", 128)
+    io(T.rst[:], [[0, 128]], 0, 0, ["rst"], 128)
+    io(T.rst[:, 0:128:16], [[0, 8]], 1048576, 0, ["rst"], 8)
+    ts(T.pi[:, 16:17], T.pi[:, 0:1], 15, None, AND, None, ["pi0"], ["pi16"], 1)
+    cp(col[:, 1:2], T.pi[:, 16:17], ["pi16"], ["c1"], 1)
+    tt(col[:, 2:3], col[:, 0:1], col[:, 1:2], SU, ["c0", "c1"], ["c2"], 1)
+    ts(col[:, 3:4], col[:, 2:3], 15.0, None, AD, None, ["c2"], ["c3"], 1)
+    ts(col[:, 10:11], col[:, 1:2], 4096.0, None, AD, None, ["c1"], ["c10"], 1)
+    ms(col[:, 11:12], 2049.5, ["c11"], 1)
     cp(col[:, 6:7], T.wk[:, 0:1], ["wk0"], ["c6"], 1)
     cp(col[:, 7:8], T.wk[:, 8:9], ["wk8"], ["c7"], 1)
-    EQ, MU, AD = ALU.is_equal, ALU.mult, ALU.add
-    x128 = T.xf[:, 0:128]
-    ts(T.idp[:], x128, col[:, 0:1], None, EQ, None, ["xf", "c0"], ["idp"], 128)
-    ts(T.idn[:], x128, col[:, 0:1], -1.0, EQ, MU, ["xf", "c0"], ["idn"], 128)
-    ts(T.idh[:], x128, col[:, 0:1], 0.5, EQ, MU, ["xf", "c0"], ["idh"], 128)
-    diag(T.idf[:], 1, "idf")
-    ts(T.shf[:], x128, col[:, 4:5], col[:, 5:6], EQ, MU, ["xf", "c4", "c5"], ["shf"], 128)
-    ts(T.bof[:], T.xg[:], col[:, 2:3], None, EQ, None, ["xg", "c2"], ["bof"], 128)
-    ts(T.big[:], T.xf[:], col[:, 3:4], None, EQ, None, ["xf", "c3"], ["big"], 144)
-    ts(T.bigh[:], T.xf[:], col[:, 3:4], None, EQ, None, ["xf", "c3"], ["bigh"], 144)
-    io(col[:, 8:9], [[0, 1]], -2048, 0, ["c8"], 1)
-    ts(T.wbig[:], T.xf[:], col[:, 3:4], col[:, 6:7], EQ, MU, ["xf", "c3", "c6"], ["wbig"], 144)
-    if EX:
-        ts(T.mc2[:], T.mc[:], -7.5, None, AD, None, ["mc"], ["mc2"], 64)
-    if MV:
-        ts(T.wbh[:], T.wbig[:], 0.5, None, MU, None, ["wbig"], ["wbh"], 72)
-        ms(col[:, 14:15], -0.5, ["c14"], 1)
-    ts(T.rs[:], T.xf[:, 0:128:16], col[:, 2:3], None, EQ, None, ["xf", "c2"], ["rs"], 8)
+    act(col[:, 8:9], col[:, 6:7], AF.Copy, ["c6"], ["c8"], 1, scale=0.5)
+    x128 = T.xb[:, 0:128]
+    ts(T.idp[:], x128, col[:, 0:1], None, EQ, None, ["xb", "c0"], ["idp"], 64)
+    act(T.idn[:], T.idp[:], AF.Copy, ["idp"], ["idn"], 128, scale=-1.0)
+    ts(T.id16[:], x128, col[:, 0:1], None, EQ, None, ["xb", "c0"], ["id16"], 64)
+    ts(T.sh16[:], T.db[:], -1.0, None, EQ, None, ["db"], ["sh16"], 64)
+    ts(T.bof[:], T.db[:], 50.0, None, ALU.is_lt, None, ["db"], ["bof"], 128)
+    ts(T.big[:], T.xb[:], col[:, 3:4], None, EQ, None, ["xb", "c3"], ["big"], 72)
+    ts(T.bigh[:], T.xb[:], col[:, 3:4], None, EQ, None, ["xb", "c3"], ["bigh"], 72)
+    ts(T.wbh[:], T.xb[:], col[:, 3:4], col[:, 8:9], EQ, MU, ["xb", "c3", "c8"], ["wbh"], 72)
+    ts(T.mc2[:], T.mc[:], -7.5, None, AD, None, ["mc"], ["mc2"], 64)
+    ts(T.rs[:], T.xb[:, 0:128:16], col[:, 2:3], None, EQ, None, ["xb", "c2"], ["rs"], 4)
     for b, s in enumerate((16.0, -32.0, 32.0, -16.0)):
-        ts(T.bo8[:, 8 * b:8 * b + 8], T.rs[:], s, None, MU, None, ["rs"], ["bo%d" % b], 8)
-    ts(T.dm[:], T.mc[:], col[:, 1:2], None, EQ, None, ["mc", "c1"], ["dm"], 128)
-    ts(T.rst[:], T.mc[:], 0.0, 1048576.0, EQ, MU, ["mc"], ["rst"], 128)
-    ms(T.c128[:], 2.0 ** -7, ["c128"], 128)
-    ms(T.cq[:], -2.0 ** -9, ["cq"], 128)
-    cp(T.rl[:, 0:8], T.xf[:, 0:8], ["xf"], ["rl"], 8)
+        act(T.bo8[:, 8 * b:8 * b + 8], T.rs[:], AF.Copy, ["rs"], ["bo%d" % b], 8, scale=s)
+    ts(T.dm[:], T.mc[:], col[:, 1:2], None, EQ, None, ["mc", "c1"], ["dm"], 64)
+    ms(T.c128[:], 2.0 ** -7, ["c128"], 64)
+    cp(T.rl[:, 0:8], T.xb[:, 0:8], ["xb"], ["rl"], 8)
+    ts(T.pi[:, 24:32], T.pi[:, 8:16], nr - 1, None, AND, None, ["pi0"], ["pi24"], 8)
+    cp(T.rl[:, 8:16], T.pi[:, 24:32], ["pi24"], ["rp"], 8)
     ib = T.ib[:, 0:8]
-    ts(ib, T.xf[:, 0:128:16], col[:, 1:2], None, AD, None, ["xf", "c1"], ["ib"], 8)
-    io(T.wj[:], [[0, 128]], 0, 0, ["wj"], 128)
-    io(T.cn[:], [[0, 48]], 0, 0, ["cn%d" % h for h in range(NP)], 48)
-    for v, n in enumerate(sizes):
-        nr = n // 16
-        xm, kr = T.xm[:, 128 * v:128 * v + n], T.kr[:, 128 * v:128 * v + n]
-        io(xm, [[1, 16], [0, nr]], 0, 0, ["xm%d" % v], n)
-        ts(xm, xm, col[:, 1:2], col[:, 7:8], EQ, MU, ["xm%d" % v, "c1", "c7"], ["xm%d" % v], n)
-        mm([(T.bG1[:, 0:n], T.bof[:], xm, True, True, n)], ["bof", "xm%d" % v], ["G1"], "bG1", True)
-        cp(kr, T.bG1[:, 0:n], ["G1"], ["kr%d" % v], n, ["bG1"])
-        ts(T.rli[:, 8 * v:8 * v + 8], ib, -(nr - 1) / 2.0, 1.0 / nr, AD, MU, ["ib"], ["rli%d" % v], 8)
-        tm = T.ib[:, 8 + 8 * v:16 + 8 * v]
-        ts(tm, T.rli[:, 8 * v:8 * v + 8], -float(nr), None, MU, None, ["rli%d" % v], ["ibm%d" % v], 8)
-        tt(tm, tm, ib, AD, ["ib", "ibm%d" % v], ["ibm%d" % v], 8)
-        cp(T.rl[:, 8 + 8 * v:16 + 8 * v], tm, ["ibm%d" % v], ["rp%d" % v], 8)
-        for b, s in enumerate((n, nr)):
-            if EX:
-                ms(T.ce[:, 16 * v + 8 * b:16 * v + 8 * b + 8], 7.5 * s, ["ce%d%d" % (v, b)], 8)
-                diag(T.idc[:, 256 * v + 128 * b:256 * v + 128 * b + 128], s, "idc%d%d" % (v, b))
-            else:
-                ts(T.rc[:, 16 * v + 8 * b:16 * v + 8 * b + 8], T.rs[:], float(s), None, MU, None, ["rs"], ["rc%d%d" % (v, b)], 8)
-        for j in range(1, 5):
-            io(T.wj[:, 64 * v + 16 * j - 16:64 * v + 16 * j - 8], [[0, 8]], (5 - j) * 16 * n, 0, ["wj"], 8)
-    ts(T.kj[:, 4:8], T.xf[:, 1:5], 32.0, None, MU, None, ["xf"], ["kj4"], 4)
-    ts(T.kj[:, 0:4], T.kj[:, 4:8], T.kr[:, 0:1], -262156.0, MU, AD, ["kj4", "kr0"], ["b10"], 4)
-    cp(T.cc[:, 0:8], ib, ["ib"], ["cc0"], 8)
-    cp(T.cc[:, 8:16], T.xf[:, 0:8], ["xf"], ["cc1"], 8)
-    ms(T.rg0[:, 64:128], 0.0, ["rg0"], 64)
-    io(T.cg0[:, 64:128], [[1, 4], [99, 2], [0, 8]], 1, 0, ["cg0"], 64)
-    io(T.cg0[:, 8:48], [[1, 5], [0, 8]], 0, 0, ["cg0_1"], 40)
-    for b in (0, 1, 2, 3, 4, 5, 7, 8, 10, 12, 14):
-        cp(T.rg0[:, 8 * b:8 * b + 8], T.rs[:], ["rs"], ["rg0"] if b > 7 else ["rg0_%d" % b], 8)
-    ts(T.cg0[:, 0:8], ib, 16.0, None, MU, None, ["ib"], ["cg0_0"], 8)
-    ts(T.rg0[:, 48:56], T.rs[:], 4096.0, None, MU, None, ["rs"], ["rg0_6"], 8)
-    io(T.cg0[:, 48:56], [[0, 8]], -40960, 0, ["cg0_6"], 8)
-    ts(T.cg0[:, 56:64], ib, 16.0, 2048.0, MU, AD, ["ib"], ["cg0_7"], 8)
-    RG = [["rg0"] + ["rg0_%d" % b for b in range(8)], ["rg1"]]
-    CG = [["cg0"] + ["cg0_%d" % b for b in range(8)], ["cg1"]]
-    cp(T.rg1[:], T.rg0[:], RG[0], ["rg1"], 64)
-    cp(T.cg1[:], T.cg0[:], CG[0], ["cg1"], 64)
-    ts(T.rg1[:, 48:56], T.rs[:], -4096.0, None, MU, None, ["rs"], ["rg1"], 8)
-    ms(T.cg1[:, 48:56], 45056.0, ["cg1"], 8)
-    ts(T.cg1[:, 56:64], ib, 16.0, None, MU, None, ["ib"], ["cg1"], 8)
-    for b, (s, a) in enumerate([(16.0, 16.0 * B["i0"]) for B in H] + [(16.0, 15.0), (16.0, 2063.0)] + [(1.0, 64.0 * n) for n in sizes]):
-        ts(T.bc[:, 8 * b:8 * b + 8], ib, s, a, MU, AD, ["ib"], ["bc%d" % b], 8)
-    tb = T.tb
-    ts(T.et[:], T.xf[:, 0:32], col[:, 1:2], None, EQ, None, ["xf", "c1"], ["et"], 32)
-    ts(T.eb[:, 0:16], T.xf[:, 0:16], col[:, 1:2], None, ALU.subtract, None, ["xf", "c1"], ["eb"], 16)
+    ts(ib, T.xb[:, 0:128:16], col[:, 1:2], None, AD, None, ["xb", "c1"], ["ib"], 8)
+    for b, s in enumerate((1.0, 1.0, 1.0, -4096.0)):
+        act(T.hc[:, 128 * b:128 * b + 128], T.idp[:], AF.Copy, ["idp"], ["hc%d" % b], 128, scale=s)
+    for b, s in enumerate((16.0, 0.0, 16.0, 0.0)):
+        act(T.hp[:, 8 * b:8 * b + 8], ib, AF.Copy, ["ib"], ["hp%d" % b], 8, scale=s)
+    ms(T.hq[:, 0:24], 7.5, ["hq0"], 12)
+    io(T.hq[:, 24:32], [[0, 8]], 14336, 0, ["hq1"], 8)
+    HK = ["hc%d" % b for b in range(4)] + ["hp%d" % b for b in range(4)] + ["hq0", "hq1"]
+    for b, s in enumerate((n, nr, ALT)):
+        act(T.cc[:, 128 * b:128 * b + 128], T.idp[:], AF.Copy, ["idp"], ["cc%d" % b], 128, scale=-float(s))
+        act(T.cp[:, 8 * b:8 * b + 8], T.xb[:, 0:8] if b == 1 else ib, AF.Copy, ["ib", "xb"], ["cp%d" % b], 8)
+        io(T.cq[:, 8 * b:8 * b + 8], [[0, 8]], int((-6.5 if b == 2 else 7.5) * s), 0, ["cq%d" % b], 8)
+    CK = ["c%s%d" % (x, b) for x in "cpq" for b in range(3)]
+    for b, a in enumerate((0.0, 16.0 * n, 2063.0)):
+        act(T.bc[:, 8 * b:8 * b + 8], ib, AF.Copy, ["ib"], ["bc%d" % b], 8, bias=a, scale=16.0)
+    for c in range(5):
+        act(T.lc[:, c:40:5], ib, AF.Copy, ["ib"], ["lc%d" % c], 8, bias=float(16 * n * (4 - c) + 15 * n if c else ALT))
     for j in range(5):
-        diag(T.dq[:, 128 * j:128 * j + 128], -16384 * j if j else -8192, "dq%d" % j)
-        io(col[:, 9 + j:10 + j], [[0, 1]], -8192 * j * j, 0, ["c%d" % (9 + j)], 1)
-    ts(tb[:, 0:16], T.xf[:, 0:16], col[:, 1:2], None, ALU.subtract, None, ["xf", "c1"], ["t0"], 16)
-    ts(tb[:, 16:32], tb[:, 0:16], -4.0, None, ALU.is_lt, None, ["t0"], ["keep"], 16)
-    ts(tb[:, 32:48], tb[:, 0:16], 0.0, None, ALU.is_ge, None, ["t0"], ["le"], 16)
-    ts(tb[:, 48:64], tb[:, 0:16], 0.0, None, ALU.is_gt, None, ["t0"], ["lt"], 16)
-    tt(tb[:, 64:80], tb[:, 16:32], tb[:, 48:64], AD, ["keep", "lt"], ["old"], 16)
-    for par in (0, 1):
-        nb, ob = (2048.0, 0.0) if par == 0 else (0.0, 2048.0)
-        al, tm, k = tb[:, 96 + 16 * par:112 + 16 * par], tb[:, 80:96], "al%d" % par
-        ts(al, tb[:, 0:16], nb + 15.0, None, AD, None, ["t0"], [k], 16)
-        ts(tm, tb[:, 48:64], col[:, 1:2], ob, AD, AD, ["lt", "c1"], ["tm"], 16)
-        tt(tm, tm, al, ALU.subtract, ["tm", k], ["tm"], 16)
-        tt(tm, tm, tb[:, 64:80], MU, ["tm", "old"], ["tm"], 16)
-        tt(al, al, tm, AD, ["tm", k], [k], 16)
+        ts(T.on[:, 128 * j:128 * j + 128], T.db[:], float(j), 4096.0, EQ, MU, ["db"], ["on%d" % j], 64)
+    ts(T.pk[:], T.db[:], 4.0, -4096.0, ALU.is_le, MU, ["db"], ["pk"], 64)
+    io(T.pl[:], [[0, 128]], -4096, 0, ["pl"], 128)
+    keep(T.pl[:], [[1, 128]], 0, -1, 0, "pl", 128)
+    keep(T.pl[:], *upb, 0, "pl", 128)
+    io(T.lo[:], [[-32, 8], [-4, 16]], 30, 2, ["lo"], 128)
+    keep(T.lo[:], [[1, 128]], 0, -1, 2, "lo", 128)
+    keep(T.lo[:], [[-1, 128]], 4, 1, 0, "lo", 128)
+    keep(T.lo[:], *lowb, 0, "lo", 128)
+    keep(T.lo[:], *upb, 0, "lo", 128)
+    io(T.i32[:], [[32, 128]], 0, 0, ["i32"], 128)
+    if GV:
+        ts(T.zv[:], T.bof[:], 16.0, None, MU, None, ["bof"], ["zv"], 128)
+        keep(T.zv[:], [[0, 32], [-1, 4]], GV - 1, 0, 0, "zv", 128)
+    io(T.dd[:], [[0, 32]], -262144, 0, ["dd"], 32)
+    keep(T.dd[:], [[1, 4], [-16, 8]], -15, 1, 0, "dd", 32)
+    keep(T.dd[:], [[0, 4], [16, 8]], 15, -1, 0, "dd", 32)
+    io(T.xm[:], [[-1, 16], [0, nr]], 15, 0, ["xm"], 128)
+    ts(T.xm[:], T.xm[:], col[:, 1:2], col[:, 7:8], EQ, MU, ["xm", "c1", "c7"], ["xm"], 128)
+    mm([(T.bG1[:, 0:128], T.bof[:], T.xm[:], True, True, 512), (T.bG1[:, 128:129], T.bof[:], col[:, 6:7], True, True, 256)],
+       ["bof", "xm", "c6"], ["G_1"], "bG_1")
+    act(T.kr[:], T.bG1[:, 0:128], AF.Copy, ["G_1"], ["kr"], 128, ["bG_1"])
+    act(col[:, 9:10], T.bG1[:, 128:129], AF.Copy, ["G_1"], ["c9"], 1, ["bG_1"], scale=1025.0)
+    act(T.kj[:, 4:8], T.xb[:, 1:5], AF.Copy, ["xb"], ["kj4"], 4, scale=32.0)
+    ts(T.kj[:, 0:4], T.kj[:, 4:8], T.kr[:, 120:121], -262156.0, MU, AD, ["kj4", "kr"], ["b10"], 4)
     for h, B in enumerate(H):
-        n, i0 = B["n"], B["i0"]
-        io(B["si"][:, 48:56], [[0, 8]], 0, 0, ["ti0_%d" % h], 8, False)
-        if EX:
-            io(B["fb"][:], [[0, 144]], 0, 0, ["fb_%d" % h], 144)
-        for c in range(11):
-            io(B["pool"][:, 2048 + c:2048 + 16 * n:16], [[0, n]], 0, 0, ["fill%d_%d" % (h, c)], n)
-        for c in range(2 if n < 128 else 0):
-            io(B["pool"][:, 2048 * c + 16 * n:2048 * c + 2048], [[0, 2048 - 16 * n]], 0, 0, ["fill%d_%d" % (h, 11 + c)], 2048 - 16 * n)
-        cp(B["M"][:, 0:n], T.nmi[:, i0:i0 + n], ["nmi"], ["M_%d" % h], n)
-        ts(B["M"][:, 128:128 + n], T.nmi[:, i0:i0 + n], -2048.0, None, AD, None, ["nmi"], ["M2_%d" % h], n)
+        io(B["fb"][:], [[0, 144]], 0, 0, ["fb_%d" % h], 144)
+        ts(B["N7"][:, 6::7], T.nmi[:, n * h:n * h + n], -2048.0, None, AD, None, ["nmi"], ["M2_%d" % h], n)
+        ms(B["bD"][:, 272:312:5], 0.0, ["rz_%d" % h], 16, ["bD_%d" % h])
+    io(T.one[:], [[0, 128]], 32, 0, ["one"], 128)
+    io(T.rsn[:], [[0, 448]], 0, 0, ["rsn"], 448)
+    io(T.rsn[:, 0:448:7], [[0, 64]], -16384, 0, ["rsn"], 64)
+    io(T.rsn[:, 5:448:7], [[0, 64]], -6144, 0, ["rsn"], 64)
+    for par in range(2):
+        for h, B in enumerate(H):
+            for c in range(11):
+                io(B["pool"][:, 4096 * par + c:4096 * par + 2048:16], [[0, n]], 0, 0, ["fill%d%d_%d" % (par, c, h)], n)
 
-    def sel(tab, q, n=128):
-        return tab[0:n, 15 - q:143 - q]
+    def sel(tab, q):
+        return tab[:, 15 - q:143 - q]
 
     def keys(h):
-        return lambda s: s + str(h % 2) if s in ("G", "bG") else s + "_%d" % h
+        return lambda s: s + "_%d" % h
 
-    def scan(B, k):
-        n = B["n"]
-        op("V", lambda: V.tensor_tensor_scan(B["run"][0:n, :], T.rst[0:n, :], B["bD"][0:n, 0:128], 0.0, AD, ALU.min), ["rst", k("D")], [k("run")], vc(128), [k("bD")])
+    def blocks(k, name, a, b):
+        return [k("%s%d" % (name, x)) for x in range(a // 8, b // 8)]
 
-    def argmin(B, k):
-        n, si = B["n"], B["si"]
-        scan(B, k)
-        cp(si[0:n, 56:64], B["run"][0:n, 15::16], [k("run")], [k("ti8")], 8)
-        ts(si[0:n, 48:56], si[0:n, 56:64], 15, None, ALU.bitwise_and, None, [k("ti8")], [k("ti0")], 8)
-        tg(B["ex"][:], si[:, 48:56], T.rl[:, 0:8], T.dm[:], MU, [k("ti0"), "rl", "dm"], [k("ex")], 128)
+    def least(B, k):
+        scan(B["run"][:], T.rst[:], B["bD"][:, 0:128], AD, MN, ["rst", k("D")], [k("run")], 128, [k("bD")])
+        ts(B["sm"][:, 32:40], B["run"][:, 15::16], 16 * MAGIC, 16 * MAGIC, AD, SU, [k("run")], [k("m32")], 8)
+        tt(B["fb"][:, 15:143:16], B["run"][:, 15::16], B["sm"][:, 32:40], SU, [k("run"), k("m32")], [k("fb")], 8)
 
-    def new(B, j):
-        return B["pool"][:, 2063 - j:2048 + 16 * B["n"]:16]
+    def spread(B, k, cv, tabs, w, kk, kw):
+        return (lambda: mm([(cv, T.idp[:], tabs[1][:, 0:w], True, False, w), (cv, T.c128[:], tabs[2][:, 0:w], False, False, w)], ["idp", "c128"] + kk, [kw], k("bD")),
+                lambda: mm([(cv, sel(B["fb"], q), tabs[0][:, q:16 * w:16], False, q == 15, w) for q in range(16)], kk + [k("fb")], [kw], k("bD")))
 
-    def middle(h, B, k, prev, kprev, j):
-        n = B["n"]
-        o = B["bM"][:, 256:256 + n]
-        mm([(o, T.cq[:], T.one[:, 0:n], True, False, n), (o, T.idh[:], prev, False, False, n)], ["cq", "one", "idh", kprev], [k("mid")], k("bM"))
-        mm([(o, T.idh[:], B["xe"][:, 0:n], False, True, n)], ["idh", k("xe")], [k("mid")], k("bM"))
-        ts(new(B, j), o, MAGIC, MAGIC, AD, ALU.subtract, [k("mid")], [k("new%d" % j)], n, [k("bM")])
+    def new(B, t, j):
+        return B["pool"][:, 4096 * (t % 2) + 15 - j:4096 * (t % 2) + 2048:16]
 
-    def place(B, k, j, win, lst, kl):
-        n = B["n"]
-        Pj, G = B["P"][:, 128 * j:128 * j + n], B["bG"][:, 0:n]
-        tg(Pj, win, lst, T.dm[:, 0:n], MU, [k("ci%d" % j), k("cj%d" % j), k("cj%dx" % j), kl, "dm"], [k("P%d" % j)], n)
-        mm([(G, T.dq[:, 0:128], B["em"][:, 128:128 + n], True, False, 32)]
-           + ([(G, T.dq[:, 128 * j:128 * j + 128], B["em"][:, 0:n], False, False, 32)] if j else [])
-           + [(G, T.bof[:], Pj, False, True, n)], ["bof", "dq0", "dq%d" % j, k("em"), k("en"), k("P%d" % j)], [k("G")], k("bG"), True)
-        act(B["pl"][:, 128 * j:128 * j + n], G, AF.Relu, [k("G"), "c%d" % (9 + j)], [k("pl%d" % j)], n, [k("bG")], col[:, 9 + j:10 + j])
+    def middle(B, k, t, j, win, lst, kk, prev, kprev):
+        if SH:
+            tg(B["sq"][:], win, lst, B["sh"][:], AD, kk + [k("sh")], [k("sq")], n)
+        else:
+            tg(B["tp"][:], win, lst, prev, AD, kk + [kprev], [k("tp")], n)
+            ts(B["sq"][:], B["tp"][:], 2049.5, None, AD, None, [k("tp")], [k("sq")], n / 2)
+        ts(new(B, t, j), B["sq"][:], -2050.0, 0.5, AD, MU, [k("sq")], [k("new%d" % j)], n / 2)
+        if SH and j < 4:
+            act(B["sh"][:], new(B, t, j), AF.Identity, [k("new%d" % j), "c11"], [k("sh")], n, (), col[:, 11:12])
+
+    def pick(B, k, j, win, lst, kk):
+        tg(B["P"][:, n * j:n * j + n], win, lst, T.dm[:], MU, kk + ["dm"], [k("P%d" % j)], n)
 
     def head(t, h):
         cur_h[0] = h
         B, par, k = H[h], t % 2, keys(h)
-        n, i0, v, si, sm, lu, M, bD = B["n"], B["i0"], B["v"], B["si"], B["sm"], B["lu"], B["M"], B["bD"]
-        nr = n // 16
-        z, kz, kS = B["z"][:, 128 * t:128 * t + n], "z%d%d" % (h, t), "S%d%d" % (h, par)
-        s0 = 4096 * par
-        mm([(B["bM"][:, 400:400 + nr], sel(T.big, q), B["z"][:, 128 * t + q:128 * t + n:16], q == 0, q == 15, 8) for q in range(16)], ["big", kz], [k("sz")], k("bM"))
-        cp(si[:, 32:32 + nr], B["bM"][:, 400:400 + nr], [k("sz")], [k("s32")], nr, [k("bM")])
-        ts(si[:, 40:40 + nr], si[:, 32:32 + nr], 15, None, ALU.bitwise_and, None, [k("s32")], [k("s40")], nr)
-        tt(B["ci"][:, 0:nr], si[:, 40:40 + nr], T.bc[:, 8 * h:8 * h + nr], AD, [k("s40"), "bc%d" % h], [k("ci0")], nr)
-        ts(lu[:, 112:112 + nr], B["ci"][:, 0:nr], -16.0 * i0, None, AD, None, [k("ci0")], [k("ln")], nr)
-        op("V", lambda: V.tensor_copy(X[:, 16 * i0:16 * (i0 + n)].indirect(lu[:, 112:112 + nr]), z), [k("ln"), kz], ["X%d" % h], 55 + n * 4)
-        mm([(bD[0:n, 0:128], T.c128[:, 0:n], T.mc[:], True, False, 128)], ["c128", "mc"], [k("D")], k("bD"))
-        w = 512 // n
+        si, sm, lu, bD, bM, bG, oh = B["si"], B["sm"], B["lu"], B["bD"], B["bM"], B["bG"], B["oh"][:]
+        z, kz, kS = B["z"][:, n * t:n * t + n], "z%d%d" % (h, t), "S%d%d" % (h, par)
+        s0 = 4096 * par + 2048
+        row = lambda m: B["pool"][:, s0 + m:s0 + 2048:16]
+        mm([(bM[:, 400:408], sel(T.big, q), B["z"][:, n * t + q:n * t + n:16], q == 0, q == 15, 8) for q in range(16)], ["big", kz], [k("sz")], k("bM"))
+        cp(si[:, 32:40], bM[:, 400:408], [k("sz")], [k("s32")], nr, [k("bM")])
+        ts(si[:, 40:48], si[:, 32:40], 15, None, AND, None, [k("s32")], [k("s40")], nr)
+        tt(B["nn"][:], si[:, 40:48], T.bc[:, 8 * h:8 * h + 8], AD, [k("s40"), "bc%d" % h], [k("nn")], nr)
+        ts(lu[:, 16:24], B["nn"][:], -2048.0 * h, None, AD, None, [k("nn")], [k("ln")], nr)
+        op("V", lambda: V.tensor_copy(X[:, 2048 * h:2048 * h + 2048].indirect(lu[:, 16:24]), z), [k("ln"), kz], ["X%d" % h], (55, 4 * n, 0))
+        pick(B, k, 0, B["nn"][:], T.rl[:, 0:8], [k("nn"), "rl"])
+        if SH:
+            act(B["sh"][:], z, AF.Identity, [kz, "c11"], [k("sh")], n, (), col[:, 11:12])
+        rows = lambda c: B["pool"][:, s0 + c:s0 + 2048:4]
+        mnc = lambda c: (B["mn"][:, 512 * c:512 * c + 512], [k("mn%d" % m) for m in range(4 * c, 4 * c + 4)])
+        mm([(bD[:, 0:128], T.c128[:], T.mc2[:], True, False, 128)]
+           + [(bD[:, m:128:16], row(m), T.bo8[:, 0:8], False, False, 8) for m in range(16) if m % 4 < GV], ["c128", "mc2", kS, "bo0"], [k("D")], k("bD"))
+        for c in range(GV, 4):
+            bk, kb = ("bG", k("G")) if c % 2 else ("bS", k("sP"))
+            mm([(B[bk][:], T.idp[:], rows(c), True, False, 512)], ["idp", kS], [kb], k(bk))
+            mm([(B[bk][:, x:512:4], T.idn[:], z, False, x == 3, n) for x in range(4)], ["idn", kz], [kb], k(bk))
+            act(mnc(c)[0], B[bk][:], AF.Abs, [kb], mnc(c)[1], 512, [k(bk)])
         if GV:
-            zp, row = B["bM"][:, 0:n], lambda m: B["pool"][:, s0 + m:s0 + 16 * n:16]
-            mm([(zp, T.idp[:], z, True, True, n)], ["idp", kz], [k("zp")], k("bM"))
-            mm([(bD[0:n, m:128:16], row(m), T.bo8[:, 0:8], False, False, 8) for m in range(GV)], [kS, "bo0"], [k("D")], k("bD"))
-            mm([(bD[0:n, m:128:16], z, T.bo8[:, 0:8], False, False, 8) for m in range(GV)], [kz, "bo0"], [k("D")], k("bD"))
-            for m in range(GV):
-                tt(B["mn"][:, n * m:n * m + n], row(m), zp, ALU.min, [kS, k("zp")], [k("mn%d" % m)], n, [k("bM")])
-        for b, m0 in enumerate(range(GV, 16, w)):
-            bk, ms_ = "bG" if b % 2 else "bS", range(m0, min(m0 + w, 16))
-            lst = []
-            for m in ms_:
-                o = B[bk][:, n * (m - m0):n * (m - m0 + 1)]
-                lst += [(o, T.idp[:], B["pool"][:, s0 + m:s0 + 16 * n:16], True, False, n), (o, T.idn[:], z, False, True, n)]
-            kb = k("sP") if bk == "bS" else k("G")
-            mm(lst, ["idp", "idn", kS, kz], [kb], k(bk))
-            act(B["mn"][:, n * m0:n * (ms_[-1] + 1)], B[bk][:, 0:n * len(ms_)], AF.Abs, [kb], [k("mn%d" % m) for m in ms_], n * len(ms_), [k(bk)])
-        for m0 in range(0, 16, w):
-            ms_ = range(m0, min(m0 + w, 16))
-            mm([(bD[0:n, m:128:16], B["mn"][:, n * m:n * m + n], T.bo8[:, 8:16] if m < GV else T.bo8[:, 0:8], False, m == 15, 8) for m in ms_],
-               [k("mn%d" % m) for m in ms_] + ["bo0", "bo1"], [k("D")], k("bD"))
-        argmin(B, k)
-        mm([(bD[:, 128:256], T.idp[:], T["cg%d" % par][:], True, False, 128), (bD[:, 128:256], B["ex"][0:n, :], T["rg%d" % par][0:n, :], False, True, 128)],
-           ["idp", k("ex")] + RG[par] + CG[par], [k("cv")], k("bD"))
-        cp(lu[:, 0:48], bD[:, 128:176], [k("cv")], [k("lg")], 48, [k("bD")])
-        o1, o2 = (ALU.max, ALU.min) if par == 0 else (ALU.min, ALU.max)
-        tt(sm[:, 16:24], bD[:, 176:184], T.bc[:, 8 * (NP + par):8 * (NP + par) + 8], o1, [k("cv"), "bc%d" % (NP + par)], [k("m16")], 8, [k("bD")])
-        tt(sm[:, 24:32], bD[:, 184:192], sm[:, 16:24], o2, [k("cv"), k("m16")], [k("m24")], 8, [k("bD")])
-        ts(B["lw"][:], bD[:, 192:256], 15.0, None, ALU.is_le, None, [k("cv")], [k("lw")], 64, [k("bD")])
-        ag(B["xe"][:, 0:n], B["pool"][:, s0:s0 + 16 * n], lu[:, 0:nr], [kS, k("lg")], [k("xe")], n)
-        middle(h, B, k, z, kz, 0)
+            mm([(bM[:, x:512:4], T.idp[:], z, True, True, n) for x in range(4)], ["idp", kz], [k("zp")], k("bM"))
+            mm([(bD[:, 0:128], z, T.zv[:], False, False, 128)], [kz, "zv"], [k("D")], k("bD"))
+            for c in range(GV):
+                tt(mnc(c)[0], rows(c), bM[:], MN, [kS, k("zp")], mnc(c)[1], 512, [k("bM")])
+        for c in (0, 2, 1, 3):
+            mm([(bD[:, 4 * x + c:128:16], B["mn"][:, 512 * c + x:512 * c + 512:4], T.bo8[:, 8:16] if c < GV else T.bo8[:, 0:8], False, c == 3 and x == 3, 8) for x in range(4)],
+               mnc(c)[1] + ["bo0", "bo1"], [k("D")], k("bD"))
+        cv = spread(B, k, bD[:, 128:160], (T.hc, T.hp, T.hq), 32, HK, k("cv"))
+        least(B, k)
+        cv[0]()
+        cv[1]()
+        cp(lu[:, 0:16], bD[:, 128:144], [k("cv")], [k("lg")], 16, [k("bD")])
+        tt(sm[:, 16:24], bD[:, 152:160], T.bc[:, 16:24], MN, [k("cv"), "bc2"], [k("m16")], 8, [k("bD")])
+        tt(sm[:, 24:32], bD[:, 144:152], sm[:, 16:24], MX, [k("cv"), k("m16")], [k("m24")], 8, [k("bD")])
+        middle(B, k, t, 0, states(B, par), lu[:, 0:8], [kS, k("lg")], z, kz)
+        ag(oh, T.dm[:, 0:16], lu[:, 8:16], ["dm", k("lg")], [k("oh")], n)
+        lst = []
         for j in range(1, 5):
-            tg(B["Qh"][:, n * j - n:n * j], T.et[:, 0:32], lu[:, 8 + 8 * j:8 + 8 * j + nr], M[:, 128:128 + n], MU, ["et", k("lg"), k("M2")], [k("Q%d" % j)], n)
-        for q0 in range(0, 16, 4):
-            mm([(B["bG"][:, 256:256 + 4 * nr], sel(T.bigh, q), B["Qh"][:, q:4 * n:16], q == 0, q == 15, 32) for q in range(q0, q0 + 4)],
-               ["bigh"] + [k("Q%d" % j) for j in range(1, 5)], [k("G")], k("bG"))
-        for j in range(1, 5):
-            c0 = B["bG"][:, 256 + nr * (j - 1):256 + nr * j]
-            ts(B["cu"][:, 128 * j - 128:128 * j - 128 + nr], c0, 2048.0, None, AD, None, [k("G")], [k("cz%d" % j)], nr, [k("bG")])
-            ts(B["ci"][:, 128 * j:128 * j + nr], c0, 2048.0, None, AD, None, [k("G")], [k("ci%d" % j)], nr, [k("bG")])
-        cp(lu[:, 120:128], sm[:, 24:32], [k("m24")], [k("l15")], 8)
-        tt(B["lw"][:], B["lw"][:], T.wj[:, 64 * v:64 * v + 64], MU, [k("lw"), "wj"], [k("lw")], 64)
-        hl = lu[:, 8:8 + nr]
-        ag(B["em"][:, 0:n], T.eb[:, 0:16], hl, ["eb", k("lg")], [k("em")], n)
-        act(B["em"][:, 128:128 + n], B["em"][:, 0:n], AF.Square, [k("em")], [k("en")], n)
-        tg(M[:, 256:256 + n], tb[:, 16:32], hl, M[:, 0:n], MU, ["keep", k("lg"), k("M")], [k("K")], n)
-        tg(M[:, 384:384 + n], tb[:, 32:48], hl, M[:, 0:n], MU, ["le", k("lg"), k("M")], [k("L")], n)
-        tg(M[:, 640:640 + n], tb[:, 96 + 16 * par:112 + 16 * par], hl, T.i16[:, 0:n], AD, ["al%d" % par, k("lg"), "i16"], [k("rf")], n)
-        cp(B["cu"][:, 512:512 + n], M[:, 640:640 + n], [k("rf")], [k("ru")], n)
+            o = bG[:, n * j - n:n * j]
+            lst += [(o, T.id16[:], B["N7"][:, 6::7], True, False, n), (o, T.on[:, 128 * j:128 * j + 128], oh, False, True, n)]
+        mm(lst, ["id16", k("M2"), k("oh")] + ["on%d" % j for j in range(1, 5)], [k("G")], k("bG"))
+        ts(B["Qh"][:], bG[:], -4096.0, -2048.0, AD, MX, [k("G")], [k("Q")], 512, [k("bG")])
+        for q0 in range(0, 16, 8):
+            mm([(bG[:, 0:32], sel(T.bigh, q), B["Qh"][:, q:512:16], q == 0, q == 15, 32) for q in range(q0, q0 + 8)], ["bigh", k("Q")], [k("G")], k("bG"))
+        ts(B["cu"][:, 120:152], bG[:, 0:32], 32768.0, None, AD, None, [k("G")], blocks(k, "cu", 120, 152), 32, [k("bG")])
+        ts(B["ci"][:, 120:152], bG[:, 0:32], 32768.0, None, AD, None, [k("G")], blocks(k, "ci", 120, 152), 32, [k("bG")])
+        cp(lu[:, 24:32], sm[:, 24:32], [k("m24")], [k("l15")], 8)
+
+    def order_list(h):
+        B, k = H[h], keys(h)
+        o = B["bM"][:, 128:256]
+        mm([(o, T.c128[:], T.i32[:], True, False, n), (o, T.lo[:], B["oh"][:], False, False, n), (o, T.pk[:], B["oh"][:], False, False, n),
+            (o, T.pl[:], B["oh"][:], False, True, n)], ["c128", "i32", "lo", "pk", "pl", k("oh")], [k("rf")], k("bM"))
+        ts(B["ru"][:], o, 0.5, col[:, 10:11], MU, AD, [k("rf"), "c10"], [k("ru")], n, [k("bM")])
 
     def corr(t, h, j):
         cur_h[0] = h
         B, k = H[h], keys(h)
-        n, v, si, sm, lu, M, bD, bS = B["n"], B["v"], B["si"], B["sm"], B["lu"], B["M"], B["bD"], B["bS"]
-        nr, c0, a0 = n // 16, 2064 - j, 16 * n * (j - 1)
-        s, ks, U, d2 = new(B, j - 1), k("new%d" % (j - 1)), B["bM"][:, 384:384 + nr], B["em"][:, 256:256 + n]
-        if MV and j > 1:
-            mm([(U, sel(T.wbh, q), B["em"][:, 256 + q:256 + n:16], q == 0, q == 15, 8) for q in range(16)], ["wbh", k("d2")], [k("U")], k("bM"))
-            mm([(bS[:, n * c:n * c + n], T.idh[:], d2, True, True, n) for c in range(NC)], ["idh", k("d2")], [k("sP")], k("bS"))
-        else:
-            mm([(U, sel(T.wbig, q), B["pool"][:, c0 + 16 * q:2048 + 16 * n:256], q == 0, q == 15, 8) for q in range(16)], ["wbig", ks], [k("U")], k("bM"))
-            mm([(bS[:, n * c:n * c + n], T.idp[:], s, True, True, n) for c in range(NC)], ["idp", ks], [k("sP")], k("bS"))
-        cp(si[:, 8:8 + nr], U, [k("U")], [k("s8")], nr, [k("bM")])
-        if MV:
-            sc = B["bM"][:, 0:n]
-            if j > 1:
-                mm([(sc, T.idh[:], d2, True, True, n)], ["idh", k("d2")], [k("zp")], k("bM"))
-                act(s, sc, AF.Copy, [k("zp")], [ks], n, [k("bM")])
-            if j < 4:
-                act(M[:, 768:768 + n], sc if j > 1 else s, AF.Identity, [k("zp") if j > 1 else ks, "c14"], [k("sh")], n, [k("bM")] if j > 1 else (), col[:, 14:15])
-        mm([(bD[0:n, 0:128], T.c128[:, 0:n], (T.mc2 if EX else T.mc)[:], True, False, 128)], ["c128", "mc", "mc2"], [k("D")], k("bD"))
-        ts(si[:, 0:nr], si[:, 8:8 + nr], 4095, None, ALU.bitwise_and, None, [k("s8")], [k("u")], nr)
-        tt(sm[:, 0:nr], si[:, 0:nr], si[:, 0:nr], MU, [k("u")], [k("sq")], nr)
+        si, sm, lu, bD, bS = B["si"], B["sm"], B["lu"], B["bD"], B["bS"]
+        a0, l0 = 16 * n * (j - 1), 8 * (j - 1)
+        s, ks, U = new(B, t, j - 1), k("new%d" % (j - 1)), B["bM"][:, 384:392]
+        mm([(U, sel(T.wbh, q), B["sq"][:, q:n:16], q == 0, q == 15, 8) for q in range(16)], ["wbh", k("sq")], [k("U")], k("bM"))
+        mm([(bS[:, n * c:n * c + n], T.idp[:], s, True, True, n) for c in range(4)], ["idp", ks], [k("sP")], k("bS"))
+        ts(si[:, 8:16], U, col[:, 9:10], None, SU, None, [k("U"), "c9"], [k("s8")], nr, [k("bM")])
+        Dm = lambda m: bD[:, 15 - m:128:16]
+        mm([(bD[:, 0:128], T.c128[:], T.mc2[:], True, False, 128), (Dm(15), B["oh"][:], T.dd[:, l0:l0 + 8], False, False, 8)],
+           ["c128", "mc2", "dd", k("oh")], [k("D")], k("bD"))
+        ts(si[:, 0:8], si[:, 8:16], 4095, None, AND, None, [k("s8")], [k("u")], nr)
+        tt(sm[:, 0:8], si[:, 0:8], si[:, 0:8], MU, [k("u")], [k("uu")], nr)
         b1 = T.kj[:, j - 1:j] if t == 0 else T.b1[:, 4 * t + j - 1:4 * t + j]
-        ts(si[:, 16:16 + nr], sm[:, 0:nr], b1, 2.0 ** -5, AD, MU, [k("sq"), "b1%d" % t], [k("base")], nr)
-        for x, (e0, e1) in zip(("", "x"), ((nr * IX, n), (0, nr * IX)) if IX else ((0, n),)):
-            rp, f0 = T.rl[:, 8 + 8 * v:8 + 8 * v + (e1 - e0) // 16], max(e0, nr)
-            tg(B["p1"][:, e0:e1], si[:, 0:nr], rp, T.kr[:, 128 * v + e0:128 * v + e1], MU, [k("u"), "rp%d" % v, "kr%d" % v], [k("p1" + x)], e1 - e0)
-            tg(B["p2"][:, e0:e1], si[:, 16:16 + nr], rp, B["p1"][:, e0:e1], AD, [k("base"), "rp%d" % v, k("p1" + x)], [k("p2" + x)], e1 - e0)
-            ts(B["ci"][:, 128 * j + f0:128 * j + e1], B["p2"][:, f0:e1], 4095, None, ALU.bitwise_and, None, [k("p2" + x)], [k("cj%d" % j + x)], e1 - f0)
-            cp(B["cu"][:, 128 * j - 128 + f0:128 * j - 128 + e1], B["ci"][:, 128 * j + f0:128 * j + e1], [k("cj%d" % j + x)], [k("cu%d" % j + x)], e1 - f0)
-        if j == 1:
-            place(B, k, 0, B["ci"][:, 0:nr], T.rl[:, 0:nr], "rl")
-        else:
-            place(B, k, j - 1, B["ci"][:, 128 * j - 128:128 * j - 128 + n], lu[:, 24 + 16 * j:24 + 16 * j + nr], k("lc%d" % (j - 1)))
+        ts(si[:, 16:24], sm[:, 0:8], b1, 2.0 ** -5, AD, MU, [k("uu"), "b1%d" % t], [k("base")], nr)
+        for x, (e0, e1) in zip("xy", ((0, nr * IX), (nr * IX, n)) if IX else ((0, n),)):
+            rp, f1 = T.rl[:, 8:8 + (e1 - e0) // 16], min(e1, n - nr)
+            tg(B["p1"][:, e0:e1], si[:, 0:8], rp, T.kr[:, e0:e1], MU, [k("u"), "rp", "kr"], [k("p1" + x)], e1 - e0)
+            tg(B["p2"][:, e0:e1], si[:, 16:24], rp, B["p1"][:, e0:e1], AD, [k("base"), "rp", k("p1" + x)], [k("p2" + x)], e1 - e0)
+            ts(B["ci"][:, l0 + e0:l0 + f1], B["p2"][:, e0:f1], 4095, None, AND, None, [k("p2" + x)], blocks(k, "ci", l0 + e0, l0 + f1), f1 - e0)
+            cp(B["cu"][:, l0 + e0:l0 + f1], B["ci"][:, l0 + e0:l0 + f1], blocks(k, "ci", l0 + e0, l0 + f1), blocks(k, "cu", l0 + e0, l0 + f1), f1 - e0)
+        if j == 2:
+            order_list(h)
         ka = lambda m: k("a%d%d" % (j, sum(1 for c in CH[1:] if c <= m)))
         am = lambda m: B["aw"][:, a0 + n * m:a0 + n * m + n]
         mnm = lambda m: B["mn"][:, n * m:n * m + n]
-        Dm = lambda m: bD[0:n, m:128:16]
-        mv = 16 - NS
-        cuts = sorted(set(x for x in VB + CH + (mv,) if x <= mv))
-        for c0_, c1 in list(zip(CH, CH[1:]))[::-1]:
-            ag(B["aw"][:, a0 + n * c0_:a0 + n * c1], X[:, 0:4096], B["cu"][:, 128 * j - 128 + nr * c0_:128 * j - 128 + nr * c1],
-               XK + [k("cu%d" % j)] + ([k("cu%dx" % j)] if c0_ < IX else []) + ([k("cz%d" % j)] if c0_ == 0 else []), [ka(c0_)], n * (c1 - c0_))
-            if c1 == 16 and NS:
+        cuts = sorted(set(x for x in VB + (NS,) if x >= NS))
+        for c0, c1 in zip(CH, CH[1:]):
+            ag(B["aw"][:, a0 + n * c0:a0 + n * c1], X[:, 0:4096], B["cu"][:, l0 + nr * c0:l0 + nr * c1],
+               XK + blocks(k, "cu", l0 + nr * c0, l0 + nr * c1), [ka(c0)], n * (c1 - c0))
+            if c0 < NS <= c1:
                 lst = []
-                for m in range(mv, 16):
-                    o = B["bG"][:, n * (m - mv):n * (m - mv + 1)]
+                for m in range(NS):
+                    o = B["bG"][:, n * m:n * m + n]
                     lst += [(o, T.idp[:], am(m), True, False, n), (o, T.idn[:], s, False, True, n)]
-                mm(lst, ["idp", "idn", ka(15), ks], [k("G")], k("bG"))
-                act(B["mn"][:, n * mv:16 * n], B["bG"][:, 0:n * NS], AF.Relu, [k("G")], [k("mn%d" % m) for m in range(mv, 16)], n * NS, [k("bG")])
-            mm([(Dm(m), am(m), T.bo8[:, 24:32] if m >= mv else T.bo8[:, 0:8], False, False, 8) for m in range(c0_, c1)], [ka(c0_), "bo0", "bo3"], [k("D")], k("bD"))
-            if c0_ == 0 and NS:
-                mm([(Dm(m), mnm(m), T.bo8[:, 16:24], False, False, 8) for m in range(mv, 16)], [k("mn%d" % m) for m in range(mv, 16)] + ["bo2"], [k("D")], k("bD"))
-            for m0, m1 in list(zip(cuts, cuts[1:]))[::-1]:
-                if c0_ <= m0 < c1:
+                mm(lst, ["idp", "idn", ks] + [ka(m) for m in range(NS)], [k("G")], k("bG"))
+                act(B["mn"][:, 0:n * NS], B["bG"][:, 0:n * NS], AF.Relu, [k("G")], [k("mn%d" % m) for m in range(NS)], n * NS, [k("bG")])
+            mm([(Dm(m), am(m), T.bo8[:, 24:32] if m < NS else T.bo8[:, 0:8], False, False, 8) for m in range(c0, c1)], [ka(c0), "bo0", "bo3"], [k("D")], k("bD"))
+            if c1 == 16 and NS:
+                mm([(Dm(m), mnm(m), T.bo8[:, 16:24], False, False, 8) for m in range(NS)], [k("mn%d" % m) for m in range(NS)] + ["bo2"], [k("D")], k("bD"))
+            for m0, m1 in zip(cuts, cuts[1:]):
+                if c0 < m1 <= c1:
                     kk = [k("mn%d" % m) for m in range(m0, m1)]
-                    tt(B["mn"][:, n * m0:n * m1], B["aw"][:, a0 + n * m0:a0 + n * m1], bS[:, 0:n * (m1 - m0)], ALU.min, [ka(m0), k("sP")], kk, n * (m1 - m0), [k("bS")])
-                    mm([(Dm(m), mnm(m), T.bo8[:, 8:16], False, m0 == 0 and m == m1 - 1, 8) for m in range(m0, m1)], kk + ["bo1"], [k("D")], k("bD"))
-        if j == 4:
-            Y = B["bG"][:, 128:128 + n]
-            mm([(Y, T.shf[:], M[:, 384:384 + n], True, False, n)], ["shf", k("L")], [k("G")], k("bG"), True)
-            mm([(Y, T.idf[:], M[:, 256:256 + n], False, False, n)], ["idf", k("K")], [k("G")], k("bG"), True)
-            for x in range(4):
-                mm([(Y, T.idf[:], B["pl"][:, 128 * x:128 * x + n], False, x == 3, n)], ["idf", k("pl%d" % x)], [k("G")], k("bG"), True)
-            act(M[:, 512:512 + n], Y, AF.Copy, [k("G")], [k("Yp")], n, [k("bG")])
-        cv = bD[:, 128:144]
-        if EX:
-            scan(B, k)
-            mm([(cv, T.idp[:], T.cc[:], True, False, 16), (cv, T.c128[:], T.ce[:, 16 * v:16 * v + 16], False, False, 16)],
-               ["idp", "cc0", "cc1", "c128", "ce%d0" % v, "ce%d1" % v], [k("cv")], k("bD"))
-            ts(sm[0:n, 32:40], B["run"][0:n, 15::16], 16 * MAGIC, 16 * MAGIC, AD, ALU.subtract, [k("run")], [k("m32")], 8)
-            tt(B["fb"][0:n, 15:143:16], B["run"][0:n, 15::16], sm[0:n, 32:40], ALU.subtract, [k("run"), k("m32")], [k("fb")], 8)
-            mm([(cv, sel(B["fb"], q, n), T.idc[0:n, 256 * v + q:256 * v + 256:16], False, q == 15, 16) for q in range(16)],
-               ["idc%d0" % v, "idc%d1" % v, k("fb")], [k("cv")], k("bD"))
-        else:
-            argmin(B, k)
-            mm([(cv, T.idp[:], T.cc[:], True, False, 16), (cv, B["ex"][0:n, :], T.rc[0:n, 16 * v:16 * v + 16], False, True, 16)],
-               ["idp", "cc0", "cc1", "rc%d0" % v, "rc%d1" % v, k("ex")], [k("cv")], k("bD"))
-        cp(lu[:, 32 + 16 * j:48 + 16 * j], cv, [k("cv")], [k("lc%d" % j)], 16, [k("bD")])
-        win, lst, kk = B["aw"][:, a0:a0 + 16 * n], lu[:, 32 + 16 * j:32 + 16 * j + nr], [ka(m) for m in CH[:-1]] + [k("lc%d" % j)]
-        if MV and j < 4:
-            tg(M[:, 896:896 + n], win, lst, M[:, 768:768 + n], AD, kk + [k("sh")], [k("tp")], n)
-            ts(d2, M[:, 896:896 + n], 2 * MAGIC, 2 * MAGIC, AD, ALU.subtract, [k("tp")], [k("d2")], n)
-            return
-        ag(B["xe"][:, 0:n], win, lst, kk, [k("xe")], n)
-        middle(h, B, k, s, ks, j)
+                    tt(B["mn"][:, n * m0:n * m1], B["aw"][:, a0 + n * m0:a0 + n * m1], bS[:, 0:n * (m1 - m0)], MN,
+                       [ka(m) for m in range(m0, m1)] + [k("sP")], kk, n * (m1 - m0), [k("bS")])
+                    mm([(Dm(m), mnm(m), T.bo8[:, 8:16], False, m == 15, 8) for m in range(m0, m1)], kk + ["bo1"], [k("D")], k("bD"))
+        c0 = 192 + 5 - j
+        cv = spread(B, k, bD[:, c0:c0 + 120:5], (T.cc, T.cp, T.cq), 24, CK, k("cv%d" % j))
+        least(B, k)
+        cv[0]()
+        cv[1]()
+        cp(lu[:, 16 + 16 * j:32 + 16 * j], bD[:, c0:c0 + 80:5], [k("cv%d" % j)], [k("lc%d" % j)], 16, [k("bD")])
+        middle(B, k, t, j, B["aw"][:, a0:a0 + 16 * n], lu[:, 16 + 16 * j:24 + 16 * j], [ka(m) for m in CH[:-1]] + [k("lc%d" % j)], s, ks)
+        pick(B, k, j, B["ci"][:, l0:l0 + n], lu[:, 24 + 16 * j:32 + 16 * j], blocks(k, "ci", l0, l0 + n) + [k("lc%d" % j)])
 
     def tail(t, h):
         cur_h[0] = h
         B, par, k = H[h], t % 2, keys(h)
-        n, i0, v, lu, M, sm = B["n"], B["i0"], B["v"], B["lu"], B["M"], B["sm"]
-        nr = n // 16
-        news = [k("new%d" % j) for j in range(5)] + [k("fill%d" % h)[:-2] + "_%d" % c for c in range(13)]
-        kS, kN, w0 = "S%d%d" % (h, par), "S%d%d" % (h, 1 - par), 2048 * par
-        win = B["pool"][:, w0:w0 + 2048 + 16 * n]
-        ts(sm[:, 64:128], lu[:, 48:112], float(n), None, ALU.is_ge, None, [k("lc%d" % j) for j in range(1, 5)], [k("nz")], 64)
-        tt(sm[:, 64:128], sm[:, 64:128], B["lw"][:], MU, [k("nz"), k("lw")], [k("nz")], 64)
-        tt(sm[:, 128:160], sm[:, 64:96], sm[:, 96:128], ALU.max, [k("nz")], [k("n2")], 32)
-        tt(sm[:, 160:168], sm[:, 128:136], sm[:, 144:152], ALU.max, [k("n2")], [k("n3")], 8)
-        b4 = NP + 2 + v
-        tt(sm[:, 168:168 + nr], T.bc[:, 8 * b4:8 * b4 + nr], sm[:, 160:160 + nr], ALU.subtract, ["bc%d" % b4, k("n3")], [k("n4")], nr)
-        cp(lu[:, 128:128 + nr], sm[:, 168:168 + nr], [k("n4")], [k("lsel")], nr)
-        tg(B["aw"][:, 64 * n:65 * n], win, lu[:, 120:120 + nr], B["z"][:, 128 * t:128 * t + n], ALU.subtract, news + [kS, k("l15"), "z%d%d" % (h, t)], [k("alt")], n)
-        zs = B["zs"][:, 128 * t:128 * t + n]
-        op("A", lambda: A.activation(zs, B["aw"][:, 0:65 * n].indirect(lu[:, 128:128 + nr]), AF.Abs),
-           [k("a%d%d" % (j, c)) for j in range(1, 5) for c in range(len(CH) - 1)] + [k("alt"), k("lsel")], [k("zs%d" % t)], 70 + n * GC)
+        lu, sm, oh = B["lu"], B["sm"], B["oh"]
+        news = [k("new%d" % j) for j in range(5)] + [k("fill%d%d" % (par, c)) for c in range(11)]
+        kS, kN = "S%d%d" % (h, par), "S%d%d" % (h, 1 - par)
+        win = B["pool"][:, 4096 * par:4096 * par + 4096]
+        scan(sm[:, 48:88], B["bD"][:, 272:312], T.lc[:], MN, MX, [k("rz")] + [k("cv%d" % j) for j in range(1, 5)] + ["lc%d" % c for c in range(5)],
+             [k("rel")], 40, [k("bD")])
+        cp(lu[:, 96:104], sm[:, 52:88:5], [k("rel")], [k("lsel")], nr)
+        tg(B["aw"][:, ALT:ALT + n], win, lu[:, 24:32], B["z"][:, n * t:n * t + n], SU, news + [kS, k("l15"), "z%d%d" % (h, t)], [k("alt")], n)
+        zs = B["zs"][:, n * t:n * t + n]
+        ag(zs, B["aw"][:], lu[:, 96:104], [k("a%d%d" % (j, c)) for j in range(1, 5) for c in range(len(CH) - 1)] + [k("alt"), k("lsel")], [k("zs%d" % t)], n, AF.Abs)
         dst = T.cores[(rank + 1 + t % 3) % len(T.cores)]
         rid, pid, _ = topo.addr(dst)
         sem = "in%d" % (NP * t + h)
-        land = B["z"][:, 128 * t + 128:128 * t + 128 + n]
-        snd = op("G", lambda: g.remote_dma(land, zs, T.sem[sem], T.sem.sent, pid, rid, topo.mask(core, dst)), [k("zs%d" % t)], [], 500, sem="remote")
+        land = B["z"][:, n * t + n:n * t + 2 * n]
+        snd = op("G", lambda: g.remote_dma(land, zs, T.sem[sem], T.sem.sent, pid, rid, topo.mask(core, dst)), [k("zs%d" % t)], [], (500, 0, 0), sem="remote")
         src = T.cores[(rank - 1 - t % 3) % len(T.cores)]
-        op("N", len(topo.engines(src, core)), [], ["z%d%d" % (h, t + 1)], 0, sem=sem, after=[(snd, NET)])
+        op("N", len(topo.engines(src, core)), [], ["z%d%d" % (h, t + 1)], (0, 0, 0), sem=sem, after=[(snd, NET)])
         if t < 3:
-            ts(T.cn[:, 8 * h:8 * h + nr], sm[:, 160:160 + nr], 0.0, None, ALU.is_gt, None, [k("n3")], ["cn%d" % h], nr)
+            ts(T.cn[:, 8 * h:8 * h + 8], sm[:, 52:88:5], float(ALT), None, ALU.is_lt, None, [k("rel")], ["cn%d" % h], nr)
         nb = 4 if t == 3 else RB
-        n0, w = 4096 * (1 - par), 16 * n // nb
+        n0, w = 4096 * (1 - par) + 2048, 2048 // nb
         for c in range(nb):
-            o, lst = B["pool"][:, n0 + w * c:n0 + w * c + w], B["cu"][:, 512 + w * c // 16:512 + w * (c + 1) // 16]
-            (vg if c >= nb - (2 if t == 3 else RV[h]) else ag)(o, win, lst, news + [kS, k("ru"), kN], [k("rb%d" % c)], w)
+            o, lst = B["pool"][:, n0 + w * c:n0 + w * c + w], B["ru"][:, w * c // 16:w * (c + 1) // 16]
+            (vg if c >= nb - (RL if t == 3 else RV[h]) else ag)(o, win, lst, news + [kS, k("ru"), kN], [k("rb%d" % c)], w)
             if t == 3:
-                dma(T.so[:, 16 * i0 + w * c:16 * i0 + w * c + w], o, [k("rb%d" % c)], [], 2200 + w)
-        last_w[kN] = op("N", None, [k("rb%d" % c) for c in range(nb)], [], 0)
-        place(B, k, 4, B["ci"][:, 512:512 + n], lu[:, 104:104 + nr], k("lc4"))
-        tt(M[:, 0:n], M[:, 512:512 + n], B["pl"][:, 512:512 + n], AD, [k("Yp"), k("pl4")], [k("M")], n)
-        if t < 3:
-            act(M[:, 128:128 + n], M[:, 0:n], AF.Identity, [k("M"), "c8"], [k("M2")], n, (), col[:, 8:9])
-        else:
-            dma(T.mo[:, i0:i0 + n], M[:, 0:n], [k("M")], [], 2500)
-            dma(T.zo[:, i0:i0 + n], B["z"][:, 512:512 + n], ["z%d4" % h], [], 2500)
+                dma(T.so[:, 2048 * h + w * c:2048 * h + w * c + w], o, [k("rb%d" % c)], [], 2200 + w)
+        last_w[kN] = op("N", None, [k("rb%d" % c) for c in range(nb)], [], (0, 0, 0))
+        for x, (bk, kb) in enumerate((("bG", "G"), ("bS", "sP"))):
+            c0, o = 64 * x, lambda c: B[bk][:, c:448:7]
+            M2, o1 = B["N7"][:, 448 * x + 6:448 * x + 448:7], oh[:, 64 * x:64 * x + 64]
+            mm([(o(5), T.id16[:], M2, True, False, 64), (o(5), T.pk[:], o1, False, True, 64), (o(6), T.sh16[:], M2, True, False, 64), (o(6), T.pl[:], o1, False, True, 64)],
+               ["id16", "sh16", "pk", "pl", k("M2"), k("oh")], [k(kb)], k(bk))
+            for j in range(5):
+                mm([(o(j), T.on[:, 128 * j:128 * j + 128], o1, True, False, 64), (o(j), T.bof[:], B["P"][:, n * j + c0:n * j + c0 + 64], False, True, 256)],
+                   ["bof", "on%d" % j, k("oh"), k("P%d" % j)], [k(kb)], k(bk))
+        for x, (bk, kb) in enumerate((("bG", "G"), ("bS", "sP"))):
+            scan(B["N7"][:, 448 * x:448 * x + 448], T.rsn[:], B[bk][:, 0:448], AD, MX, ["rsn", k("G"), k("sP")], [k("M2"), k("M2%d" % x)], 448, [k(bk)])
+        if t == 3:
+            ts(B["M"][:], B["N7"][:, 6::7], 2048.0, None, AD, None, [k("M2")], [k("M")], n)
+            dma(T.mo[:, n * h:n * h + n], B["M"][:], [k("M")], [], 2500)
+            dma(T.zo[:, n * h:n * h + n], B["z"][:, 512:640], ["z%d4" % h], [], 2500)
 
     for t in range(4):
         for h in range(NP):
@@ -509,14 +439,12 @@ def build(g, core, T, topo, ops):
         for h in range(NP):
             tail(t, h)
         if t < 3:
-            cn, cni, bD, kb = T.cn, T.cni, H[-1]["bM"], "bM_%d" % (NP - 1)
-            op("V", lambda: V.tensor_reduce(cn[:, 32:33], cn[:, 0:8 * NP], AX.X, AD), ["cn%d" % h for h in range(NP)], ["cs"], vc(24))
-            cp(T.cb[:, 0:1], cn[:, 32:33], ["cs"], ["cb"], 1)
-            mm([(bD[:, 416:417], T.one[:], T.cb[:, 0:1], True, True, 1)], ["one", "cb"], ["ct"], kb)
-            cp(cni[:, 0:1], bD[:, 416:417], ["ct"], ["cni0"], 1, [kb])
-            ts(cni[:, 4:5], cni[:, 0:1], 63, None, ALU.bitwise_and, None, ["cni0"], ["cni4"], 1)
-            ts(cn[:, 36:37], cni[:, 4:5], 32.0, None, MU, None, ["cni4"], ["a32"], 1)
-            ts(T.b1[:, 4 * t + 4:4 * t + 8], T.kj[:, 0:4], cn[:, 36:37], None, AD, None, ["b10", "a32"], ["b1%d" % (t + 1)], 4)
+            cni, o, kb = T.cni, H[-1]["bM"][:, 416:417], "bM_%d" % (NP - 1)
+            mm([(o, T.one[:], T.cn[:, c:c + 1], c == 0, c == 15, 1) for c in range(16)], ["one", "cn0", "cn1"], ["ct"], kb)
+            cp(cni[:, 0:1], o, ["ct"], ["cni0"], 1, [kb])
+            ts(cni[:, 4:5], cni[:, 0:1], 2047, None, AND, None, ["cni0"], ["cni4"], 1)
+            cp(T.kj[:, 4:5], cni[:, 4:5], ["cni4", "b10"], ["a32", "kj4"], 1)
+            ts(T.b1[:, 4 * t + 4:4 * t + 8], T.kj[:, 0:4], T.kj[:, 4:5], None, AD, None, ["b10", "a32"], ["b1%d" % (t + 1)], 4)
 
 
 def lat(ops, a, b):
@@ -531,58 +459,77 @@ def lat(ops, a, b):
     return HOP
 
 
+def costs(ops, model):
+    f, gc = model
+    return [o["c"][0] + 0.83 * f * (o["c"][1] + gc * o["c"][2]) for o in ops]
+
+
+def replay(ops, bw, order, cost):
+    fin = [0.0] * len(ops)
+    free = {e: 0.0 for e in "VAPGYN"}
+    for i in order:
+        e = ops[i]["e"]
+        t0 = max([fin[d] + l for d, l in bw[i]] + [0.0 if e == "N" else free[e]])
+        fin[i] = t0 + cost[i]
+        free[e] = t0 + 60.0 if e == "Y" else fin[i]
+    return max(fin)
+
+
 def schedule(ops):
-    n = len(ops)
-    fw, bw = [[] for _ in range(n)], [[] for _ in range(n)]
+    m = len(ops)
+    fw, bw = [[] for _ in range(m)], [[] for _ in range(m)]
     for i, o in enumerate(ops):
         for d in o["deps"]:
             fw[d].append((i, lat(ops, d, i)))
             bw[i].append((d, lat(ops, d, i)))
-    pr = [0.0] * n
-    for i in range(n - 1, -1, -1):
-        pr[i] = ops[i]["cost"] + max([pr[s] + l for s, l in fw[i]], default=0.0)
-    pr = [pr[i] - BONUS * ops[i]["h"] for i in range(n)]
+    cs = [costs(ops, x) for x in MODELS]
+    cost = cs[0]
+    pr = [0.0] * m
+    for i in range(m - 1, -1, -1):
+        pr[i] = cost[i] + max([pr[s] + l for s, l in fw[i]], default=0.0)
+    pr = [pr[i] - BONUS * ops[i]["h"] for i in range(m)]
     best, x = None, SEED
     for p in range(PASSES):
-        order, fin = listed(ops, fw, pr)
-        if best is None or max(fin) <= best[1]:
-            best = (order, max(fin), fin)
+        order, fin = listed(ops, fw, pr, cost)
+        val = sum(replay(ops, bw, order, c) / sum(c) for c in cs)
+        if best is None or val <= best[1]:
+            best = (order, val, fin)
         if p >= 4:
             fin = list(best[2])
             x = (x * 1103515245 + 12345) % 2147483648
-            a = best[1] * x / 2147483648
+            a = max(fin) * x / 2147483648
             x = (x * 1103515245 + 12345) % 2147483648
             sh = SHIFT * (x / 1073741824 - 1)
-            for i in range(n):
+            for i in range(m):
                 if abs(fin[i] - a) < SPAN:
                     x = (x * 1103515245 + 12345) % 2147483648
                     fin[i] += NOISE * x / 2147483648 + sh * ops[i]["h"]
-        pr = listed(ops, bw, fin)[1] if p % 2 else [ops[i]["cost"] - fin[i] for i in range(n)]
-    return best[:2]
+        pr = listed(ops, bw, fin, cost)[1] if p % 2 else [cost[i] - fin[i] for i in range(m)]
+    return best[0], bw
 
 
 PLAN = {}
 
 
-def listed(ops, edges, pr):
-    n = len(ops)
-    left = [0] * n
-    for i in range(n):
+def listed(ops, edges, pr, cost):
+    m = len(ops)
+    left = [0] * m
+    for i in range(m):
         for s, _ in edges[i]:
             left[s] += 1
-    rdy, fin = [0.0] * n, [0.0] * n
+    rdy, fin = [0.0] * m, [0.0] * m
     free = {e: 0.0 for e in "VAPGYN"}
     cand = {e: [] for e in free}
-    for i in range(n):
+    for i in range(m):
         if not left[i]:
             cand[ops[i]["e"]].append(i)
     order = []
-    while len(order) < n:
+    while len(order) < m:
         t0, e = min((max(free[e], min(rdy[i] for i in cand[e])), e) for e in free if cand[e])
         i = max((x for x in cand[e] if rdy[x] <= t0 + LOOK), key=lambda x: (pr[x], -x))
         cand[e].remove(i)
         t0 = max(t0, rdy[i])
-        fin[i] = t0 + ops[i]["cost"]
+        fin[i] = t0 + cost[i]
         free[e] = t0 + 60.0 if e in "YN" else fin[i]
         order.append(i)
         for s, l in edges[i]:
@@ -636,6 +583,6 @@ def rank_program(g, core, T, topo):
         clock[i][s] = cnt[s]
     cores = T.cores
     r = T.rank_of(core)
-    g.wait_ge(T.sem.sent, sum(len(PARTS) * len(topo.engines(core, cores[(r + 1 + t % 3) % len(cores)])) for t in range(4)))
+    g.wait_ge(T.sem.sent, sum(NP * len(topo.engines(core, cores[(r + 1 + t % 3) % len(cores)])) for t in range(4)))
     for s in sorted(cnt):
         g.wait_ge(T.sem[s], cnt[s])

@@ -2,15 +2,21 @@ from concourse.mybir import AluOpType as ALU, ActivationFunctionType as AF, Axis
 
 NP, n, nr = 2, 128, 8
 NS = 4
-CH = (0, 4, 8, 12, 15, 16)
-VB = (0, 4, 8, 12, 16)
-IX = 4
+CH = (0, 4, 6, 10, 13, 15, 16)
+VB = (4, 6, 10, 13, 16)
+IX = 6
+CV = (4,)
+PU = 0
 GV = 2
 SH = 1
-RB, RV, RL = 8, (2, 4), 2
-BONUS, LOOK, PASSES, NOISE, SEED, SHIFT, SPAN = 2000.0, 60.0, 600, 300.0, 5, 1000.0, 6000.0
-HOP, SAME, NET = 110.0, 70.0, 3500.0
-MODELS = ((1.15, 1.55), (1.0, 1.2), (1.3, 1.9))
+RB, RV, RL = 8, (1, 1), 2
+LO = (0, 3, 1, 2, 4, 8, 5, 6, 7)
+BONUS, LOOK, PASSES, NOISE, SEED, SHIFT, SPAN = 2000.0, 60.0, 40, 300.0, 5, 1000.0, 6000.0
+WEIGH = (((1.0, 1.2, 5, 85, 32, 19, 0.8), 250.0, 110.0, 2500.0), ((1.1, 1.56, 12, 60, 64, 12, 0.8), 175.0, 155.0, 2600.0),
+         ((1.25, 1.8, 10, 100, 64, 20, 0.7), 110.0, 185.0, 3000.0))
+CYCLES, STEPS = 4, ((130, 300, 0), (150, 600, 300), (100, 300, 0), (190, 400, 200), (110, 300, 0))
+HOP, SAME, NET = 175.0, 155.0, 2600.0
+MODELS = (WEIGH[1][0],)
 MAGIC = 12582912.0
 ALT = 64 * n
 BF, F32, I32, U16, F16 = "bfloat16", "float32", "int32", "uint16", "float16"
@@ -22,11 +28,11 @@ for _n, _w, _d in [("xb", 144, BF), ("db", 128, BF), ("mc", 128, BF), ("mc2", 12
                    ("one", 128, BF), ("kr", 128, F32), ("rl", 16, U16), ("rs", 8, BF), ("ib", 8, F32), ("hc", 512, BF), ("cc", 384, BF),
                    ("hp", 32, BF), ("hq", 32, BF), ("cp", 32, BF), ("cq", 32, BF), ("on", 640, BF), ("pk", 128, BF), ("pl", 128, BF),
                    ("lo", 128, BF), ("dd", 32, BF), ("i32", 128, BF), ("zv", 128, BF), ("rsn", 448, BF), ("lc", 40, F32), ("kj", 8, F32), ("b1", 16, F32),
-                   ("cn", 16, BF), ("cni", 16, I32), ("bc", 24, F32)]:
+                   ("cn", 16, BF), ("cni", 16, I32), ("bc", 16, F32), ("cnt", 2048, F32)]:
     SCRATCH[_n] = ("sbuf", [128, _w], _d)
 PER = [("pool", 8192, BF), ("aw", 65 * n, BF), ("mn", 2048, BF), ("z", 640, BF), ("zs", 512, BF), ("run", 128, F32), ("si", 64, I32),
        ("lu", 112, U16), ("sm", 96, F32), ("p1", 128, F32), ("p2", 128, I32), ("ci", 152, I32), ("cu", 152, U16), ("ru", 128, U16),
-       ("nn", 8, I32), ("P", 640, F32), ("Qh", 512, F16), ("N7", 896, F16), ("oh", 128, BF), ("sq", 128, F16), ("tp", 128, F16),
+       ("P", 640, F32), ("Qh", 512, F16), ("N7", 896, F16), ("oh", 128, BF), ("sq", 128, F16), ("tp", 128, F16),
        ("sh", 128, F32), ("fb", 144, BF), ("M", 128, F32)]
 for _h in "01":
     for _n, _w, _d in PER:
@@ -41,7 +47,7 @@ def build(g, core, T, topo, ops):
     rank = T.rank_of(core)
     V, A, P = g.vector, g.scalar, g.tensor
     last_w, readers, bank = {}, {}, {}
-    cur_h = [0]
+    cur_h = [0, "start", 0]
 
     def op(e, fn, r, w, cost, banks=(), sem=None, after=()):
         i = len(ops)
@@ -69,7 +75,8 @@ def build(g, core, T, topo, ops):
         for x, lat_ in after:
             deps[x] = lat_
         deps.pop(i, None)
-        ops.append({"e": e, "fn": fn, "deps": deps, "c": cost, "sem": sem, "h": cur_h[0]})
+        cur_h[2] += 1
+        ops.append({"e": e, "fn": fn, "deps": deps, "c": cost, "sem": sem, "h": cur_h[0], "k": (cur_h[1], cur_h[2])})
         return i
 
     def ts(out, in0, s1, s2, o0, o1, r, w, c, banks=()):
@@ -130,15 +137,16 @@ def build(g, core, T, topo, ops):
     def states(B, par):
         return B["pool"][:, 4096 * par + 2048:4096 * par + 4096]
 
-    for h, B in enumerate(H):
-        dma(B["z"][:, 0:n], T.arr[:, n * h:n * h + n], [], ["z%d0" % h], 2200)
-        dma(states(B, 0), T.st[:, 2048 * h:2048 * h + 2048], [], ["S%d0" % h], 3500 + 1300 * h)
-        if h == 0:
-            dma(T.wk[:, 0:1], T.wt[:], [], ["wk0"], 2200)
-            dma(T.wk[:, 8:9], T.kap[:], [], ["wk8"], 2200)
-            dma(T.nmi[:], T.nm[:], [], ["nmi"], 4500)
-    for h in range(NP):
-        dma(X[:, 2048 * h:2048 * h + 2048], T.rec[:, 2048 * h:2048 * h + 2048], [], ["X%d" % h], 7500 + 1300 * h)
+    loads = [(H[0]["z"][:, 0:n], T.arr[:, 0:n], "z00", 32), (T.wk[:, 0:1], T.wt[:], "wk0", 8), (T.wk[:, 8:9], T.kap[:], "wk8", 8),
+             (states(H[0], 0), T.st[:, 0:2048], "S00", 512), (H[1]["z"][:, 0:n], T.arr[:, n:2 * n], "z10", 32),
+             (X[:, 0:2048], T.rec[:, 0:2048], "X0", 512), (X[:, 2048:4096], T.rec[:, 2048:4096], "X1", 512),
+             (T.nmi[:], T.nm[:], "nmi", 128), (states(H[1], 0), T.st[:, 2048:4096], "S10", 512)]
+    for x in range(len(loads)):
+        o, i, kk, _ = loads[LO[x]]
+        c = 2000 + 3 * sum(loads[y][3] for y in LO[:x + 1])
+        d = dma(o, i, [], [kk], c)
+        if x:
+            ops[d]["deps"][d - 1] = 60.0 - ops[d - 1]["c"][0]
 
     lowb, upb = ([[16, 8], [0, 16]], 15, -1), ([[-16, 8], [0, 16]], 0, 1)
     io(col[:, 0:1], [[0, 1]], 0, 1, ["c0"], 1)
@@ -174,7 +182,6 @@ def build(g, core, T, topo, ops):
         act(T.bo8[:, 8 * b:8 * b + 8], T.rs[:], AF.Copy, ["rs"], ["bo%d" % b], 8, scale=s)
     ts(T.dm[:], T.mc[:], col[:, 1:2], None, EQ, None, ["mc", "c1"], ["dm"], 64)
     ms(T.c128[:], 2.0 ** -7, ["c128"], 64)
-    cp(T.rl[:, 0:8], T.xb[:, 0:8], ["xb"], ["rl"], 8)
     ts(T.pi[:, 24:32], T.pi[:, 8:16], nr - 1, None, AND, None, ["pi0"], ["pi24"], 8)
     cp(T.rl[:, 8:16], T.pi[:, 24:32], ["pi24"], ["rp"], 8)
     ib = T.ib[:, 0:8]
@@ -191,7 +198,7 @@ def build(g, core, T, topo, ops):
         act(T.cp[:, 8 * b:8 * b + 8], T.xb[:, 0:8] if b == 1 else ib, AF.Copy, ["ib", "xb"], ["cp%d" % b], 8)
         io(T.cq[:, 8 * b:8 * b + 8], [[0, 8]], int((-6.5 if b == 2 else 7.5) * s), 0, ["cq%d" % b], 8)
     CK = ["c%s%d" % (x, b) for x in "cpq" for b in range(3)]
-    for b, a in enumerate((0.0, 16.0 * n, 2063.0)):
+    for b, a in enumerate((0.0, 2063.0)):
         act(T.bc[:, 8 * b:8 * b + 8], ib, AF.Copy, ["ib"], ["bc%d" % b], 8, bias=a, scale=16.0)
     for c in range(5):
         act(T.lc[:, c:40:5], ib, AF.Copy, ["ib"], ["lc%d" % c], 8, bias=float(16 * n * (4 - c) + 15 * n if c else ALT))
@@ -223,8 +230,10 @@ def build(g, core, T, topo, ops):
     ts(T.kj[:, 0:4], T.kj[:, 4:8], T.kr[:, 120:121], -262156.0, MU, AD, ["kj4", "kr"], ["b10"], 4)
     for h, B in enumerate(H):
         io(B["fb"][:], [[0, 144]], 0, 0, ["fb_%d" % h], 144)
-        ts(B["N7"][:, 6::7], T.nmi[:, n * h:n * h + n], -2048.0, None, AD, None, ["nmi"], ["M2_%d" % h], n)
+        ts(B["N7"][:, 6::7], T.nmi[:, n * h:n * h + n], -2048.0, None, AD, None, ["nmi"], ["M20_%d" % h, "M21_%d" % h], n)
         ms(B["bD"][:, 272:312:5], 0.0, ["rz_%d" % h], 16, ["bD_%d" % h])
+    for x in range(4):
+        io(T.cnt[:, 512 * x:512 * x + 512], [[1, 512]], 512 * x, 0, ["cnt"], 512)
     io(T.one[:], [[0, 128]], 32, 0, ["one"], 128)
     io(T.rsn[:], [[0, 448]], 0, 0, ["rsn"], 448)
     io(T.rsn[:, 0:448:7], [[0, 64]], -16384, 0, ["rsn"], 64)
@@ -268,20 +277,35 @@ def build(g, core, T, topo, ops):
     def pick(B, k, j, win, lst, kk):
         tg(B["P"][:, n * j:n * j + n], win, lst, T.dm[:], MU, kk + ["dm"], [k("P%d" % j)], n)
 
+    BIDS = (("bM", "zp"), ("bG", "G"))
+
+    def bid(B, k, x, j):
+        (bk, kb), o1 = BIDS[x], B["oh"][:, 64 * x:64 * x + 64]
+        o = lambda c: B[bk][:, c:448:7]
+        if j == 5:
+            M2 = B["N7"][:, 448 * x + 6:448 * x + 448:7]
+            mm([(o(5), T.id16[:], M2, True, False, 64), (o(5), T.pk[:], o1, False, True, 64), (o(6), T.sh16[:], M2, True, False, 64), (o(6), T.pl[:], o1, False, True, 64)],
+               ["id16", "sh16", "pk", "pl", k("M2%d" % x), k("oh")], [k(kb)], k(bk))
+        else:
+            mm([(o(j), T.on[:, 128 * j:128 * j + 128], o1, True, False, 64), (o(j), T.bof[:], B["P"][:, n * j + 64 * x:n * j + 64 * x + 64], False, True, 256)],
+               ["bof", "on%d" % j, k("oh"), k("P%d" % j)], [k(kb)], k(bk))
+
     def head(t, h):
-        cur_h[0] = h
+        cur_h[:] = [h, "head%d" % h, 0]
         B, par, k = H[h], t % 2, keys(h)
         si, sm, lu, bD, bM, bG, oh = B["si"], B["sm"], B["lu"], B["bD"], B["bM"], B["bG"], B["oh"][:]
         z, kz, kS = B["z"][:, n * t:n * t + n], "z%d%d" % (h, t), "S%d%d" % (h, par)
         s0 = 4096 * par + 2048
         row = lambda m: B["pool"][:, s0 + m:s0 + 2048:16]
-        mm([(bM[:, 400:408], sel(T.big, q), B["z"][:, n * t + q:n * t + n:16], q == 0, q == 15, 8) for q in range(16)], ["big", kz], [k("sz")], k("bM"))
-        cp(si[:, 32:40], bM[:, 400:408], [k("sz")], [k("s32")], nr, [k("bM")])
+        sz = bM[:, 456:464]
+        mm([(sz, sel(T.big, q), B["z"][:, n * t + q:n * t + n:16], q == 0, q == 15, 8) for q in range(16)], ["big", kz], [k("sz")], k("bM"))
+        cp(si[:, 32:40], sz, [k("sz")], [k("s32")], nr, [k("bM")])
         ts(si[:, 40:48], si[:, 32:40], 15, None, AND, None, [k("s32")], [k("s40")], nr)
-        tt(B["nn"][:], si[:, 40:48], T.bc[:, 8 * h:8 * h + 8], AD, [k("s40"), "bc%d" % h], [k("nn")], nr)
-        ts(lu[:, 16:24], B["nn"][:], -2048.0 * h, None, AD, None, [k("nn")], [k("ln")], nr)
+        tt(sm[:, 88:96], si[:, 40:48], T.bc[:, 0:8], AD, [k("s40"), "bc0"], [k("nn")], nr)
+        cp(lu[:, 16:24], sm[:, 88:96], [k("nn")], [k("ln")], nr)
         op("V", lambda: V.tensor_copy(X[:, 2048 * h:2048 * h + 2048].indirect(lu[:, 16:24]), z), [k("ln"), kz], ["X%d" % h], (55, 4 * n, 0))
-        pick(B, k, 0, B["nn"][:], T.rl[:, 0:8], [k("nn"), "rl"])
+        op("A", lambda: A.activation(B["P"][:, 0:n], T.cnt[:].indirect(lu[:, 16:24]), AF.Copy, bias=128.0 * h, scale=0.0625),
+           [k("ln"), "cnt"], [k("P0")], (70, 0, n))
         if SH:
             act(B["sh"][:], z, AF.Identity, [kz, "c11"], [k("sh")], n, (), col[:, 11:12])
         rows = lambda c: B["pool"][:, s0 + c:s0 + 2048:4]
@@ -289,7 +313,7 @@ def build(g, core, T, topo, ops):
         mm([(bD[:, 0:128], T.c128[:], T.mc2[:], True, False, 128)]
            + [(bD[:, m:128:16], row(m), T.bo8[:, 0:8], False, False, 8) for m in range(16) if m % 4 < GV], ["c128", "mc2", kS, "bo0"], [k("D")], k("bD"))
         for c in range(GV, 4):
-            bk, kb = ("bG", k("G")) if c % 2 else ("bS", k("sP"))
+            bk, kb = ("bM", k("zp")) if c == 2 and not GV else ("bG", k("G")) if c % 2 else ("bS", k("sP"))
             mm([(B[bk][:], T.idp[:], rows(c), True, False, 512)], ["idp", kS], [kb], k(bk))
             mm([(B[bk][:, x:512:4], T.idn[:], z, False, x == 3, n) for x in range(4)], ["idn", kz], [kb], k(bk))
             act(mnc(c)[0], B[bk][:], AF.Abs, [kb], mnc(c)[1], 512, [k(bk)])
@@ -306,7 +330,7 @@ def build(g, core, T, topo, ops):
         cv[0]()
         cv[1]()
         cp(lu[:, 0:16], bD[:, 128:144], [k("cv")], [k("lg")], 16, [k("bD")])
-        tt(sm[:, 16:24], bD[:, 152:160], T.bc[:, 16:24], MN, [k("cv"), "bc2"], [k("m16")], 8, [k("bD")])
+        tt(sm[:, 16:24], bD[:, 152:160], T.bc[:, 8:16], MN, [k("cv"), "bc1"], [k("m16")], 8, [k("bD")])
         tt(sm[:, 24:32], bD[:, 144:152], sm[:, 16:24], MX, [k("cv"), k("m16")], [k("m24")], 8, [k("bD")])
         middle(B, k, t, 0, states(B, par), lu[:, 0:8], [kS, k("lg")], z, kz)
         ag(oh, T.dm[:, 0:16], lu[:, 8:16], ["dm", k("lg")], [k("oh")], n)
@@ -314,30 +338,29 @@ def build(g, core, T, topo, ops):
         for j in range(1, 5):
             o = bG[:, n * j - n:n * j]
             lst += [(o, T.id16[:], B["N7"][:, 6::7], True, False, n), (o, T.on[:, 128 * j:128 * j + 128], oh, False, True, n)]
-        mm(lst, ["id16", k("M2"), k("oh")] + ["on%d" % j for j in range(1, 5)], [k("G")], k("bG"))
+        mm(lst, ["id16", k("M20"), k("M21"), k("oh")] + ["on%d" % j for j in range(1, 5)], [k("G")], k("bG"))
         ts(B["Qh"][:], bG[:], -4096.0, -2048.0, AD, MX, [k("G")], [k("Q")], 512, [k("bG")])
         for q0 in range(0, 16, 8):
             mm([(bG[:, 0:32], sel(T.bigh, q), B["Qh"][:, q:512:16], q == 0, q == 15, 32) for q in range(q0, q0 + 8)], ["bigh", k("Q")], [k("G")], k("bG"))
         ts(B["cu"][:, 120:152], bG[:, 0:32], 32768.0, None, AD, None, [k("G")], blocks(k, "cu", 120, 152), 32, [k("bG")])
         ts(B["ci"][:, 120:152], bG[:, 0:32], 32768.0, None, AD, None, [k("G")], blocks(k, "ci", 120, 152), 32, [k("bG")])
         cp(lu[:, 24:32], sm[:, 24:32], [k("m24")], [k("l15")], 8)
-
-    def order_list(h):
-        B, k = H[h], keys(h)
-        o = B["bM"][:, 128:256]
-        mm([(o, T.c128[:], T.i32[:], True, False, n), (o, T.lo[:], B["oh"][:], False, False, n), (o, T.pk[:], B["oh"][:], False, False, n),
-            (o, T.pl[:], B["oh"][:], False, True, n)], ["c128", "i32", "lo", "pk", "pl", k("oh")], [k("rf")], k("bM"))
-        ts(B["ru"][:], o, 0.5, col[:, 10:11], MU, AD, [k("rf"), "c10"], [k("ru")], n, [k("bM")])
+        o = bM[:, 0:128]
+        mm([(o, T.c128[:], T.i32[:], True, False, n), (o, T.lo[:], oh, False, False, n), (o, T.pk[:], oh, False, False, n),
+            (o, T.pl[:], oh, False, True, n)], ["c128", "i32", "lo", "pk", "pl", k("oh")], [k("zp")], k("bM"))
+        ts(B["ru"][:], o, 0.5, col[:, 10:11], MU, AD, [k("zp"), "c10"], [k("ru")], n, [k("bM")])
+        bid(B, k, 0, 5)
+        bid(B, k, 0, 0)
 
     def corr(t, h, j):
-        cur_h[0] = h
+        cur_h[:] = [h, "corr%d%d" % (h, j), 0]
         B, k = H[h], keys(h)
         si, sm, lu, bD, bS = B["si"], B["sm"], B["lu"], B["bD"], B["bS"]
         a0, l0 = 16 * n * (j - 1), 8 * (j - 1)
-        s, ks, U = new(B, t, j - 1), k("new%d" % (j - 1)), B["bM"][:, 384:392]
-        mm([(U, sel(T.wbh, q), B["sq"][:, q:n:16], q == 0, q == 15, 8) for q in range(16)], ["wbh", k("sq")], [k("U")], k("bM"))
+        s, ks, U = new(B, t, j - 1), k("new%d" % (j - 1)), bD[:, 384:392]
+        mm([(U, sel(T.wbh, q), B["sq"][:, q:n:16], q == 0, q == 15, 8) for q in range(16)], ["wbh", k("sq")], [k("U")], k("bD"))
         mm([(bS[:, n * c:n * c + n], T.idp[:], s, True, True, n) for c in range(4)], ["idp", ks], [k("sP")], k("bS"))
-        ts(si[:, 8:16], U, col[:, 9:10], None, SU, None, [k("U"), "c9"], [k("s8")], nr, [k("bM")])
+        ts(si[:, 8:16], U, col[:, 9:10], None, SU, None, [k("U"), "c9"], [k("s8")], nr, [k("bD")])
         Dm = lambda m: bD[:, 15 - m:128:16]
         mm([(bD[:, 0:128], T.c128[:], T.mc2[:], True, False, 128), (Dm(15), B["oh"][:], T.dd[:, l0:l0 + 8], False, False, 8)],
            ["c128", "mc2", "dd", k("oh")], [k("D")], k("bD"))
@@ -347,18 +370,19 @@ def build(g, core, T, topo, ops):
         ts(si[:, 16:24], sm[:, 0:8], b1, 2.0 ** -5, AD, MU, [k("uu"), "b1%d" % t], [k("base")], nr)
         for x, (e0, e1) in zip("xy", ((0, nr * IX), (nr * IX, n)) if IX else ((0, n),)):
             rp, f1 = T.rl[:, 8:8 + (e1 - e0) // 16], min(e1, n - nr)
-            tg(B["p1"][:, e0:e1], si[:, 0:8], rp, T.kr[:, e0:e1], MU, [k("u"), "rp", "kr"], [k("p1" + x)], e1 - e0)
+            if not PU:
+                tg(B["p1"][:, e0:e1], si[:, 0:8], rp, T.kr[:, e0:e1], MU, [k("u"), "rp", "kr"], [k("p1" + x)], e1 - e0)
+            elif x == "x":
+                tg(B["p1"][:], si[:, 0:8], T.rl[:, 8:16], T.kr[:], MU, [k("u"), "rp", "kr"], [k("p1x"), k("p1y")], n)
             tg(B["p2"][:, e0:e1], si[:, 16:24], rp, B["p1"][:, e0:e1], AD, [k("base"), "rp", k("p1" + x)], [k("p2" + x)], e1 - e0)
             ts(B["ci"][:, l0 + e0:l0 + f1], B["p2"][:, e0:f1], 4095, None, AND, None, [k("p2" + x)], blocks(k, "ci", l0 + e0, l0 + f1), f1 - e0)
             cp(B["cu"][:, l0 + e0:l0 + f1], B["ci"][:, l0 + e0:l0 + f1], blocks(k, "ci", l0 + e0, l0 + f1), blocks(k, "cu", l0 + e0, l0 + f1), f1 - e0)
-        if j == 2:
-            order_list(h)
         ka = lambda m: k("a%d%d" % (j, sum(1 for c in CH[1:] if c <= m)))
         am = lambda m: B["aw"][:, a0 + n * m:a0 + n * m + n]
         mnm = lambda m: B["mn"][:, n * m:n * m + n]
         cuts = sorted(set(x for x in VB + (NS,) if x >= NS))
         for c0, c1 in zip(CH, CH[1:]):
-            ag(B["aw"][:, a0 + n * c0:a0 + n * c1], X[:, 0:4096], B["cu"][:, l0 + nr * c0:l0 + nr * c1],
+            (vg if c0 in CV else ag)(B["aw"][:, a0 + n * c0:a0 + n * c1], X[:, 0:4096], B["cu"][:, l0 + nr * c0:l0 + nr * c1],
                XK + blocks(k, "cu", l0 + nr * c0, l0 + nr * c1), [ka(c0)], n * (c1 - c0))
             if c0 < NS <= c1:
                 lst = []
@@ -384,9 +408,10 @@ def build(g, core, T, topo, ops):
         cp(lu[:, 16 + 16 * j:32 + 16 * j], bD[:, c0:c0 + 80:5], [k("cv%d" % j)], [k("lc%d" % j)], 16, [k("bD")])
         middle(B, k, t, j, B["aw"][:, a0:a0 + 16 * n], lu[:, 16 + 16 * j:24 + 16 * j], [ka(m) for m in CH[:-1]] + [k("lc%d" % j)], s, ks)
         pick(B, k, j, B["ci"][:, l0:l0 + n], lu[:, 24 + 16 * j:32 + 16 * j], blocks(k, "ci", l0, l0 + n) + [k("lc%d" % j)])
+        bid(B, k, 0, j)
 
     def tail(t, h):
-        cur_h[0] = h
+        cur_h[:] = [h, "tail%d%d" % (h, t == 3), 0]
         B, par, k = H[h], t % 2, keys(h)
         lu, sm, oh = B["lu"], B["sm"], B["oh"]
         news = [k("new%d" % j) for j in range(5)] + [k("fill%d%d" % (par, c)) for c in range(11)]
@@ -415,18 +440,12 @@ def build(g, core, T, topo, ops):
             if t == 3:
                 dma(T.so[:, 2048 * h + w * c:2048 * h + w * c + w], o, [k("rb%d" % c)], [], 2200 + w)
         last_w[kN] = op("N", None, [k("rb%d" % c) for c in range(nb)], [], (0, 0, 0))
-        for x, (bk, kb) in enumerate((("bG", "G"), ("bS", "sP"))):
-            c0, o = 64 * x, lambda c: B[bk][:, c:448:7]
-            M2, o1 = B["N7"][:, 448 * x + 6:448 * x + 448:7], oh[:, 64 * x:64 * x + 64]
-            mm([(o(5), T.id16[:], M2, True, False, 64), (o(5), T.pk[:], o1, False, True, 64), (o(6), T.sh16[:], M2, True, False, 64), (o(6), T.pl[:], o1, False, True, 64)],
-               ["id16", "sh16", "pk", "pl", k("M2"), k("oh")], [k(kb)], k(bk))
-            for j in range(5):
-                mm([(o(j), T.on[:, 128 * j:128 * j + 128], o1, True, False, 64), (o(j), T.bof[:], B["P"][:, n * j + c0:n * j + c0 + 64], False, True, 256)],
-                   ["bof", "on%d" % j, k("oh"), k("P%d" % j)], [k(kb)], k(bk))
-        for x, (bk, kb) in enumerate((("bG", "G"), ("bS", "sP"))):
-            scan(B["N7"][:, 448 * x:448 * x + 448], T.rsn[:], B[bk][:, 0:448], AD, MX, ["rsn", k("G"), k("sP")], [k("M2"), k("M2%d" % x)], 448, [k(bk)])
+        for j in (5, 0, 1, 2, 3, 4):
+            bid(B, k, 1, j)
+        for x, (bk, kb) in enumerate(BIDS):
+            scan(B["N7"][:, 448 * x:448 * x + 448], T.rsn[:], B[bk][:, 0:448], AD, MX, ["rsn", k(kb)], [k("M2%d" % x)], 448, [k(bk)])
         if t == 3:
-            ts(B["M"][:], B["N7"][:, 6::7], 2048.0, None, AD, None, [k("M2")], [k("M")], n)
+            ts(B["M"][:], B["N7"][:, 6::7], 2048.0, None, AD, None, [k("M20"), k("M21")], [k("M")], n)
             dma(T.mo[:, n * h:n * h + n], B["M"][:], [k("M")], [], 2500)
             dma(T.zo[:, n * h:n * h + n], B["z"][:, 512:640], ["z%d4" % h], [], 2500)
 
@@ -439,9 +458,10 @@ def build(g, core, T, topo, ops):
         for h in range(NP):
             tail(t, h)
         if t < 3:
-            cni, o, kb = T.cni, H[-1]["bM"][:, 416:417], "bM_%d" % (NP - 1)
-            mm([(o, T.one[:], T.cn[:, c:c + 1], c == 0, c == 15, 1) for c in range(16)], ["one", "cn0", "cn1"], ["ct"], kb)
-            cp(cni[:, 0:1], o, ["ct"], ["cni0"], 1, [kb])
+            cni, o, kb = T.cni, H[-1]["bM"][:, 480:488], "bM_%d" % (NP - 1)
+            mm([(o, T.one[:], T.cn[:, 8 * h:8 * h + 8], h == 0, h == NP - 1, 8) for h in range(NP)], ["one", "cn0", "cn1"], ["ct"], kb)
+            op("V", lambda: V.tensor_reduce(T.kj[:, 5:6], o, AX.X, AD), ["ct", "b10"], ["cs", "kj4"], (55, 8, 0), [kb])
+            cp(cni[:, 0:1], T.kj[:, 5:6], ["cs"], ["cni0"], 1)
             ts(cni[:, 4:5], cni[:, 0:1], 2047, None, AND, None, ["cni0"], ["cni4"], 1)
             cp(T.kj[:, 4:5], cni[:, 4:5], ["cni4", "b10"], ["a32", "kj4"], 1)
             ts(T.b1[:, 4 * t + 4:4 * t + 8], T.kj[:, 0:4], T.kj[:, 4:5], None, AD, None, ["b10", "a32"], ["b1%d" % (t + 1)], 4)
@@ -460,8 +480,17 @@ def lat(ops, a, b):
 
 
 def costs(ops, model):
-    f, gc = model
-    return [o["c"][0] + 0.83 * f * (o["c"][1] + gc * o["c"][2]) for o in ops]
+    f, gc, v0, a0, least, p0, pc = model
+    out = []
+    for o in ops:
+        e, (c0, c, x) = o["e"], o["c"]
+        if x:
+            out.append(c0 - 5 + 0.83 * f * gc * x)
+        elif e in "VA":
+            out.append((v0 if e == "V" else a0) + 0.83 * f * max(least, c))
+        else:
+            out.append(p0 + 0.83 * f * pc * c if e == "P" else c0 + 0.83 * f * c)
+    return out
 
 
 def replay(ops, bw, order, cost):
@@ -540,13 +569,234 @@ def listed(ops, edges, pr, cost):
     return order, fin
 
 
+def improve(ops, W, order, steps, seed):
+    m, K = len(ops), range(len(W))
+    en = [o["e"] for o in ops]
+    hold = [[60.0 if en[i] == "Y" else w[0][i] for i in range(m)] for w in W]
+    direct = [set(d for d, _ in W[0][1][i]) for i in range(m)]
+    order, qp, qn, z = list(order), [-1] * m, [-1] * m, [seed]
+    R, Q = [[0.0] * m for _ in K], [[0.0] * m for _ in K]
+
+    def rnd():
+        z[0] = (z[0] * 1103515245 + 12345) % 2147483648
+        return z[0] / 2147483648
+
+    def links(seg, last, nxt):
+        for i in seg:
+            if en[i] != "N":
+                j = last.get(en[i], -1)
+                qp[i], qn[i], last[en[i]] = j, nxt.get(en[i], -1), i
+                if j >= 0:
+                    qn[j] = i
+
+    def heads(seg, k):
+        r, h, (cost, bw, _) = R[k], hold[k], W[k]
+        for i in seg:
+            j = qp[i]
+            t = r[j] + h[j] if j >= 0 else 0.0
+            for d, l in bw[i]:
+                v = r[d] + cost[d] + l
+                if v > t:
+                    t = v
+            r[i] = t
+
+    def tails(seg, k):
+        q, h, (cost, _, fw) = Q[k], hold[k], W[k]
+        for i in reversed(seg):
+            j, c = qn[i], cost[i]
+            t = h[i] + q[j] if j >= 0 else c
+            if c > t:
+                t = c
+            for s, l in fw[i]:
+                v = c + l + q[s]
+                if v > t:
+                    t = v
+            q[i] = t
+
+    def length(seg, k):
+        r, q = R[k], Q[k]
+        return max(r[i] + q[i] for i in seg)
+
+    def shake(seg, iters, step, norm):
+        inw, top, before, after = set(seg), sorted(seg), {}, {}
+        for i in seg:
+            if en[i] != "N":
+                if en[i] not in before and qp[i] >= 0 and qp[i] not in inw:
+                    before[en[i]] = qp[i]
+                if qn[i] not in inw:
+                    after[en[i]] = qn[i]
+        out = [{i: max([l + Q[k][s] for s, l in W[k][2][i] if s not in inw] + [0.0]) + W[k][0][i] for i in seg} for k in K]
+        base = [{i: max([R[k][d] + W[k][0][d] + l for d, l in W[k][1][i] if d not in inw] + [0.0]) for i in seg} for k in K]
+        pre = [{i: [(d, l + W[k][0][d]) for d, l in W[k][1][i] if d in inw] for i in seg} for k in K]
+        each = [length(seg, k) for k in K]
+        best, bseg = sum(each[k] / norm[k] for k in K), seg
+        bst = [{i: R[k][i] for i in seg} for k in K]
+        late = [{i: each[k] - Q[k][i] for i in seg} for k in K]
+        for it in range(iters):
+            k = it % len(W)
+            a, sh, p, b0, pk, h = rnd() * (rnd() < 0.5), (rnd() - 0.5) * 4 * step, {}, bst[k], pre[k], hold[k]
+            c0, sp = b0[seg[int(rnd() * len(seg))]], 300.0 + 2500.0 * rnd()
+            for i in top:
+                v = b0[i]
+                if abs(v - c0) < sp:
+                    v += a * max(min(late[k][i] - v, 1500.0), 0.0) + rnd() * step + sh * ops[i]["h"]
+                for d, _ in pk[i]:
+                    if p[d] >= v:
+                        v = p[d] + 0.001
+                p[i] = v
+            st, S, F, lim = {}, {e: [] for e in after}, {e: [] for e in after}, each[k] + 150.0
+            for i in sorted(seg, key=p.get):
+                t, e = base[k][i], en[i]
+                for d, l in pk[i]:
+                    if st[d] + l > t:
+                        t = st[d] + l
+                if e != "N":
+                    s, f, c = S[e], F[e], h[i]
+                    if e in before:
+                        t = max(t, R[k][before[e]] + h[before[e]])
+                    x = len(s)
+                    while x and f[x - 1] > t:
+                        x -= 1
+                    while x < len(s) and s[x] < t + c:
+                        t = f[x]
+                        x += 1
+                    s.insert(x, t)
+                    f.insert(x, t + c)
+                st[i] = t
+                if t + out[k][i] > lim:
+                    break
+            else:
+                new = sorted(seg, key=lambda i: (st[i], i))
+                links(new, dict(before), after)
+                now = []
+                for y in K:
+                    heads(new, y)
+                    r = R[y]
+                    now.append(max(max(r[i] + out[y][i], r[i] + hold[y][i] + Q[y][qn[i]] if qn[i] >= 0 and qn[i] not in inw else 0.0) for i in new))
+                val = sum(now[y] / norm[y] for y in K)
+                if val <= best:
+                    best, bseg, each = val, new, now
+                    bst = [{i: R[y][i] for i in seg} for y in K]
+        return bseg
+
+    def swaps(seg, iters, norm):
+        inw, best, bseg, tabu = set(seg), sum(length(seg, k) / norm[k] for k in K), list(seg), {}
+        for it in range(iters):
+            k = it % len(W)
+            r, q, h, (cost, bw, fw) = R[k], Q[k], hold[k], W[k]
+            L, pick, pv = length(seg, k) - 0.01, None, 1e18
+            for u in seg:
+                v = qn[u]
+                if v >= 0 and r[u] + q[u] > L and v in inw and r[u] + h[u] + q[v] > L and u not in direct[v] and tabu.get((u, v), -1) < it:
+                    p, s2 = qp[u], qn[v]
+                    rv = max([r[d] + cost[d] + l for d, l in bw[v]] + [r[p] + h[p] if p >= 0 else 0.0])
+                    ru = max([r[d] + cost[d] + l for d, l in bw[u]] + [rv + h[v]])
+                    qu = max([cost[u] + l + q[s] for s, l in fw[u]] + [cost[u], h[u] + q[s2] if s2 >= 0 else 0.0])
+                    qv = max([cost[v] + l + q[s] for s, l in fw[v]] + [cost[v], h[v] + qu])
+                    e = max(rv + qv, ru + qu) + 20.0 * rnd()
+                    if e < pv:
+                        pick, pv = (u, v), e
+            if pick is None:
+                continue
+            u, v = pick
+            tabu[(v, u)] = it + 8 + int(8 * rnd())
+            p, s2 = qp[u], qn[v]
+            qp[v], qn[v], qp[u], qn[u] = p, u, v, s2
+            if p >= 0:
+                qn[p] = v
+            if s2 >= 0:
+                qp[s2] = u
+            iu, iv = seg.index(u), seg.index(v)
+            mid, anc = seg[iu:iv + 1], {v}
+            for y in reversed(mid[1:-1]):
+                if qn[y] in anc or any(s in anc for s, _ in fw[y]):
+                    anc.add(y)
+            seg[iu:iv + 1] = [y for y in mid if y in anc] + [y for y in mid if y not in anc]
+            for y in K:
+                heads(seg[iu:], y)
+                tails(seg[:iv + 1], y)
+            val = sum(length(seg, y) / norm[y] for y in K)
+            if val < best - 1e-7:
+                best, bseg = val, list(seg)
+        return bseg
+
+    norm = None
+    for width, iters, step, a0, a1 in steps:
+        a = a0 - int(width * rnd())
+        while a < a1:
+            lo, hi = max(a, 0), min(a + width, m)
+            a += width
+            if hi > lo:
+                links(order, {}, {})
+                for k in K:
+                    heads(order, k)
+                    tails(order, k)
+                norm = norm or [length(order, k) for k in K]
+                order[lo:hi] = shake(order[lo:hi], iters, step, norm) if step else swaps(order[lo:hi], iters, norm)
+    return order
+
+
+def repeat(ops, order, cost, bw):
+    st, free, mem = [0.0] * len(ops), {e: 0.0 for e in "VAPGYN"}, {}
+    for i in order:
+        e = ops[i]["e"]
+        st[i] = max([st[d] + cost[d] + l for d, l in bw[i]] + [0.0 if e == "N" else free[e]])
+        free[e] = st[i] + (60.0 if e == "Y" else cost[i])
+    for i, o in enumerate(ops):
+        mem.setdefault(o["k"], []).append(i)
+    ref = mem[("corr02", 1)]
+    span, p = st[ref[2]] - st[ref[1]], list(st)
+    for l in mem.values():
+        if len(l) >= 3:
+            x = 1 if st[l[1]] >= st[ref[1]] else 2
+            for y, i in enumerate(l):
+                p[i] = st[l[x]] + (y - x) * span
+    first, last = p[ref[0]] - st[ref[0]], p[ref[3]] - st[ref[3]]
+    for i, o in enumerate(ops):
+        if len(mem[o["k"]]) < 3:
+            p[i] = st[i] + (last if o["k"][0][0] == "t" else first)
+        elif st[i] < st[ref[0]]:
+            p[i] = st[i] + first
+        elif st[i] > st[mem[("corr04", 1)][3]]:
+            p[i] = st[i] + last
+    for i in range(len(ops)):
+        for d, _ in bw[i]:
+            if p[d] >= p[i]:
+                p[i] = p[d] + 0.001
+    return sorted(range(len(ops)), key=lambda i: (p[i], i))
+
+
+def plan(ops):
+    order, bw0 = schedule(ops)
+    m, W = len(ops), []
+    for model, hop, same, net in WEIGH:
+        bw = [[(d, {HOP: hop, SAME: same, NET: net}.get(l, l)) for d, l in b] for b in bw0]
+        fw = [[] for _ in ops]
+        for i in range(m):
+            for d, l in bw[i]:
+                fw[d].append((i, l))
+        W.append((costs(ops, model), bw, fw))
+    ref = [i for i, o in enumerate(ops) if o["k"] == ("corr02", 1)]
+    best = None
+    for c in range(CYCLES):
+        a, b = order.index(ref[1]), order.index(ref[2])
+        order = repeat(ops, improve(ops, W, order, [x + (a, b) for x in STEPS], SEED + c), W[1][0], W[1][1])
+        val = sum(replay(ops, w[1], order, w[0]) / sum(w[0]) for w in W)
+        if best is None or val < best[0]:
+            best = (val, order)
+    order = best[1]
+    a, b = order.index(ref[0]), order.index(ref[3])
+    ends = [x + y for _ in range(2) for y in ((0, a + 50), (b, m)) for x in STEPS[:3]]
+    return improve(ops, W, order, ends + [STEPS[0] + (0, m), STEPS[2] + (0, m)], SEED)
+
+
 def rank_program(g, core, T, topo):
     if T.rank_of(core) is None:
         return
     ops = []
     build(g, core, T, topo, ops)
     if "order" not in PLAN:
-        PLAN["order"] = schedule(ops)[0]
+        PLAN["order"] = plan(ops)
     order = PLAN["order"]
     Q = {"V": g.vector, "A": g.scalar, "P": g.tensor, "G": g, "Y": g.sync}
     know = {e: {} for e in Q}
@@ -562,7 +812,7 @@ def rank_program(g, core, T, topo):
             cnt[o["sem"]] = o["fn"]
             continue
         kn = know[e]
-        need = [x for d in o["deps"] for x in join.get(d, [d]) if not (e == "P" and ops[x]["e"] == "P")]
+        need = [x for d in o["deps"] for x in join.get(d, [d]) if not (e == "P" and ops[x]["e"] == "P") and o["deps"][d] >= 0]
         for d in sorted(need, key=lambda d: -mark[d][1]):
             s, v = mark[d]
             if kn.get(s, 0) < v and not any(clock[x].get(s, 0) >= v for x in need if mark[x][0] != s):

from concourse.mybir import AluOpType as ALU, ActivationFunctionType as AF, AxisListType as AX

NP, n, nr = 2, 128, 8
NS = 4
CH = (0, 4, 6, 10, 13, 15, 16)
VB = (4, 6, 10, 13, 16)
IX = 6
CV = (4,)
PU = 0
GV = 2
SH = 1
RB, RV, RL = 8, (1, 1), 2
LO = (0, 3, 1, 2, 4, 8, 5, 6, 7)
BONUS, LOOK, PASSES, NOISE, SEED, SHIFT, SPAN = 2000.0, 60.0, 40, 300.0, 5, 1000.0, 6000.0
WEIGH = (((1.0, 1.2, 5, 85, 32, 19, 0.8), 250.0, 110.0, 2500.0), ((1.1, 1.56, 12, 60, 64, 12, 0.8), 175.0, 155.0, 2600.0),
         ((1.25, 1.8, 10, 100, 64, 20, 0.7), 110.0, 185.0, 3000.0))
CYCLES, STEPS = 4, ((130, 300, 0), (150, 600, 300), (100, 300, 0), (190, 400, 200), (110, 300, 0))
HOP, SAME, NET = 175.0, 155.0, 2600.0
MODELS = (WEIGH[1][0],)
MAGIC = 12582912.0
ALT = 64 * n
BF, F32, I32, U16, F16 = "bfloat16", "float32", "int32", "uint16", "float16"

SCRATCH = {"X": ("sbuf", [128, 4096], BF), "nmi": ("sbuf", [128, 256], I32), "wk": ("sbuf", [128, 16], I32)}
for _n, _w, _d in [("xb", 144, BF), ("db", 128, BF), ("mc", 128, BF), ("mc2", 128, BF), ("xm", 128, F32), ("pi", 32, I32), ("col", 16, F32),
                   ("big", 144, BF), ("bigh", 144, F16), ("wbh", 144, F16), ("idp", 128, BF), ("idn", 128, BF), ("id16", 128, F16),
                   ("sh16", 128, F16), ("bof", 128, F32), ("bo8", 32, BF), ("dm", 128, BF), ("rst", 128, BF), ("c128", 128, BF),
                   ("one", 128, BF), ("kr", 128, F32), ("rl", 16, U16), ("rs", 8, BF), ("ib", 8, F32), ("hc", 512, BF), ("cc", 384, BF),
                   ("hp", 32, BF), ("hq", 32, BF), ("cp", 32, BF), ("cq", 32, BF), ("on", 640, BF), ("pk", 128, BF), ("pl", 128, BF),
                   ("lo", 128, BF), ("dd", 32, BF), ("i32", 128, BF), ("zv", 128, BF), ("rsn", 448, BF), ("lc", 40, F32), ("kj", 8, F32), ("b1", 16, F32),
                   ("cn", 16, BF), ("cni", 16, I32), ("bc", 16, F32), ("cnt", 2048, F32)]:
    SCRATCH[_n] = ("sbuf", [128, _w], _d)
PER = [("pool", 8192, BF), ("aw", 65 * n, BF), ("mn", 2048, BF), ("z", 640, BF), ("zs", 512, BF), ("run", 128, F32), ("si", 64, I32),
       ("lu", 112, U16), ("sm", 96, F32), ("p1", 128, F32), ("p2", 128, I32), ("ci", 152, I32), ("cu", 152, U16), ("ru", 128, U16),
       ("P", 640, F32), ("Qh", 512, F16), ("N7", 896, F16), ("oh", 128, BF), ("sq", 128, F16), ("tp", 128, F16),
       ("sh", 128, F32), ("fb", 144, BF), ("M", 128, F32)]
for _h in "01":
    for _n, _w, _d in PER:
        SCRATCH[_n + _h] = ("sbuf", [128, _w], _d)
    for _n in ("bS", "bD", "bM", "bG"):
        SCRATCH[_n + _h] = ("psum", [128, 512], F32)
SEMAPHORES = (["qV", "qA", "qP", "qG", "sent"] + ["d%d" % i for i in range(32)] + ["in%d" % i for i in range(8)])
EQ, MU, AD, SU, MX, MN, AND = ALU.is_equal, ALU.mult, ALU.add, ALU.subtract, ALU.max, ALU.min, ALU.bitwise_and


def build(g, core, T, topo, ops):
    rank = T.rank_of(core)
    V, A, P = g.vector, g.scalar, g.tensor
    last_w, readers, bank = {}, {}, {}
    cur_h = [0, "start", 0]

    def op(e, fn, r, w, cost, banks=(), sem=None, after=()):
        i = len(ops)
        deps = {}
        for k in r:
            if k in last_w:
                deps[last_w[k]] = 0.0
        for k in w:
            if k in last_w:
                deps[last_w[k]] = 0.0
            for x in readers.get(k, ()):
                deps[x] = 0.0
        for k in r:
            readers.setdefault(k, []).append(i)
        for k in w:
            last_w[k] = i
            readers[k] = []
        for b in banks:
            en, cur, prev = bank.get(b, (e, [], []))
            if en != e:
                cur, prev = [], cur
            for x in prev + (cur[-1:] if e == "P" else []):
                deps[x] = 0.0
            bank[b] = (e, cur + [i], prev)
        for x, lat_ in after:
            deps[x] = lat_
        deps.pop(i, None)
        cur_h[2] += 1
        ops.append({"e": e, "fn": fn, "deps": deps, "c": cost, "sem": sem, "h": cur_h[0], "k": (cur_h[1], cur_h[2])})
        return i

    def ts(out, in0, s1, s2, o0, o1, r, w, c, banks=()):
        if o1 is None:
            return op("V", lambda: V.tensor_scalar(out, in0, s1, None, o0), r, w, (55, c, 0), banks)
        return op("V", lambda: V.tensor_scalar(out, in0, s1, s2, o0, o1), r, w, (55, c, 0), banks)

    def tt(out, in0, in1, o, r, w, c, banks=()):
        return op("V", lambda: V.tensor_tensor(out, in0, in1, o), r, w, (55, c if banks else 2 * c, 0), banks)

    def tg(out, win, lst, in1, o, r, w, c):
        return op("V", lambda: V.tensor_tensor(out, win.indirect(lst), in1, o), r, w, (55, 0, c))

    def cp(out, in_, r, w, c, banks=()):
        return op("V", lambda: V.tensor_copy(out, in_), r, w, (55, c, 0), banks)

    def ms(out, x, w, c, banks=()):
        return op("V", lambda: V.memset(out, float(x)), [], w, (55, c / 2, 0), banks)

    def scan(out, d0, d1, o0, o1, r, w, c, banks):
        return op("V", lambda: V.tensor_tensor_scan(out, d0, d1, 0.0, o0, o1), r, w, (55, c, 0), banks)

    def ag(out, win, lst, r, w, c, f=AF.Copy):
        return op("A", lambda: A.activation(out, win.indirect(lst), f), r, w, (70, 0, c))

    def vg(out, win, lst, r, w, c):
        return op("V", lambda: V.tensor_copy(out, win.indirect(lst)), r, w, (55, 0, c))

    def act(out, in_, f, r, w, c, banks=(), bias=0.0, scale=1.0):
        return op("A", lambda: A.activation(out, in_, f, bias=bias, scale=scale), r, w, (70, c, 0), banks)

    def mm(lst, r, w, bk):
        def fn():
            for o, l, x, a, b, _ in lst:
                ins = P.matmul(o, l, x, a, b)
            return ins
        return op("P", fn, r, w, (20, sum(max(64, m[5]) for m in lst) / 2, 0), [bk])

    def io(out, pat, base, cm, w, c, flag=True):
        if flag:
            return op("G", lambda: g.iota(out, pat, base, cm, allow_small_or_imprecise_dtypes=True), [], w, (130, 2 * c, 0))
        return op("G", lambda: g.iota(out, pat, base, cm), [], w, (130, 2 * c, 0))

    def keep(out, pat, base, cm, fill, k, c):
        return op("G", lambda: g.affine_select(out, out, pat, ALU.is_ge, float(fill), base, cm), [k], [k], (170, 2 * c, 0))

    nd = [0]

    def dma(out, in_, r, w, cost):
        s = "d%d" % nd[0]
        nd[0] += 1
        return op("Y", lambda: g.sync.dma_start(out, in_), r, w, (cost, 0, 0), sem=s)

    H = [{x: T[x + str(h)] for x in [y[0] for y in PER] + ["bS", "bD", "bM", "bG"]} for h in range(NP)]
    X, col = T.X, T.col
    XK = ["X%d" % h for h in range(NP)]

    def states(B, par):
        return B["pool"][:, 4096 * par + 2048:4096 * par + 4096]

    loads = [(H[0]["z"][:, 0:n], T.arr[:, 0:n], "z00", 32), (T.wk[:, 0:1], T.wt[:], "wk0", 8), (T.wk[:, 8:9], T.kap[:], "wk8", 8),
             (states(H[0], 0), T.st[:, 0:2048], "S00", 512), (H[1]["z"][:, 0:n], T.arr[:, n:2 * n], "z10", 32),
             (X[:, 0:2048], T.rec[:, 0:2048], "X0", 512), (X[:, 2048:4096], T.rec[:, 2048:4096], "X1", 512),
             (T.nmi[:], T.nm[:], "nmi", 128), (states(H[1], 0), T.st[:, 2048:4096], "S10", 512)]
    for x in range(len(loads)):
        o, i, kk, _ = loads[LO[x]]
        c = 2000 + 3 * sum(loads[y][3] for y in LO[:x + 1])
        d = dma(o, i, [], [kk], c)
        if x:
            ops[d]["deps"][d - 1] = 60.0 - ops[d - 1]["c"][0]

    lowb, upb = ([[16, 8], [0, 16]], 15, -1), ([[-16, 8], [0, 16]], 0, 1)
    io(col[:, 0:1], [[0, 1]], 0, 1, ["c0"], 1)
    io(T.pi[:, 0:16], [[0, 16]], 0, 1, ["pi0"], 16, False)
    io(T.xb[:], [[1, 144]], 0, 0, ["xb"], 144)
    io(T.mc[:], [[0, 8], [1, 16]], 0, 0, ["mc"], 128)
    io(T.db[:], [[1, 128]], 0, -1, ["db"], 128)
    keep(T.db[:], *lowb, 99, "db", 128)
    keep(T.db[:], *upb, 99, "db", 128)
    io(T.rst[:], [[0, 128]], 0, 0, ["rst"], 128)
    io(T.rst[:, 0:128:16], [[0, 8]], 1048576, 0, ["rst"], 8)
    ts(T.pi[:, 16:17], T.pi[:, 0:1], 15, None, AND, None, ["pi0"], ["pi16"], 1)
    cp(col[:, 1:2], T.pi[:, 16:17], ["pi16"], ["c1"], 1)
    tt(col[:, 2:3], col[:, 0:1], col[:, 1:2], SU, ["c0", "c1"], ["c2"], 1)
    ts(col[:, 3:4], col[:, 2:3], 15.0, None, AD, None, ["c2"], ["c3"], 1)
    ts(col[:, 10:11], col[:, 1:2], 4096.0, None, AD, None, ["c1"], ["c10"], 1)
    ms(col[:, 11:12], 2049.5, ["c11"], 1)
    cp(col[:, 6:7], T.wk[:, 0:1], ["wk0"], ["c6"], 1)
    cp(col[:, 7:8], T.wk[:, 8:9], ["wk8"], ["c7"], 1)
    act(col[:, 8:9], col[:, 6:7], AF.Copy, ["c6"], ["c8"], 1, scale=0.5)
    x128 = T.xb[:, 0:128]
    ts(T.idp[:], x128, col[:, 0:1], None, EQ, None, ["xb", "c0"], ["idp"], 64)
    act(T.idn[:], T.idp[:], AF.Copy, ["idp"], ["idn"], 128, scale=-1.0)
    ts(T.id16[:], x128, col[:, 0:1], None, EQ, None, ["xb", "c0"], ["id16"], 64)
    ts(T.sh16[:], T.db[:], -1.0, None, EQ, None, ["db"], ["sh16"], 64)
    ts(T.bof[:], T.db[:], 50.0, None, ALU.is_lt, None, ["db"], ["bof"], 128)
    ts(T.big[:], T.xb[:], col[:, 3:4], None, EQ, None, ["xb", "c3"], ["big"], 72)
    ts(T.bigh[:], T.xb[:], col[:, 3:4], None, EQ, None, ["xb", "c3"], ["bigh"], 72)
    ts(T.wbh[:], T.xb[:], col[:, 3:4], col[:, 8:9], EQ, MU, ["xb", "c3", "c8"], ["wbh"], 72)
    ts(T.mc2[:], T.mc[:], -7.5, None, AD, None, ["mc"], ["mc2"], 64)
    ts(T.rs[:], T.xb[:, 0:128:16], col[:, 2:3], None, EQ, None, ["xb", "c2"], ["rs"], 4)
    for b, s in enumerate((16.0, -32.0, 32.0, -16.0)):
        act(T.bo8[:, 8 * b:8 * b + 8], T.rs[:], AF.Copy, ["rs"], ["bo%d" % b], 8, scale=s)
    ts(T.dm[:], T.mc[:], col[:, 1:2], None, EQ, None, ["mc", "c1"], ["dm"], 64)
    ms(T.c128[:], 2.0 ** -7, ["c128"], 64)
    ts(T.pi[:, 24:32], T.pi[:, 8:16], nr - 1, None, AND, None, ["pi0"], ["pi24"], 8)
    cp(T.rl[:, 8:16], T.pi[:, 24:32], ["pi24"], ["rp"], 8)
    ib = T.ib[:, 0:8]
    ts(ib, T.xb[:, 0:128:16], col[:, 1:2], None, AD, None, ["xb", "c1"], ["ib"], 8)
    for b, s in enumerate((1.0, 1.0, 1.0, -4096.0)):
        act(T.hc[:, 128 * b:128 * b + 128], T.idp[:], AF.Copy, ["idp"], ["hc%d" % b], 128, scale=s)
    for b, s in enumerate((16.0, 0.0, 16.0, 0.0)):
        act(T.hp[:, 8 * b:8 * b + 8], ib, AF.Copy, ["ib"], ["hp%d" % b], 8, scale=s)
    ms(T.hq[:, 0:24], 7.5, ["hq0"], 12)
    io(T.hq[:, 24:32], [[0, 8]], 14336, 0, ["hq1"], 8)
    HK = ["hc%d" % b for b in range(4)] + ["hp%d" % b for b in range(4)] + ["hq0", "hq1"]
    for b, s in enumerate((n, nr, ALT)):
        act(T.cc[:, 128 * b:128 * b + 128], T.idp[:], AF.Copy, ["idp"], ["cc%d" % b], 128, scale=-float(s))
        act(T.cp[:, 8 * b:8 * b + 8], T.xb[:, 0:8] if b == 1 else ib, AF.Copy, ["ib", "xb"], ["cp%d" % b], 8)
        io(T.cq[:, 8 * b:8 * b + 8], [[0, 8]], int((-6.5 if b == 2 else 7.5) * s), 0, ["cq%d" % b], 8)
    CK = ["c%s%d" % (x, b) for x in "cpq" for b in range(3)]
    for b, a in enumerate((0.0, 2063.0)):
        act(T.bc[:, 8 * b:8 * b + 8], ib, AF.Copy, ["ib"], ["bc%d" % b], 8, bias=a, scale=16.0)
    for c in range(5):
        act(T.lc[:, c:40:5], ib, AF.Copy, ["ib"], ["lc%d" % c], 8, bias=float(16 * n * (4 - c) + 15 * n if c else ALT))
    for j in range(5):
        ts(T.on[:, 128 * j:128 * j + 128], T.db[:], float(j), 4096.0, EQ, MU, ["db"], ["on%d" % j], 64)
    ts(T.pk[:], T.db[:], 4.0, -4096.0, ALU.is_le, MU, ["db"], ["pk"], 64)
    io(T.pl[:], [[0, 128]], -4096, 0, ["pl"], 128)
    keep(T.pl[:], [[1, 128]], 0, -1, 0, "pl", 128)
    keep(T.pl[:], *upb, 0, "pl", 128)
    io(T.lo[:], [[-32, 8], [-4, 16]], 30, 2, ["lo"], 128)
    keep(T.lo[:], [[1, 128]], 0, -1, 2, "lo", 128)
    keep(T.lo[:], [[-1, 128]], 4, 1, 0, "lo", 128)
    keep(T.lo[:], *lowb, 0, "lo", 128)
    keep(T.lo[:], *upb, 0, "lo", 128)
    io(T.i32[:], [[32, 128]], 0, 0, ["i32"], 128)
    if GV:
        ts(T.zv[:], T.bof[:], 16.0, None, MU, None, ["bof"], ["zv"], 128)
        keep(T.zv[:], [[0, 32], [-1, 4]], GV - 1, 0, 0, "zv", 128)
    io(T.dd[:], [[0, 32]], -262144, 0, ["dd"], 32)
    keep(T.dd[:], [[1, 4], [-16, 8]], -15, 1, 0, "dd", 32)
    keep(T.dd[:], [[0, 4], [16, 8]], 15, -1, 0, "dd", 32)
    io(T.xm[:], [[-1, 16], [0, nr]], 15, 0, ["xm"], 128)
    ts(T.xm[:], T.xm[:], col[:, 1:2], col[:, 7:8], EQ, MU, ["xm", "c1", "c7"], ["xm"], 128)
    mm([(T.bG1[:, 0:128], T.bof[:], T.xm[:], True, True, 512), (T.bG1[:, 128:129], T.bof[:], col[:, 6:7], True, True, 256)],
       ["bof", "xm", "c6"], ["G_1"], "bG_1")
    act(T.kr[:], T.bG1[:, 0:128], AF.Copy, ["G_1"], ["kr"], 128, ["bG_1"])
    act(col[:, 9:10], T.bG1[:, 128:129], AF.Copy, ["G_1"], ["c9"], 1, ["bG_1"], scale=1025.0)
    act(T.kj[:, 4:8], T.xb[:, 1:5], AF.Copy, ["xb"], ["kj4"], 4, scale=32.0)
    ts(T.kj[:, 0:4], T.kj[:, 4:8], T.kr[:, 120:121], -262156.0, MU, AD, ["kj4", "kr"], ["b10"], 4)
    for h, B in enumerate(H):
        io(B["fb"][:], [[0, 144]], 0, 0, ["fb_%d" % h], 144)
        ts(B["N7"][:, 6::7], T.nmi[:, n * h:n * h + n], -2048.0, None, AD, None, ["nmi"], ["M20_%d" % h, "M21_%d" % h], n)
        ms(B["bD"][:, 272:312:5], 0.0, ["rz_%d" % h], 16, ["bD_%d" % h])
    for x in range(4):
        io(T.cnt[:, 512 * x:512 * x + 512], [[1, 512]], 512 * x, 0, ["cnt"], 512)
    io(T.one[:], [[0, 128]], 32, 0, ["one"], 128)
    io(T.rsn[:], [[0, 448]], 0, 0, ["rsn"], 448)
    io(T.rsn[:, 0:448:7], [[0, 64]], -16384, 0, ["rsn"], 64)
    io(T.rsn[:, 5:448:7], [[0, 64]], -6144, 0, ["rsn"], 64)
    for par in range(2):
        for h, B in enumerate(H):
            for c in range(11):
                io(B["pool"][:, 4096 * par + c:4096 * par + 2048:16], [[0, n]], 0, 0, ["fill%d%d_%d" % (par, c, h)], n)

    def sel(tab, q):
        return tab[:, 15 - q:143 - q]

    def keys(h):
        return lambda s: s + "_%d" % h

    def blocks(k, name, a, b):
        return [k("%s%d" % (name, x)) for x in range(a // 8, b // 8)]

    def least(B, k):
        scan(B["run"][:], T.rst[:], B["bD"][:, 0:128], AD, MN, ["rst", k("D")], [k("run")], 128, [k("bD")])
        ts(B["sm"][:, 32:40], B["run"][:, 15::16], 16 * MAGIC, 16 * MAGIC, AD, SU, [k("run")], [k("m32")], 8)
        tt(B["fb"][:, 15:143:16], B["run"][:, 15::16], B["sm"][:, 32:40], SU, [k("run"), k("m32")], [k("fb")], 8)

    def spread(B, k, cv, tabs, w, kk, kw):
        return (lambda: mm([(cv, T.idp[:], tabs[1][:, 0:w], True, False, w), (cv, T.c128[:], tabs[2][:, 0:w], False, False, w)], ["idp", "c128"] + kk, [kw], k("bD")),
                lambda: mm([(cv, sel(B["fb"], q), tabs[0][:, q:16 * w:16], False, q == 15, w) for q in range(16)], kk + [k("fb")], [kw], k("bD")))

    def new(B, t, j):
        return B["pool"][:, 4096 * (t % 2) + 15 - j:4096 * (t % 2) + 2048:16]

    def middle(B, k, t, j, win, lst, kk, prev, kprev):
        if SH:
            tg(B["sq"][:], win, lst, B["sh"][:], AD, kk + [k("sh")], [k("sq")], n)
        else:
            tg(B["tp"][:], win, lst, prev, AD, kk + [kprev], [k("tp")], n)
            ts(B["sq"][:], B["tp"][:], 2049.5, None, AD, None, [k("tp")], [k("sq")], n / 2)
        ts(new(B, t, j), B["sq"][:], -2050.0, 0.5, AD, MU, [k("sq")], [k("new%d" % j)], n / 2)
        if SH and j < 4:
            act(B["sh"][:], new(B, t, j), AF.Identity, [k("new%d" % j), "c11"], [k("sh")], n, (), col[:, 11:12])

    def pick(B, k, j, win, lst, kk):
        tg(B["P"][:, n * j:n * j + n], win, lst, T.dm[:], MU, kk + ["dm"], [k("P%d" % j)], n)

    BIDS = (("bM", "zp"), ("bG", "G"))

    def bid(B, k, x, j):
        (bk, kb), o1 = BIDS[x], B["oh"][:, 64 * x:64 * x + 64]
        o = lambda c: B[bk][:, c:448:7]
        if j == 5:
            M2 = B["N7"][:, 448 * x + 6:448 * x + 448:7]
            mm([(o(5), T.id16[:], M2, True, False, 64), (o(5), T.pk[:], o1, False, True, 64), (o(6), T.sh16[:], M2, True, False, 64), (o(6), T.pl[:], o1, False, True, 64)],
               ["id16", "sh16", "pk", "pl", k("M2%d" % x), k("oh")], [k(kb)], k(bk))
        else:
            mm([(o(j), T.on[:, 128 * j:128 * j + 128], o1, True, False, 64), (o(j), T.bof[:], B["P"][:, n * j + 64 * x:n * j + 64 * x + 64], False, True, 256)],
               ["bof", "on%d" % j, k("oh"), k("P%d" % j)], [k(kb)], k(bk))

    def head(t, h):
        cur_h[:] = [h, "head%d" % h, 0]
        B, par, k = H[h], t % 2, keys(h)
        si, sm, lu, bD, bM, bG, oh = B["si"], B["sm"], B["lu"], B["bD"], B["bM"], B["bG"], B["oh"][:]
        z, kz, kS = B["z"][:, n * t:n * t + n], "z%d%d" % (h, t), "S%d%d" % (h, par)
        s0 = 4096 * par + 2048
        row = lambda m: B["pool"][:, s0 + m:s0 + 2048:16]
        sz = bM[:, 456:464]
        mm([(sz, sel(T.big, q), B["z"][:, n * t + q:n * t + n:16], q == 0, q == 15, 8) for q in range(16)], ["big", kz], [k("sz")], k("bM"))
        cp(si[:, 32:40], sz, [k("sz")], [k("s32")], nr, [k("bM")])
        ts(si[:, 40:48], si[:, 32:40], 15, None, AND, None, [k("s32")], [k("s40")], nr)
        tt(sm[:, 88:96], si[:, 40:48], T.bc[:, 0:8], AD, [k("s40"), "bc0"], [k("nn")], nr)
        cp(lu[:, 16:24], sm[:, 88:96], [k("nn")], [k("ln")], nr)
        op("V", lambda: V.tensor_copy(X[:, 2048 * h:2048 * h + 2048].indirect(lu[:, 16:24]), z), [k("ln"), kz], ["X%d" % h], (55, 4 * n, 0))
        op("A", lambda: A.activation(B["P"][:, 0:n], T.cnt[:].indirect(lu[:, 16:24]), AF.Copy, bias=128.0 * h, scale=0.0625),
           [k("ln"), "cnt"], [k("P0")], (70, 0, n))
        if SH:
            act(B["sh"][:], z, AF.Identity, [kz, "c11"], [k("sh")], n, (), col[:, 11:12])
        rows = lambda c: B["pool"][:, s0 + c:s0 + 2048:4]
        mnc = lambda c: (B["mn"][:, 512 * c:512 * c + 512], [k("mn%d" % m) for m in range(4 * c, 4 * c + 4)])
        mm([(bD[:, 0:128], T.c128[:], T.mc2[:], True, False, 128)]
           + [(bD[:, m:128:16], row(m), T.bo8[:, 0:8], False, False, 8) for m in range(16) if m % 4 < GV], ["c128", "mc2", kS, "bo0"], [k("D")], k("bD"))
        for c in range(GV, 4):
            bk, kb = ("bM", k("zp")) if c == 2 and not GV else ("bG", k("G")) if c % 2 else ("bS", k("sP"))
            mm([(B[bk][:], T.idp[:], rows(c), True, False, 512)], ["idp", kS], [kb], k(bk))
            mm([(B[bk][:, x:512:4], T.idn[:], z, False, x == 3, n) for x in range(4)], ["idn", kz], [kb], k(bk))
            act(mnc(c)[0], B[bk][:], AF.Abs, [kb], mnc(c)[1], 512, [k(bk)])
        if GV:
            mm([(bM[:, x:512:4], T.idp[:], z, True, True, n) for x in range(4)], ["idp", kz], [k("zp")], k("bM"))
            mm([(bD[:, 0:128], z, T.zv[:], False, False, 128)], [kz, "zv"], [k("D")], k("bD"))
            for c in range(GV):
                tt(mnc(c)[0], rows(c), bM[:], MN, [kS, k("zp")], mnc(c)[1], 512, [k("bM")])
        for c in (0, 2, 1, 3):
            mm([(bD[:, 4 * x + c:128:16], B["mn"][:, 512 * c + x:512 * c + 512:4], T.bo8[:, 8:16] if c < GV else T.bo8[:, 0:8], False, c == 3 and x == 3, 8) for x in range(4)],
               mnc(c)[1] + ["bo0", "bo1"], [k("D")], k("bD"))
        cv = spread(B, k, bD[:, 128:160], (T.hc, T.hp, T.hq), 32, HK, k("cv"))
        least(B, k)
        cv[0]()
        cv[1]()
        cp(lu[:, 0:16], bD[:, 128:144], [k("cv")], [k("lg")], 16, [k("bD")])
        tt(sm[:, 16:24], bD[:, 152:160], T.bc[:, 8:16], MN, [k("cv"), "bc1"], [k("m16")], 8, [k("bD")])
        tt(sm[:, 24:32], bD[:, 144:152], sm[:, 16:24], MX, [k("cv"), k("m16")], [k("m24")], 8, [k("bD")])
        middle(B, k, t, 0, states(B, par), lu[:, 0:8], [kS, k("lg")], z, kz)
        ag(oh, T.dm[:, 0:16], lu[:, 8:16], ["dm", k("lg")], [k("oh")], n)
        lst = []
        for j in range(1, 5):
            o = bG[:, n * j - n:n * j]
            lst += [(o, T.id16[:], B["N7"][:, 6::7], True, False, n), (o, T.on[:, 128 * j:128 * j + 128], oh, False, True, n)]
        mm(lst, ["id16", k("M20"), k("M21"), k("oh")] + ["on%d" % j for j in range(1, 5)], [k("G")], k("bG"))
        ts(B["Qh"][:], bG[:], -4096.0, -2048.0, AD, MX, [k("G")], [k("Q")], 512, [k("bG")])
        for q0 in range(0, 16, 8):
            mm([(bG[:, 0:32], sel(T.bigh, q), B["Qh"][:, q:512:16], q == 0, q == 15, 32) for q in range(q0, q0 + 8)], ["bigh", k("Q")], [k("G")], k("bG"))
        ts(B["cu"][:, 120:152], bG[:, 0:32], 32768.0, None, AD, None, [k("G")], blocks(k, "cu", 120, 152), 32, [k("bG")])
        ts(B["ci"][:, 120:152], bG[:, 0:32], 32768.0, None, AD, None, [k("G")], blocks(k, "ci", 120, 152), 32, [k("bG")])
        cp(lu[:, 24:32], sm[:, 24:32], [k("m24")], [k("l15")], 8)
        o = bM[:, 0:128]
        mm([(o, T.c128[:], T.i32[:], True, False, n), (o, T.lo[:], oh, False, False, n), (o, T.pk[:], oh, False, False, n),
            (o, T.pl[:], oh, False, True, n)], ["c128", "i32", "lo", "pk", "pl", k("oh")], [k("zp")], k("bM"))
        ts(B["ru"][:], o, 0.5, col[:, 10:11], MU, AD, [k("zp"), "c10"], [k("ru")], n, [k("bM")])
        bid(B, k, 0, 5)
        bid(B, k, 0, 0)

    def corr(t, h, j):
        cur_h[:] = [h, "corr%d%d" % (h, j), 0]
        B, k = H[h], keys(h)
        si, sm, lu, bD, bS = B["si"], B["sm"], B["lu"], B["bD"], B["bS"]
        a0, l0 = 16 * n * (j - 1), 8 * (j - 1)
        s, ks, U = new(B, t, j - 1), k("new%d" % (j - 1)), bD[:, 384:392]
        mm([(U, sel(T.wbh, q), B["sq"][:, q:n:16], q == 0, q == 15, 8) for q in range(16)], ["wbh", k("sq")], [k("U")], k("bD"))
        mm([(bS[:, n * c:n * c + n], T.idp[:], s, True, True, n) for c in range(4)], ["idp", ks], [k("sP")], k("bS"))
        ts(si[:, 8:16], U, col[:, 9:10], None, SU, None, [k("U"), "c9"], [k("s8")], nr, [k("bD")])
        Dm = lambda m: bD[:, 15 - m:128:16]
        mm([(bD[:, 0:128], T.c128[:], T.mc2[:], True, False, 128), (Dm(15), B["oh"][:], T.dd[:, l0:l0 + 8], False, False, 8)],
           ["c128", "mc2", "dd", k("oh")], [k("D")], k("bD"))
        ts(si[:, 0:8], si[:, 8:16], 4095, None, AND, None, [k("s8")], [k("u")], nr)
        tt(sm[:, 0:8], si[:, 0:8], si[:, 0:8], MU, [k("u")], [k("uu")], nr)
        b1 = T.kj[:, j - 1:j] if t == 0 else T.b1[:, 4 * t + j - 1:4 * t + j]
        ts(si[:, 16:24], sm[:, 0:8], b1, 2.0 ** -5, AD, MU, [k("uu"), "b1%d" % t], [k("base")], nr)
        for x, (e0, e1) in zip("xy", ((0, nr * IX), (nr * IX, n)) if IX else ((0, n),)):
            rp, f1 = T.rl[:, 8:8 + (e1 - e0) // 16], min(e1, n - nr)
            if not PU:
                tg(B["p1"][:, e0:e1], si[:, 0:8], rp, T.kr[:, e0:e1], MU, [k("u"), "rp", "kr"], [k("p1" + x)], e1 - e0)
            elif x == "x":
                tg(B["p1"][:], si[:, 0:8], T.rl[:, 8:16], T.kr[:], MU, [k("u"), "rp", "kr"], [k("p1x"), k("p1y")], n)
            tg(B["p2"][:, e0:e1], si[:, 16:24], rp, B["p1"][:, e0:e1], AD, [k("base"), "rp", k("p1" + x)], [k("p2" + x)], e1 - e0)
            ts(B["ci"][:, l0 + e0:l0 + f1], B["p2"][:, e0:f1], 4095, None, AND, None, [k("p2" + x)], blocks(k, "ci", l0 + e0, l0 + f1), f1 - e0)
            cp(B["cu"][:, l0 + e0:l0 + f1], B["ci"][:, l0 + e0:l0 + f1], blocks(k, "ci", l0 + e0, l0 + f1), blocks(k, "cu", l0 + e0, l0 + f1), f1 - e0)
        ka = lambda m: k("a%d%d" % (j, sum(1 for c in CH[1:] if c <= m)))
        am = lambda m: B["aw"][:, a0 + n * m:a0 + n * m + n]
        mnm = lambda m: B["mn"][:, n * m:n * m + n]
        cuts = sorted(set(x for x in VB + (NS,) if x >= NS))
        for c0, c1 in zip(CH, CH[1:]):
            (vg if c0 in CV else ag)(B["aw"][:, a0 + n * c0:a0 + n * c1], X[:, 0:4096], B["cu"][:, l0 + nr * c0:l0 + nr * c1],
               XK + blocks(k, "cu", l0 + nr * c0, l0 + nr * c1), [ka(c0)], n * (c1 - c0))
            if c0 < NS <= c1:
                lst = []
                for m in range(NS):
                    o = B["bG"][:, n * m:n * m + n]
                    lst += [(o, T.idp[:], am(m), True, False, n), (o, T.idn[:], s, False, True, n)]
                mm(lst, ["idp", "idn", ks] + [ka(m) for m in range(NS)], [k("G")], k("bG"))
                act(B["mn"][:, 0:n * NS], B["bG"][:, 0:n * NS], AF.Relu, [k("G")], [k("mn%d" % m) for m in range(NS)], n * NS, [k("bG")])
            mm([(Dm(m), am(m), T.bo8[:, 24:32] if m < NS else T.bo8[:, 0:8], False, False, 8) for m in range(c0, c1)], [ka(c0), "bo0", "bo3"], [k("D")], k("bD"))
            if c1 == 16 and NS:
                mm([(Dm(m), mnm(m), T.bo8[:, 16:24], False, False, 8) for m in range(NS)], [k("mn%d" % m) for m in range(NS)] + ["bo2"], [k("D")], k("bD"))
            for m0, m1 in zip(cuts, cuts[1:]):
                if c0 < m1 <= c1:
                    kk = [k("mn%d" % m) for m in range(m0, m1)]
                    tt(B["mn"][:, n * m0:n * m1], B["aw"][:, a0 + n * m0:a0 + n * m1], bS[:, 0:n * (m1 - m0)], MN,
                       [ka(m) for m in range(m0, m1)] + [k("sP")], kk, n * (m1 - m0), [k("bS")])
                    mm([(Dm(m), mnm(m), T.bo8[:, 8:16], False, m == 15, 8) for m in range(m0, m1)], kk + ["bo1"], [k("D")], k("bD"))
        c0 = 192 + 5 - j
        cv = spread(B, k, bD[:, c0:c0 + 120:5], (T.cc, T.cp, T.cq), 24, CK, k("cv%d" % j))
        least(B, k)
        cv[0]()
        cv[1]()
        cp(lu[:, 16 + 16 * j:32 + 16 * j], bD[:, c0:c0 + 80:5], [k("cv%d" % j)], [k("lc%d" % j)], 16, [k("bD")])
        middle(B, k, t, j, B["aw"][:, a0:a0 + 16 * n], lu[:, 16 + 16 * j:24 + 16 * j], [ka(m) for m in CH[:-1]] + [k("lc%d" % j)], s, ks)
        pick(B, k, j, B["ci"][:, l0:l0 + n], lu[:, 24 + 16 * j:32 + 16 * j], blocks(k, "ci", l0, l0 + n) + [k("lc%d" % j)])
        bid(B, k, 0, j)

    def tail(t, h):
        cur_h[:] = [h, "tail%d%d" % (h, t == 3), 0]
        B, par, k = H[h], t % 2, keys(h)
        lu, sm, oh = B["lu"], B["sm"], B["oh"]
        news = [k("new%d" % j) for j in range(5)] + [k("fill%d%d" % (par, c)) for c in range(11)]
        kS, kN = "S%d%d" % (h, par), "S%d%d" % (h, 1 - par)
        win = B["pool"][:, 4096 * par:4096 * par + 4096]
        scan(sm[:, 48:88], B["bD"][:, 272:312], T.lc[:], MN, MX, [k("rz")] + [k("cv%d" % j) for j in range(1, 5)] + ["lc%d" % c for c in range(5)],
             [k("rel")], 40, [k("bD")])
        cp(lu[:, 96:104], sm[:, 52:88:5], [k("rel")], [k("lsel")], nr)
        tg(B["aw"][:, ALT:ALT + n], win, lu[:, 24:32], B["z"][:, n * t:n * t + n], SU, news + [kS, k("l15"), "z%d%d" % (h, t)], [k("alt")], n)
        zs = B["zs"][:, n * t:n * t + n]
        ag(zs, B["aw"][:], lu[:, 96:104], [k("a%d%d" % (j, c)) for j in range(1, 5) for c in range(len(CH) - 1)] + [k("alt"), k("lsel")], [k("zs%d" % t)], n, AF.Abs)
        dst = T.cores[(rank + 1 + t % 3) % len(T.cores)]
        rid, pid, _ = topo.addr(dst)
        sem = "in%d" % (NP * t + h)
        land = B["z"][:, n * t + n:n * t + 2 * n]
        snd = op("G", lambda: g.remote_dma(land, zs, T.sem[sem], T.sem.sent, pid, rid, topo.mask(core, dst)), [k("zs%d" % t)], [], (500, 0, 0), sem="remote")
        src = T.cores[(rank - 1 - t % 3) % len(T.cores)]
        op("N", len(topo.engines(src, core)), [], ["z%d%d" % (h, t + 1)], (0, 0, 0), sem=sem, after=[(snd, NET)])
        if t < 3:
            ts(T.cn[:, 8 * h:8 * h + 8], sm[:, 52:88:5], float(ALT), None, ALU.is_lt, None, [k("rel")], ["cn%d" % h], nr)
        nb = 4 if t == 3 else RB
        n0, w = 4096 * (1 - par) + 2048, 2048 // nb
        for c in range(nb):
            o, lst = B["pool"][:, n0 + w * c:n0 + w * c + w], B["ru"][:, w * c // 16:w * (c + 1) // 16]
            (vg if c >= nb - (RL if t == 3 else RV[h]) else ag)(o, win, lst, news + [kS, k("ru"), kN], [k("rb%d" % c)], w)
            if t == 3:
                dma(T.so[:, 2048 * h + w * c:2048 * h + w * c + w], o, [k("rb%d" % c)], [], 2200 + w)
        last_w[kN] = op("N", None, [k("rb%d" % c) for c in range(nb)], [], (0, 0, 0))
        for j in (5, 0, 1, 2, 3, 4):
            bid(B, k, 1, j)
        for x, (bk, kb) in enumerate(BIDS):
            scan(B["N7"][:, 448 * x:448 * x + 448], T.rsn[:], B[bk][:, 0:448], AD, MX, ["rsn", k(kb)], [k("M2%d" % x)], 448, [k(bk)])
        if t == 3:
            ts(B["M"][:], B["N7"][:, 6::7], 2048.0, None, AD, None, [k("M20"), k("M21")], [k("M")], n)
            dma(T.mo[:, n * h:n * h + n], B["M"][:], [k("M")], [], 2500)
            dma(T.zo[:, n * h:n * h + n], B["z"][:, 512:640], ["z%d4" % h], [], 2500)

    for t in range(4):
        for h in range(NP):
            head(t, h)
        for j in range(1, 5):
            for h in range(NP):
                corr(t, h, j)
        for h in range(NP):
            tail(t, h)
        if t < 3:
            cni, o, kb = T.cni, H[-1]["bM"][:, 480:488], "bM_%d" % (NP - 1)
            mm([(o, T.one[:], T.cn[:, 8 * h:8 * h + 8], h == 0, h == NP - 1, 8) for h in range(NP)], ["one", "cn0", "cn1"], ["ct"], kb)
            op("V", lambda: V.tensor_reduce(T.kj[:, 5:6], o, AX.X, AD), ["ct", "b10"], ["cs", "kj4"], (55, 8, 0), [kb])
            cp(cni[:, 0:1], T.kj[:, 5:6], ["cs"], ["cni0"], 1)
            ts(cni[:, 4:5], cni[:, 0:1], 2047, None, AND, None, ["cni0"], ["cni4"], 1)
            cp(T.kj[:, 4:5], cni[:, 4:5], ["cni4", "b10"], ["a32", "kj4"], 1)
            ts(T.b1[:, 4 * t + 4:4 * t + 8], T.kj[:, 0:4], T.kj[:, 4:5], None, AD, None, ["b10", "a32"], ["b1%d" % (t + 1)], 4)


def lat(ops, a, b):
    x = ops[b]["deps"][a]
    if x:
        return x
    ea, eb = ops[a]["e"], ops[b]["e"]
    if eb == "N":
        return 0.0
    if ea == eb and not ops[a]["sem"]:
        return 0.0 if ea == "P" else SAME
    return HOP


def costs(ops, model):
    f, gc, v0, a0, least, p0, pc = model
    out = []
    for o in ops:
        e, (c0, c, x) = o["e"], o["c"]
        if x:
            out.append(c0 - 5 + 0.83 * f * gc * x)
        elif e in "VA":
            out.append((v0 if e == "V" else a0) + 0.83 * f * max(least, c))
        else:
            out.append(p0 + 0.83 * f * pc * c if e == "P" else c0 + 0.83 * f * c)
    return out


def replay(ops, bw, order, cost):
    fin = [0.0] * len(ops)
    free = {e: 0.0 for e in "VAPGYN"}
    for i in order:
        e = ops[i]["e"]
        t0 = max([fin[d] + l for d, l in bw[i]] + [0.0 if e == "N" else free[e]])
        fin[i] = t0 + cost[i]
        free[e] = t0 + 60.0 if e == "Y" else fin[i]
    return max(fin)


def schedule(ops):
    m = len(ops)
    fw, bw = [[] for _ in range(m)], [[] for _ in range(m)]
    for i, o in enumerate(ops):
        for d in o["deps"]:
            fw[d].append((i, lat(ops, d, i)))
            bw[i].append((d, lat(ops, d, i)))
    cs = [costs(ops, x) for x in MODELS]
    cost = cs[0]
    pr = [0.0] * m
    for i in range(m - 1, -1, -1):
        pr[i] = cost[i] + max([pr[s] + l for s, l in fw[i]], default=0.0)
    pr = [pr[i] - BONUS * ops[i]["h"] for i in range(m)]
    best, x = None, SEED
    for p in range(PASSES):
        order, fin = listed(ops, fw, pr, cost)
        val = sum(replay(ops, bw, order, c) / sum(c) for c in cs)
        if best is None or val <= best[1]:
            best = (order, val, fin)
        if p >= 4:
            fin = list(best[2])
            x = (x * 1103515245 + 12345) % 2147483648
            a = max(fin) * x / 2147483648
            x = (x * 1103515245 + 12345) % 2147483648
            sh = SHIFT * (x / 1073741824 - 1)
            for i in range(m):
                if abs(fin[i] - a) < SPAN:
                    x = (x * 1103515245 + 12345) % 2147483648
                    fin[i] += NOISE * x / 2147483648 + sh * ops[i]["h"]
        pr = listed(ops, bw, fin, cost)[1] if p % 2 else [cost[i] - fin[i] for i in range(m)]
    return best[0], bw


PLAN = {}


def listed(ops, edges, pr, cost):
    m = len(ops)
    left = [0] * m
    for i in range(m):
        for s, _ in edges[i]:
            left[s] += 1
    rdy, fin = [0.0] * m, [0.0] * m
    free = {e: 0.0 for e in "VAPGYN"}
    cand = {e: [] for e in free}
    for i in range(m):
        if not left[i]:
            cand[ops[i]["e"]].append(i)
    order = []
    while len(order) < m:
        t0, e = min((max(free[e], min(rdy[i] for i in cand[e])), e) for e in free if cand[e])
        i = max((x for x in cand[e] if rdy[x] <= t0 + LOOK), key=lambda x: (pr[x], -x))
        cand[e].remove(i)
        t0 = max(t0, rdy[i])
        fin[i] = t0 + cost[i]
        free[e] = t0 + 60.0 if e in "YN" else fin[i]
        order.append(i)
        for s, l in edges[i]:
            rdy[s] = max(rdy[s], fin[i] + l)
            left[s] -= 1
            if not left[s]:
                cand[ops[s]["e"]].append(s)
    return order, fin


def improve(ops, W, order, steps, seed):
    m, K = len(ops), range(len(W))
    en = [o["e"] for o in ops]
    hold = [[60.0 if en[i] == "Y" else w[0][i] for i in range(m)] for w in W]
    direct = [set(d for d, _ in W[0][1][i]) for i in range(m)]
    order, qp, qn, z = list(order), [-1] * m, [-1] * m, [seed]
    R, Q = [[0.0] * m for _ in K], [[0.0] * m for _ in K]

    def rnd():
        z[0] = (z[0] * 1103515245 + 12345) % 2147483648
        return z[0] / 2147483648

    def links(seg, last, nxt):
        for i in seg:
            if en[i] != "N":
                j = last.get(en[i], -1)
                qp[i], qn[i], last[en[i]] = j, nxt.get(en[i], -1), i
                if j >= 0:
                    qn[j] = i

    def heads(seg, k):
        r, h, (cost, bw, _) = R[k], hold[k], W[k]
        for i in seg:
            j = qp[i]
            t = r[j] + h[j] if j >= 0 else 0.0
            for d, l in bw[i]:
                v = r[d] + cost[d] + l
                if v > t:
                    t = v
            r[i] = t

    def tails(seg, k):
        q, h, (cost, _, fw) = Q[k], hold[k], W[k]
        for i in reversed(seg):
            j, c = qn[i], cost[i]
            t = h[i] + q[j] if j >= 0 else c
            if c > t:
                t = c
            for s, l in fw[i]:
                v = c + l + q[s]
                if v > t:
                    t = v
            q[i] = t

    def length(seg, k):
        r, q = R[k], Q[k]
        return max(r[i] + q[i] for i in seg)

    def shake(seg, iters, step, norm):
        inw, top, before, after = set(seg), sorted(seg), {}, {}
        for i in seg:
            if en[i] != "N":
                if en[i] not in before and qp[i] >= 0 and qp[i] not in inw:
                    before[en[i]] = qp[i]
                if qn[i] not in inw:
                    after[en[i]] = qn[i]
        out = [{i: max([l + Q[k][s] for s, l in W[k][2][i] if s not in inw] + [0.0]) + W[k][0][i] for i in seg} for k in K]
        base = [{i: max([R[k][d] + W[k][0][d] + l for d, l in W[k][1][i] if d not in inw] + [0.0]) for i in seg} for k in K]
        pre = [{i: [(d, l + W[k][0][d]) for d, l in W[k][1][i] if d in inw] for i in seg} for k in K]
        each = [length(seg, k) for k in K]
        best, bseg = sum(each[k] / norm[k] for k in K), seg
        bst = [{i: R[k][i] for i in seg} for k in K]
        late = [{i: each[k] - Q[k][i] for i in seg} for k in K]
        for it in range(iters):
            k = it % len(W)
            a, sh, p, b0, pk, h = rnd() * (rnd() < 0.5), (rnd() - 0.5) * 4 * step, {}, bst[k], pre[k], hold[k]
            c0, sp = b0[seg[int(rnd() * len(seg))]], 300.0 + 2500.0 * rnd()
            for i in top:
                v = b0[i]
                if abs(v - c0) < sp:
                    v += a * max(min(late[k][i] - v, 1500.0), 0.0) + rnd() * step + sh * ops[i]["h"]
                for d, _ in pk[i]:
                    if p[d] >= v:
                        v = p[d] + 0.001
                p[i] = v
            st, S, F, lim = {}, {e: [] for e in after}, {e: [] for e in after}, each[k] + 150.0
            for i in sorted(seg, key=p.get):
                t, e = base[k][i], en[i]
                for d, l in pk[i]:
                    if st[d] + l > t:
                        t = st[d] + l
                if e != "N":
                    s, f, c = S[e], F[e], h[i]
                    if e in before:
                        t = max(t, R[k][before[e]] + h[before[e]])
                    x = len(s)
                    while x and f[x - 1] > t:
                        x -= 1
                    while x < len(s) and s[x] < t + c:
                        t = f[x]
                        x += 1
                    s.insert(x, t)
                    f.insert(x, t + c)
                st[i] = t
                if t + out[k][i] > lim:
                    break
            else:
                new = sorted(seg, key=lambda i: (st[i], i))
                links(new, dict(before), after)
                now = []
                for y in K:
                    heads(new, y)
                    r = R[y]
                    now.append(max(max(r[i] + out[y][i], r[i] + hold[y][i] + Q[y][qn[i]] if qn[i] >= 0 and qn[i] not in inw else 0.0) for i in new))
                val = sum(now[y] / norm[y] for y in K)
                if val <= best:
                    best, bseg, each = val, new, now
                    bst = [{i: R[y][i] for i in seg} for y in K]
        return bseg

    def swaps(seg, iters, norm):
        inw, best, bseg, tabu = set(seg), sum(length(seg, k) / norm[k] for k in K), list(seg), {}
        for it in range(iters):
            k = it % len(W)
            r, q, h, (cost, bw, fw) = R[k], Q[k], hold[k], W[k]
            L, pick, pv = length(seg, k) - 0.01, None, 1e18
            for u in seg:
                v = qn[u]
                if v >= 0 and r[u] + q[u] > L and v in inw and r[u] + h[u] + q[v] > L and u not in direct[v] and tabu.get((u, v), -1) < it:
                    p, s2 = qp[u], qn[v]
                    rv = max([r[d] + cost[d] + l for d, l in bw[v]] + [r[p] + h[p] if p >= 0 else 0.0])
                    ru = max([r[d] + cost[d] + l for d, l in bw[u]] + [rv + h[v]])
                    qu = max([cost[u] + l + q[s] for s, l in fw[u]] + [cost[u], h[u] + q[s2] if s2 >= 0 else 0.0])
                    qv = max([cost[v] + l + q[s] for s, l in fw[v]] + [cost[v], h[v] + qu])
                    e = max(rv + qv, ru + qu) + 20.0 * rnd()
                    if e < pv:
                        pick, pv = (u, v), e
            if pick is None:
                continue
            u, v = pick
            tabu[(v, u)] = it + 8 + int(8 * rnd())
            p, s2 = qp[u], qn[v]
            qp[v], qn[v], qp[u], qn[u] = p, u, v, s2
            if p >= 0:
                qn[p] = v
            if s2 >= 0:
                qp[s2] = u
            iu, iv = seg.index(u), seg.index(v)
            mid, anc = seg[iu:iv + 1], {v}
            for y in reversed(mid[1:-1]):
                if qn[y] in anc or any(s in anc for s, _ in fw[y]):
                    anc.add(y)
            seg[iu:iv + 1] = [y for y in mid if y in anc] + [y for y in mid if y not in anc]
            for y in K:
                heads(seg[iu:], y)
                tails(seg[:iv + 1], y)
            val = sum(length(seg, y) / norm[y] for y in K)
            if val < best - 1e-7:
                best, bseg = val, list(seg)
        return bseg

    norm = None
    for width, iters, step, a0, a1 in steps:
        a = a0 - int(width * rnd())
        while a < a1:
            lo, hi = max(a, 0), min(a + width, m)
            a += width
            if hi > lo:
                links(order, {}, {})
                for k in K:
                    heads(order, k)
                    tails(order, k)
                norm = norm or [length(order, k) for k in K]
                order[lo:hi] = shake(order[lo:hi], iters, step, norm) if step else swaps(order[lo:hi], iters, norm)
    return order


def repeat(ops, order, cost, bw):
    st, free, mem = [0.0] * len(ops), {e: 0.0 for e in "VAPGYN"}, {}
    for i in order:
        e = ops[i]["e"]
        st[i] = max([st[d] + cost[d] + l for d, l in bw[i]] + [0.0 if e == "N" else free[e]])
        free[e] = st[i] + (60.0 if e == "Y" else cost[i])
    for i, o in enumerate(ops):
        mem.setdefault(o["k"], []).append(i)
    ref = mem[("corr02", 1)]
    span, p = st[ref[2]] - st[ref[1]], list(st)
    for l in mem.values():
        if len(l) >= 3:
            x = 1 if st[l[1]] >= st[ref[1]] else 2
            for y, i in enumerate(l):
                p[i] = st[l[x]] + (y - x) * span
    first, last = p[ref[0]] - st[ref[0]], p[ref[3]] - st[ref[3]]
    for i, o in enumerate(ops):
        if len(mem[o["k"]]) < 3:
            p[i] = st[i] + (last if o["k"][0][0] == "t" else first)
        elif st[i] < st[ref[0]]:
            p[i] = st[i] + first
        elif st[i] > st[mem[("corr04", 1)][3]]:
            p[i] = st[i] + last
    for i in range(len(ops)):
        for d, _ in bw[i]:
            if p[d] >= p[i]:
                p[i] = p[d] + 0.001
    return sorted(range(len(ops)), key=lambda i: (p[i], i))


def plan(ops):
    order, bw0 = schedule(ops)
    m, W = len(ops), []
    for model, hop, same, net in WEIGH:
        bw = [[(d, {HOP: hop, SAME: same, NET: net}.get(l, l)) for d, l in b] for b in bw0]
        fw = [[] for _ in ops]
        for i in range(m):
            for d, l in bw[i]:
                fw[d].append((i, l))
        W.append((costs(ops, model), bw, fw))
    ref = [i for i, o in enumerate(ops) if o["k"] == ("corr02", 1)]
    best = None
    for c in range(CYCLES):
        a, b = order.index(ref[1]), order.index(ref[2])
        order = repeat(ops, improve(ops, W, order, [x + (a, b) for x in STEPS], SEED + c), W[1][0], W[1][1])
        val = sum(replay(ops, w[1], order, w[0]) / sum(w[0]) for w in W)
        if best is None or val < best[0]:
            best = (val, order)
    order = best[1]
    a, b = order.index(ref[0]), order.index(ref[3])
    ends = [x + y for _ in range(2) for y in ((0, a + 50), (b, m)) for x in STEPS[:3]]
    return improve(ops, W, order, ends + [STEPS[0] + (0, m), STEPS[2] + (0, m)], SEED)


def rank_program(g, core, T, topo):
    if T.rank_of(core) is None:
        return
    ops = []
    build(g, core, T, topo, ops)
    if "order" not in PLAN:
        PLAN["order"] = plan(ops)
    order = PLAN["order"]
    Q = {"V": g.vector, "A": g.scalar, "P": g.tensor, "G": g, "Y": g.sync}
    know = {e: {} for e in Q}
    cnt, mark, clock, join = {}, {}, {}, {}
    for i in order:
        o = ops[i]
        e = o["e"]
        if e == "N" and o["fn"] is None:
            join[i] = list(o["deps"])
            continue
        if e == "N":
            mark[i], clock[i] = (o["sem"], o["fn"]), {o["sem"]: o["fn"]}
            cnt[o["sem"]] = o["fn"]
            continue
        kn = know[e]
        need = [x for d in o["deps"] for x in join.get(d, [d]) if not (e == "P" and ops[x]["e"] == "P") and o["deps"][d] >= 0]
        for d in sorted(need, key=lambda d: -mark[d][1]):
            s, v = mark[d]
            if kn.get(s, 0) < v and not any(clock[x].get(s, 0) >= v for x in need if mark[x][0] != s):
                Q[e].wait_ge(T.sem[s], v)
                kn[s] = v
        for d in need:
            for s, v in clock[d].items():
                kn[s] = max(kn.get(s, 0), v)
        ins = o["fn"]()
        if o["sem"] == "remote":
            mark[i], clock[i] = ("sent", 0), {}
            continue
        s, inc = (o["sem"], 16) if o["sem"] else ("q" + e, 1)
        ins.then_inc(T.sem[s], inc)
        cnt[s] = cnt.get(s, 0) + inc
        mark[i] = (s, cnt[s])
        clock[i] = dict(kn)
        clock[i][s] = cnt[s]
    cores = T.cores
    r = T.rank_of(core)
    g.wait_ge(T.sem.sent, sum(NP * len(topo.engines(core, cores[(r + 1 + t % 3) % len(cores)])) for t in range(4)))
    for s in sorted(cnt):
        g.wait_ge(T.sem[s], cnt[s])
